import numpy as np
import ml_dtypes


def mxq(x, axis, fmt="e4m3"):
    dtype, down = {"e4m3": (ml_dtypes.float8_e4m3fn, 7), "e5m2": (ml_dtypes.float8_e5m2, 14)}[fmt]
    v = np.moveaxis(np.asarray(x, np.float32).astype(ml_dtypes.bfloat16).astype(np.float64), axis, -1)
    blocks = v.reshape(v.shape[:-1] + (-1, 32))
    amax = np.abs(blocks).max(-1, keepdims=True)
    byte = np.maximum(np.where(amax > 0, np.frexp(amax)[1] - 1 + 127, 0) - down, 1)
    scale = np.exp2(byte - 127.0)
    codes = (blocks / scale).astype(np.float32).astype(dtype).astype(np.float64)
    return np.moveaxis((codes * scale).reshape(v.shape), -1, axis)


WIDE = False


def mx_kscale(k):
    if not WIDE:
        return np.ones(k)
    levels = np.array([18, -18])
    if k % 512:
        return np.exp2(np.random.permutation(np.resize(levels, k // 32))).repeat(32)
    a = np.empty((k // 512, 16))
    for p in range(k // 512):
        a[p, :8] = np.random.permutation(np.resize(levels, 8))
        for g in range(8):
            far = levels[np.abs(levels - a[p, g]) >= 10]
            a[p, g + 8] = far[np.random.randint(len(far))]
    return np.exp2(a.ravel()).repeat(32)


def f64(x):
    return np.asarray(x).astype(np.float64)


def striped(idx):
    return np.tile(np.asarray(idx).reshape(-1, 16).T, (8, 1)).astype(np.uint16)


def unstriped(offs):
    return offs[:16].T.reshape(-1).astype(np.int64)


B, N, T, D, R, TU = 1, 512, 2048, 512, 512, 2048


def setup_inputs():
    n = np.random.standard_normal
    idx = np.random.permutation(T)[:B * N]
    uidx = np.random.permutation(TU)[:B * R]
    s = mx_kscale(D)[:, None]
    z = np.ones(TU)
    z[uidx] = mx_kscale(B * R)
    u = np.ones(T)
    u[idx] = mx_kscale(B * N)
    r = np.random.uniform(0.5, 2.0, T) * u
    ur = np.random.uniform(0.5, 2.0, TU) * z
    return {
        "uT": (n((D, TU)) * s / ur).astype(np.float32),
        "vT": (n((D, T)) * (1.00 / np.sqrt(D)) / s / r).astype(np.float32),
        "y": n((B, R, N)).astype(np.float32),
        "us": ur[uidx].reshape(B, R, 1).astype(np.float32),
        "ts": np.tile(r, (128, 1)).astype(np.float32),
        "offs": striped(idx),
        "uoffs": striped(uidx),
    }


def reference(uT, vT, y, us, ts, offs, uoffs):
    idx = unstriped(offs)
    pick = lambda x: x[:, idx].reshape(x.shape[0], B, N).transpose(1, 0, 2)
    uidx = unstriped(uoffs)
    w = pick(f64(vT))
    x = f64(uT)[:, uidx].reshape(D, B, R).transpose(1, 0, 2)
    a = mxq(x, 1, "e4m3").transpose(0, 2, 1) @ mxq(w, 1, "e4m3")
    sc = f64(us) * pick(f64(ts))[:, :1, :]
    a = a * sc
    g = np.minimum(np.maximum(a - f64(y), -1.0), 1.0)
    h = sc * g
    dv = mxq(x, 2, "e4m3") @ mxq(h, 1, "e5m2")
    gv = np.zeros((D, T))
    gv[:, idx] = dv.transpose(1, 0, 2).reshape(D, B * N)
    du = mxq(w, 2, "e4m3") @ mxq(h, 2, "e5m2").transpose(0, 2, 1)
    gu = np.zeros((D, TU))
    gu[:, uidx] = du.transpose(1, 0, 2).reshape(D, B * R)
    return gv, gu

@@ -1,0 +1,181 @@
+from contextlib import ExitStack
+
+import concourse.mybir as mybir
+from concourse.masks import make_identity
+
+F32 = mybir.dt.float32
+BF16 = mybir.dt.bfloat16
+U32 = mybir.dt.uint32
+U16 = mybir.dt.uint16
+U8 = mybir.dt.uint8
+E4M3 = mybir.dt.float8_e4m3fn_x4
+E5M2 = mybir.dt.float8_e5m2_x4
+ALU = mybir.AluOpType
+COPY = mybir.ActivationFunctionType.Copy
+
+P = 128
+PACK = 4
+L = 512
+T = 2048
+HALF = L // 2
+
+FLOPS = 3 * 2 * L * L * L
+
+
+def tile_attend_gmf_hub_vu_kernel(tc, uT, vT, y, us, ts, offs, uoffs, out_0, out_1):
+    nc = tc.nc
+    with ExitStack() as ctx:
+        keep = ctx.enter_context(tc.tile_pool(name="keep", bufs=1))
+        ring = ctx.enter_context(tc.tile_pool(name="ring", bufs=4))
+        acc_pool = ctx.enter_context(tc.psum_pool(name="acc", bufs=4))
+        turn_pool = ctx.enter_context(tc.psum_pool(name="turn", bufs=4))
+
+        user_list = keep.tile([P, L // 16], U16, name="user_list")
+        item_list = keep.tile([P, L // 16], U16, name="item_list")
+        u_planes = [keep.tile([P, T], F32, name="u_plane%d" % t) for t in range(PACK)]
+        v_planes = [keep.tile([P, T], F32, name="v_plane%d" % t) for t in range(PACK)]
+        ts_table = keep.tile([P, T], F32, name="ts_table")
+        us_cols = keep.tile([P, PACK], F32, name="us_cols")
+        y_rows = keep.tile([P, PACK, L], F32, name="y_rows")
+        item_windows = [keep.tile([P, T], F32, name="item_window%d" % k) for k in range(2)]
+        user_windows = [keep.tile([P, T], F32, name="user_window%d" % k) for k in range(2)]
+        identity = keep.tile([P, P], F32, name="identity")
+
+        def operand(name):
+            values = keep.tile([P, L * PACK], BF16, name=name + "_values", align_bytes=64)
+            codes = keep.tile([P, L], U32, name=name + "_codes", align_bytes=64)
+            scales = keep.tile([P, L], U8, name=name + "_scales", align_bytes=64)
+            return values, codes, scales
+
+        def quantize(op, fmt, lo=0, hi=L):
+            values, codes, scales = op
+            nc.vector.quantize_mx(
+                out=codes[:, lo:hi].bitcast(fmt), scales=scales[:, lo:hi], in_=values[:, PACK * lo : PACK * hi]
+            )
+
+        def product(stationary, k, moving, moving_fmt):
+            acc = acc_pool.tile([P, L], F32, name="acc")
+            cols = slice(k * P, (k + 1) * P)
+            nc.tensor.matmul_mx(
+                out=acc[:],
+                lhsT=stationary[1][:, cols].bitcast(E4M3),
+                lhsT_scale=stationary[2][:, cols],
+                rhs=moving[1][:].bitcast(moving_fmt),
+                rhs_scale=moving[2][:],
+                start=True,
+                stop=True,
+            )
+            return acc
+
+        def turn(words, target):
+            turned = target[:].rearrange("m (p u e s) -> m p u e s", u=2, e=2, s=PACK)
+            for u in range(2):
+                bank = turn_pool.tile([P, PACK, P], F32, name="turn")
+                for s in range(PACK):
+                    nc.tensor.transpose(bank[:, s, :], words[:, s, :, u], identity[:])
+                pairs = bank[:].rearrange("m s p -> m (s p)").bitcast(BF16)
+                nc.scalar.copy(turned[:, :, u, :, :], pairs.rearrange("m (s p e) -> m p e s", s=PACK, e=2))
+
+        x_d, x_r, w_d, w_i, h_r, h_i = [operand(n) for n in ("x_d", "x_r", "w_d", "w_i", "h_r", "h_i")]
+
+        u_rows = uT.rearrange("(p t) c -> t p c", t=PACK)
+        v_rows = vT.rearrange("(p t) c -> t p c", t=PACK)
+        nc.vector.memset(ts_table[:], 0.0)
+        nc.sync.dma_start(u_planes[0][:], u_rows[0])
+        nc.sync.dma_start(user_list[:], uoffs)
+        nc.sync.dma_start(item_list[:], offs)
+        nc.scalar.dma_start(us_cols[:], us.rearrange("b (p s) o -> p (b s o)", s=PACK))
+        nc.scalar.dma_start(ts_table[0:1, :], ts[0:1, :])
+        for t in range(1, PACK):
+            nc.sync.dma_start(u_planes[t][:], u_rows[t])
+        for t in range(PACK):
+            nc.sync.dma_start(v_planes[t][:], v_rows[t])
+        nc.sync.dma_start(y_rows[:], y.rearrange("b (p s) i -> p (b s) i", s=PACK))
+
+        make_identity(nc, identity[:])
+        for window in item_windows + user_windows:
+            nc.vector.memset(window[:], 0.0)
+
+        ts_row = keep.tile([P, L], F32, name="ts_row")
+        nc.vector.tensor_copy(ts_row[:], ts_table[:].indirect(item_list[:]))
+        ts_turned = turn_pool.tile([P, PACK, P], F32, name="turn")
+        for j in range(PACK):
+            nc.tensor.transpose(ts_turned[:, j, :], ts_row[:, j * P : (j + 1) * P], identity[:])
+        ts_cols = keep.tile([P, PACK], F32, name="ts_cols")
+        nc.scalar.copy(ts_cols[:], ts_turned[:, :, 0])
+        ts_spread = turn_pool.tile([P, PACK, P], F32, name="turn")
+        for j in range(PACK):
+            nc.tensor.transpose(ts_spread[:, j, :], ts_cols[:, j : j + 1].to_broadcast([P, P]), identity[:])
+        scale = keep.tile([P, PACK, L], F32, name="scale")
+        for s in range(PACK):
+            nc.scalar.activation(
+                scale[:, s, :], ts_spread[:].rearrange("p j m -> p (j m)"), COPY, scale=us_cols[:, s : s + 1]
+            )
+        scale_packed = keep.tile([P, L, PACK], F32, name="scale_packed")
+        nc.scalar.copy(scale_packed[:], scale[:].rearrange("p s i -> p i s"))
+
+        x_planes = keep.tile([P, PACK, L], F32, name="x_planes")
+        for t in range(PACK):
+            nc.vector.tensor_copy(x_planes[:, t, :], u_planes[t][:].indirect(user_list[:]))
+        nc.scalar.copy(
+            x_d[0][:].rearrange("p (s m t) -> p m t s", s=PACK, t=PACK),
+            x_planes[:].rearrange("p t (m s) -> p m t s", s=PACK),
+        )
+        turn(x_d[0][:].bitcast(F32).rearrange("p (s m u) -> p s m u", s=PACK, u=2), x_r[0])
+
+        w_packed = w_d[0][:].rearrange("p (i t) -> p i t", t=PACK)
+        for t in range(PACK):
+            nc.vector.tensor_copy(w_packed[:, :, t], v_planes[t][:].indirect(item_list[:]))
+            if t == 1:
+                quantize(x_d, E4M3)
+            if t == 2:
+                quantize(x_r, E4M3)
+        quantize(w_d, E4M3)
+
+        scaled = keep.tile([P, PACK, L], F32, name="scaled")
+        for s in range(PACK):
+            acc = product(x_d, s, w_d, E4M3)
+            nc.vector.tensor_tensor(scaled[:, s, :], acc[:], scale[:, s, :], ALU.mult)
+        turn(w_d[0][:].bitcast(F32).rearrange("p (m s u) -> p s m u", s=PACK, u=2), w_i[0])
+
+        residual = keep.tile([P, PACK, L], F32, name="residual")
+        halves = (slice(0, HALF), slice(HALF, L))
+        nc.vector.tensor_tensor(residual[:, 0:2, :], scaled[:, 0:2, :], y_rows[:, 0:2, :], ALU.subtract)
+        for cols in halves:
+            nc.vector.tensor_tensor(residual[:, 2:4, cols], scaled[:, 2:4, cols], y_rows[:, 2:4, cols], ALU.subtract)
+        clipped = keep.tile([P, L, PACK], F32, name="clipped")
+        for cols in halves:
+            nc.vector.tensor_scalar(
+                clipped[:, cols, :], residual[:, :, cols].rearrange("p s i -> p i s"), -1.0, 1.0, ALU.max, ALU.min
+            )
+        h_packed = h_r[0][:].rearrange("p (i s) -> p i s", s=PACK)
+        for cols in halves:
+            nc.vector.tensor_tensor(h_packed[:, cols, :], clipped[:, cols, :], scale_packed[:, cols, :], ALU.mult)
+        for cols in halves:
+            quantize(h_r, E5M2, cols.start, cols.stop)
+        quantize(w_i, E4M3)
+
+        def finish(stationary, moving, k, windows, places, out):
+            acc = product(stationary, k, moving, E5M2)
+            sums = ring.tile([P, L], F32, name="sums")
+            nc.scalar.copy(sums[:], acc[:])
+            window = windows[k % 2]
+            nc.vector.tensor_copy(window[:].indirect(places[:]), sums[:])
+            nc.sync.dma_start(out[k * P : (k + 1) * P, :], window[:])
+
+        def items(k):
+            finish(x_r, h_r, k, item_windows, item_list, out_0)
+
+        def users(k):
+            finish(w_i, h_i, k, user_windows, user_list, out_1)
+
+        items(0)
+        items(1)
+        turn(h_r[0][:].bitcast(F32).rearrange("p (m s u) -> p s m u", s=PACK, u=2), h_i[0])
+        quantize(h_i, E5M2)
+        users(0)
+        items(2)
+        users(1)
+        items(3)
+        users(2)
+        users(3)

@@ -18,6 +18,7 @@ PACK = 4
 L = 512
 T = 2048
 HALF = L // 2
+WINDOWS = 3
 
 FLOPS = 3 * 2 * L * L * L
 
@@ -26,9 +27,11 @@ def tile_attend_gmf_hub_vu_kernel(tc, uT, vT, y, us, ts, offs, uoffs, out_0, out
     nc = tc.nc
     with ExitStack() as ctx:
         keep = ctx.enter_context(tc.tile_pool(name="keep", bufs=1))
-        ring = ctx.enter_context(tc.tile_pool(name="ring", bufs=4))
-        acc_pool = ctx.enter_context(tc.psum_pool(name="acc", bufs=4))
-        turn_pool = ctx.enter_context(tc.psum_pool(name="turn", bufs=4))
+        ring = ctx.enter_context(tc.tile_pool(name="ring", bufs=8))
+        psum = ctx.enter_context(tc.psum_pool(name="psum", bufs=1))
+
+        def bank_tile(b):
+            return psum.tile([P, L], F32, name="bank%d" % b)
 
         user_list = keep.tile([P, L // 16], U16, name="user_list")
         item_list = keep.tile([P, L // 16], U16, name="item_list")
@@ -37,8 +40,8 @@ def tile_attend_gmf_hub_vu_kernel(tc, uT, vT, y, us, ts, offs, uoffs, out_0, out
         ts_table = keep.tile([P, T], F32, name="ts_table")
         us_cols = keep.tile([P, PACK], F32, name="us_cols")
         y_rows = keep.tile([P, PACK, L], F32, name="y_rows")
-        item_windows = [keep.tile([P, T], F32, name="item_window%d" % k) for k in range(2)]
-        user_windows = [keep.tile([P, T], F32, name="user_window%d" % k) for k in range(2)]
+        item_windows = [keep.tile([P, T], F32, name="item_window%d" % k) for k in range(WINDOWS)]
+        user_windows = [keep.tile([P, T], F32, name="user_window%d" % k) for k in range(WINDOWS)]
         identity = keep.tile([P, P], F32, name="identity")
 
         def operand(name):
@@ -53,27 +56,25 @@ def tile_attend_gmf_hub_vu_kernel(tc, uT, vT, y, us, ts, offs, uoffs, out_0, out
                 out=codes[:, lo:hi].bitcast(fmt), scales=scales[:, lo:hi], in_=values[:, PACK * lo : PACK * hi]
             )
 
-        def product(stationary, k, moving, moving_fmt):
-            acc = acc_pool.tile([P, L], F32, name="acc")
+        def product(acc, stationary, k, moving, moving_fmt, n_cols):
             cols = slice(k * P, (k + 1) * P)
             nc.tensor.matmul_mx(
-                out=acc[:],
+                out=acc,
                 lhsT=stationary[1][:, cols].bitcast(E4M3),
                 lhsT_scale=stationary[2][:, cols],
-                rhs=moving[1][:].bitcast(moving_fmt),
-                rhs_scale=moving[2][:],
+                rhs=moving[1][:, n_cols].bitcast(moving_fmt),
+                rhs_scale=moving[2][:, n_cols],
                 start=True,
                 stop=True,
             )
-            return acc
 
-        def turn(words, target):
+        def turn(words, target, banks):
             turned = target[:].rearrange("m (p u e s) -> m p u e s", u=2, e=2, s=PACK)
             for u in range(2):
-                bank = turn_pool.tile([P, PACK, P], F32, name="turn")
+                bank = bank_tile(banks[u])
                 for s in range(PACK):
-                    nc.tensor.transpose(bank[:, s, :], words[:, s, :, u], identity[:])
-                pairs = bank[:].rearrange("m s p -> m (s p)").bitcast(BF16)
+                    nc.tensor.transpose(bank[:, s * P : (s + 1) * P], words[:, s, :, u], identity[:])
+                pairs = bank[:].bitcast(BF16)
                 nc.scalar.copy(turned[:, :, u, :, :], pairs.rearrange("m (s p e) -> m p e s", s=PACK, e=2))
 
         x_d, x_r, w_d, w_i, h_r, h_i = [operand(n) for n in ("x_d", "x_r", "w_d", "w_i", "h_r", "h_i")]
@@ -85,8 +86,9 @@ def tile_attend_gmf_hub_vu_kernel(tc, uT, vT, y, us, ts, offs, uoffs, out_0, out
         nc.sync.dma_start(user_list[:], uoffs)
         nc.sync.dma_start(item_list[:], offs)
         nc.scalar.dma_start(us_cols[:], us.rearrange("b (p s) o -> p (b s o)", s=PACK))
-        nc.scalar.dma_start(ts_table[0:1, :], ts[0:1, :])
-        for t in range(1, PACK):
+        nc.sync.dma_start(u_planes[1][:], u_rows[1])
+        nc.sync.dma_start(ts_table[0:1, :], ts[0:1, :])
+        for t in range(2, PACK):
             nc.sync.dma_start(u_planes[t][:], u_rows[t])
         for t in range(PACK):
             nc.sync.dma_start(v_planes[t][:], v_rows[t])
@@ -94,55 +96,65 @@ def tile_attend_gmf_hub_vu_kernel(tc, uT, vT, y, us, ts, offs, uoffs, out_0, out
 
         make_identity(nc, identity[:])
         for window in item_windows + user_windows:
-            nc.vector.memset(window[:], 0.0)
-
-        ts_row = keep.tile([P, L], F32, name="ts_row")
-        nc.vector.tensor_copy(ts_row[:], ts_table[:].indirect(item_list[:]))
-        ts_turned = turn_pool.tile([P, PACK, P], F32, name="turn")
-        for j in range(PACK):
-            nc.tensor.transpose(ts_turned[:, j, :], ts_row[:, j * P : (j + 1) * P], identity[:])
-        ts_cols = keep.tile([P, PACK], F32, name="ts_cols")
-        nc.scalar.copy(ts_cols[:], ts_turned[:, :, 0])
-        ts_spread = turn_pool.tile([P, PACK, P], F32, name="turn")
-        for j in range(PACK):
-            nc.tensor.transpose(ts_spread[:, j, :], ts_cols[:, j : j + 1].to_broadcast([P, P]), identity[:])
-        scale = keep.tile([P, PACK, L], F32, name="scale")
-        for s in range(PACK):
-            nc.scalar.activation(
-                scale[:, s, :], ts_spread[:].rearrange("p j m -> p (j m)"), COPY, scale=us_cols[:, s : s + 1]
-            )
-        scale_packed = keep.tile([P, L, PACK], F32, name="scale_packed")
-        nc.scalar.copy(scale_packed[:], scale[:].rearrange("p s i -> p i s"))
+            nc.gpsimd.memset(window[:], 0.0)
 
         x_planes = keep.tile([P, PACK, L], F32, name="x_planes")
         for t in range(PACK):
             nc.vector.tensor_copy(x_planes[:, t, :], u_planes[t][:].indirect(user_list[:]))
-        nc.scalar.copy(
+        nc.vector.tensor_copy(
             x_d[0][:].rearrange("p (s m t) -> p m t s", s=PACK, t=PACK),
             x_planes[:].rearrange("p t (m s) -> p m t s", s=PACK),
         )
-        turn(x_d[0][:].bitcast(F32).rearrange("p (s m u) -> p s m u", s=PACK, u=2), x_r[0])
+        turn(x_d[0][:].bitcast(F32).rearrange("p (s m u) -> p s m u", s=PACK, u=2), x_r[0], (6, 7))
+
+        ts_row = keep.tile([P, L], F32, name="ts_row")
+        nc.vector.tensor_copy(ts_row[:], ts_table[:].indirect(item_list[:]))
+        ts_turned = bank_tile(4)
+        for j in range(PACK):
+            nc.tensor.transpose(ts_turned[:, j * P : (j + 1) * P], ts_row[:, j * P : (j + 1) * P], identity[:])
+        ts_cols = keep.tile([P, PACK], F32, name="ts_cols")
+        nc.scalar.copy(ts_cols[:], ts_turned[:, 0:L:P])
+        ts_spread = bank_tile(5)
+        for j in range(PACK):
+            nc.tensor.transpose(
+                ts_spread[:, j * P : (j + 1) * P], ts_cols[:, j : j + 1].to_broadcast([P, P]), identity[:]
+            )
+        scale = keep.tile([P, PACK, L], F32, name="scale")
+        for s in range(PACK):
+            nc.scalar.activation(
+                scale[:, s, :], ts_spread[:], COPY, scale=us_cols[:, s : s + 1]
+            )
+        scale_packed = keep.tile([P, L, PACK], F32, name="scale_packed")
+        nc.scalar.copy(scale_packed[:], scale[:].rearrange("p s i -> p i s"))
 
         w_packed = w_d[0][:].rearrange("p (i t) -> p i t", t=PACK)
-        for t in range(PACK):
+        halves = (slice(0, HALF), slice(HALF, L))
+        for t in range(PACK - 1):
             nc.vector.tensor_copy(w_packed[:, :, t], v_planes[t][:].indirect(item_list[:]))
             if t == 1:
                 quantize(x_d, E4M3)
-            if t == 2:
-                quantize(x_r, E4M3)
-        quantize(w_d, E4M3)
+        for cols in halves:
+            places = item_list[:, cols.start // 16 : cols.stop // 16]
+            nc.vector.tensor_copy(w_packed[:, cols, PACK - 1], v_planes[PACK - 1][:].indirect(places))
+        for cols in halves:
+            quantize(w_d, E4M3, cols.start, cols.stop)
+        quantize(x_r, E4M3)
 
         scaled = keep.tile([P, PACK, L], F32, name="scaled")
-        for s in range(PACK):
-            acc = product(x_d, s, w_d, E4M3)
-            nc.vector.tensor_tensor(scaled[:, s, :], acc[:], scale[:, s, :], ALU.mult)
-        turn(w_d[0][:].bitcast(F32).rearrange("p (m s u) -> p s m u", s=PACK, u=2), w_i[0])
+        for n, cols in enumerate(halves):
+            for pair in range(2):
+                acc = bank_tile(2 * n + pair)
+                for e in range(2):
+                    product(acc[:, e * HALF : (e + 1) * HALF], x_d, 2 * pair + e, w_d, E4M3, cols)
+                rows = slice(2 * pair, 2 * pair + 2)
+                nc.vector.tensor_tensor(
+                    scaled[:, rows, cols], acc[:].rearrange("p (e i) -> p e i", e=2), scale[:, rows, cols], ALU.mult
+                )
+        turn(w_d[0][:].bitcast(F32).rearrange("p (m s u) -> p s m u", s=PACK, u=2), w_i[0], (0, 1))
 
         residual = keep.tile([P, PACK, L], F32, name="residual")
-        halves = (slice(0, HALF), slice(HALF, L))
-        nc.vector.tensor_tensor(residual[:, 0:2, :], scaled[:, 0:2, :], y_rows[:, 0:2, :], ALU.subtract)
         for cols in halves:
-            nc.vector.tensor_tensor(residual[:, 2:4, cols], scaled[:, 2:4, cols], y_rows[:, 2:4, cols], ALU.subtract)
+            nc.vector.tensor_tensor(residual[:, :, cols], scaled[:, :, cols], y_rows[:, :, cols], ALU.subtract)
         clipped = keep.tile([P, L, PACK], F32, name="clipped")
         for cols in halves:
             nc.vector.tensor_scalar(
@@ -155,27 +167,29 @@ def tile_attend_gmf_hub_vu_kernel(tc, uT, vT, y, us, ts, offs, uoffs, out_0, out
             quantize(h_r, E5M2, cols.start, cols.stop)
         quantize(w_i, E4M3)
 
-        def finish(stationary, moving, k, windows, places, out):
-            acc = product(stationary, k, moving, E5M2)
+        def finish(bank, stationary, moving, k, windows, places, out, pieces):
+            acc = bank_tile(bank)
+            product(acc[:], stationary, k, moving, E5M2, slice(0, L))
             sums = ring.tile([P, L], F32, name="sums")
-            nc.scalar.copy(sums[:], acc[:])
-            window = windows[k % 2]
-            nc.vector.tensor_copy(window[:].indirect(places[:]), sums[:])
+            window = windows[k % WINDOWS]
+            for cols in pieces:
+                nc.scalar.copy(sums[:, cols], acc[:, cols])
+                nc.vector.tensor_copy(window[:].indirect(places[:, cols.start // 16 : cols.stop // 16]), sums[:, cols])
             nc.sync.dma_start(out[k * P : (k + 1) * P, :], window[:])
 
         def items(k):
-            finish(x_r, h_r, k, item_windows, item_list, out_0)
+            finish(4 + k, x_r, h_r, k, item_windows, item_list, out_0, halves if k == 0 else (slice(0, L),))
 
         def users(k):
-            finish(w_i, h_i, k, user_windows, user_list, out_1)
+            finish(k, w_i, h_i, k, user_windows, user_list, out_1, (slice(0, L),))
 
         items(0)
         items(1)
-        turn(h_r[0][:].bitcast(F32).rearrange("p (m s u) -> p s m u", s=PACK, u=2), h_i[0])
+        turn(h_r[0][:].bitcast(F32).rearrange("p (m s u) -> p s m u", s=PACK, u=2), h_i[0], (4, 5))
+        items(2)
         quantize(h_i, E5M2)
         users(0)
-        items(2)
-        users(1)
         items(3)
+        users(1)
         users(2)
         users(3)

@@ -27,7 +27,6 @@ def tile_attend_gmf_hub_vu_kernel(tc, uT, vT, y, us, ts, offs, uoffs, out_0, out
     nc = tc.nc
     with ExitStack() as ctx:
         keep = ctx.enter_context(tc.tile_pool(name="keep", bufs=1))
-        ring = ctx.enter_context(tc.tile_pool(name="ring", bufs=8))
         psum = ctx.enter_context(tc.psum_pool(name="psum", bufs=1))
 
         def bank_tile(b):
@@ -36,7 +35,7 @@ def tile_attend_gmf_hub_vu_kernel(tc, uT, vT, y, us, ts, offs, uoffs, out_0, out
         user_list = keep.tile([P, L // 16], U16, name="user_list")
         item_list = keep.tile([P, L // 16], U16, name="item_list")
         u_planes = [keep.tile([P, T], F32, name="u_plane%d" % t) for t in range(PACK)]
-        v_planes = [keep.tile([P, T], F32, name="v_plane%d" % t) for t in range(PACK)]
+        v_planes = [keep.tile([P, T], F32, name="v_plane%d" % t, align_bytes=64) for t in range(PACK)]
         ts_table = keep.tile([P, T], F32, name="ts_table")
         us_cols = keep.tile([P, PACK], F32, name="us_cols")
         y_rows = keep.tile([P, PACK, L], F32, name="y_rows")
@@ -44,9 +43,11 @@ def tile_attend_gmf_hub_vu_kernel(tc, uT, vT, y, us, ts, offs, uoffs, out_0, out
         user_windows = [keep.tile([P, T], F32, name="user_window%d" % k) for k in range(WINDOWS)]
         identity = keep.tile([P, P], F32, name="identity")
 
-        def operand(name):
-            values = keep.tile([P, L * PACK], BF16, name=name + "_values", align_bytes=64)
-            codes = keep.tile([P, L], U32, name=name + "_codes", align_bytes=64)
+        def packed_values(name):
+            return keep.tile([P, L * PACK], BF16, name=name + "_values", align_bytes=64)
+
+        def operand(name, values, codes_tag=None):
+            codes = keep.tile([P, L], U32, name=codes_tag or name + "_codes", align_bytes=64)
             scales = keep.tile([P, L], U8, name=name + "_scales", align_bytes=64)
             return values, codes, scales
 
@@ -77,11 +78,16 @@ def tile_attend_gmf_hub_vu_kernel(tc, uT, vT, y, us, ts, offs, uoffs, out_0, out
                 pairs = bank[:].bitcast(BF16)
                 nc.scalar.copy(turned[:, :, u, :, :], pairs.rearrange("m (s p e) -> m p e s", s=PACK, e=2))
 
-        x_d, x_r, w_d, w_i, h_r, h_i = [operand(n) for n in ("x_d", "x_r", "w_d", "w_i", "h_r", "h_i")]
+        x_d = operand("x_d", packed_values("x_d"), "v_plane1")
+        x_r = operand("x_r", packed_values("x_r"), "v_plane3")
+        w_d = operand("w_d", packed_values("w_d"))
+        h_r = operand("h_r", packed_values("h_r"))
+        w_i_values = packed_values("w_i")
+        h_i_values = packed_values("h_i")
 
         u_rows = uT.rearrange("(p t) c -> t p c", t=PACK)
         v_rows = vT.rearrange("(p t) c -> t p c", t=PACK)
-        nc.vector.memset(ts_table[:], 0.0)
+        nc.vector.memset(ts_table[:].bitcast(U32), 0)
         nc.sync.dma_start(u_planes[0][:], u_rows[0])
         nc.sync.dma_start(user_list[:], uoffs)
         nc.sync.dma_start(item_list[:], offs)
@@ -101,7 +107,7 @@ def tile_attend_gmf_hub_vu_kernel(tc, uT, vT, y, us, ts, offs, uoffs, out_0, out
         x_planes = keep.tile([P, PACK, L], F32, name="x_planes")
         for t in range(PACK):
             nc.vector.tensor_copy(x_planes[:, t, :], u_planes[t][:].indirect(user_list[:]))
-        nc.vector.tensor_copy(
+        nc.scalar.copy(
             x_d[0][:].rearrange("p (s m t) -> p m t s", s=PACK, t=PACK),
             x_planes[:].rearrange("p t (m s) -> p m t s", s=PACK),
         )
@@ -124,8 +130,6 @@ def tile_attend_gmf_hub_vu_kernel(tc, uT, vT, y, us, ts, offs, uoffs, out_0, out
             nc.scalar.activation(
                 scale[:, s, :], ts_spread[:], COPY, scale=us_cols[:, s : s + 1]
             )
-        scale_packed = keep.tile([P, L, PACK], F32, name="scale_packed")
-        nc.scalar.copy(scale_packed[:], scale[:].rearrange("p s i -> p i s"))
 
         w_packed = w_d[0][:].rearrange("p (i t) -> p i t", t=PACK)
         halves = (slice(0, HALF), slice(HALF, L))
@@ -133,6 +137,8 @@ def tile_attend_gmf_hub_vu_kernel(tc, uT, vT, y, us, ts, offs, uoffs, out_0, out
             nc.vector.tensor_copy(w_packed[:, :, t], v_planes[t][:].indirect(item_list[:]))
             if t == 1:
                 quantize(x_d, E4M3)
+        scale_packed = keep.tile([P, L, PACK], F32, name="v_plane2", align_bytes=64)
+        nc.scalar.copy(scale_packed[:], scale[:].rearrange("p s i -> p i s"))
         for cols in halves:
             places = item_list[:, cols.start // 16 : cols.stop // 16]
             nc.vector.tensor_copy(w_packed[:, cols, PACK - 1], v_planes[PACK - 1][:].indirect(places))
@@ -150,12 +156,12 @@ def tile_attend_gmf_hub_vu_kernel(tc, uT, vT, y, us, ts, offs, uoffs, out_0, out
                 nc.vector.tensor_tensor(
                     scaled[:, rows, cols], acc[:].rearrange("p (e i) -> p e i", e=2), scale[:, rows, cols], ALU.mult
                 )
-        turn(w_d[0][:].bitcast(F32).rearrange("p (m s u) -> p s m u", s=PACK, u=2), w_i[0], (0, 1))
+        turn(w_d[0][:].bitcast(F32).rearrange("p (m s u) -> p s m u", s=PACK, u=2), w_i_values, (0, 1))
 
         residual = keep.tile([P, PACK, L], F32, name="residual")
         for cols in halves:
             nc.vector.tensor_tensor(residual[:, :, cols], scaled[:, :, cols], y_rows[:, :, cols], ALU.subtract)
-        clipped = keep.tile([P, L, PACK], F32, name="clipped")
+        clipped = keep.tile([P, L, PACK], F32, name="clipped", align_bytes=64)
         for cols in halves:
             nc.vector.tensor_scalar(
                 clipped[:, cols, :], residual[:, :, cols].rearrange("p s i -> p i s"), -1.0, 1.0, ALU.max, ALU.min
@@ -165,12 +171,13 @@ def tile_attend_gmf_hub_vu_kernel(tc, uT, vT, y, us, ts, offs, uoffs, out_0, out
             nc.vector.tensor_tensor(h_packed[:, cols, :], clipped[:, cols, :], scale_packed[:, cols, :], ALU.mult)
         for cols in halves:
             quantize(h_r, E5M2, cols.start, cols.stop)
+        w_i = operand("w_i", w_i_values, "clipped")
         quantize(w_i, E4M3)
 
-        def finish(bank, stationary, moving, k, windows, places, out, pieces):
+        def finish(side, bank, stationary, moving, k, windows, places, out, pieces):
             acc = bank_tile(bank)
             product(acc[:], stationary, k, moving, E5M2, slice(0, L))
-            sums = ring.tile([P, L], F32, name="sums")
+            sums = keep.tile([P, L], F32, name="%s_sums%d" % (side, k), align_bytes=64)
             window = windows[k % WINDOWS]
             for cols in pieces:
                 nc.scalar.copy(sums[:, cols], acc[:, cols])
@@ -178,18 +185,19 @@ def tile_attend_gmf_hub_vu_kernel(tc, uT, vT, y, us, ts, offs, uoffs, out_0, out
             nc.sync.dma_start(out[k * P : (k + 1) * P, :], window[:])
 
         def items(k):
-            finish(4 + k, x_r, h_r, k, item_windows, item_list, out_0, halves if k == 0 else (slice(0, L),))
+            finish("item", 4 + k, x_r, h_r, k, item_windows, item_list, out_0, halves if k == 0 else (slice(0, L),))
 
         def users(k):
-            finish(k, w_i, h_i, k, user_windows, user_list, out_1, (slice(0, L),))
+            finish("user", k, w_i, h_i, k, user_windows, user_list, out_1, (slice(0, L),))
 
         items(0)
         items(1)
-        turn(h_r[0][:].bitcast(F32).rearrange("p (m s u) -> p s m u", s=PACK, u=2), h_i[0], (4, 5))
+        turn(h_r[0][:].bitcast(F32).rearrange("p (m s u) -> p s m u", s=PACK, u=2), h_i_values, (4, 5))
         items(2)
+        h_i = operand("h_i", h_i_values, "item_sums1")
         quantize(h_i, E5M2)
-        users(0)
         items(3)
+        users(0)
         users(1)
         users(2)
         users(3)

@@ -78,7 +78,7 @@ def tile_attend_gmf_hub_vu_kernel(tc, uT, vT, y, us, ts, offs, uoffs, out_0, out
                 pairs = bank[:].bitcast(BF16)
                 nc.scalar.copy(turned[:, :, u, :, :], pairs.rearrange("m (s p e) -> m p e s", s=PACK, e=2))
 
-        x_d = operand("x_d", packed_values("x_d"), "v_plane1")
+        x_d = operand("x_d", packed_values("x_d"), "v_plane2")
         x_r = operand("x_r", packed_values("x_r"), "v_plane3")
         w_d = operand("w_d", packed_values("w_d"))
         h_r = operand("h_r", packed_values("h_r"))
@@ -135,9 +135,11 @@ def tile_attend_gmf_hub_vu_kernel(tc, uT, vT, y, us, ts, offs, uoffs, out_0, out
         halves = (slice(0, HALF), slice(HALF, L))
         for t in range(PACK - 1):
             nc.vector.tensor_copy(w_packed[:, :, t], v_planes[t][:].indirect(item_list[:]))
-            if t == 1:
-                quantize(x_d, E4M3)
-        scale_packed = keep.tile([P, L, PACK], F32, name="v_plane2", align_bytes=64)
+        quantize(x_d, E4M3)
+        warm = bank_tile(2)
+        for k in range(3):
+            product(warm[:], x_d, k, x_d, E4M3, slice(0, L))
+        scale_packed = keep.tile([P, L, PACK], F32, name="v_plane1", align_bytes=64)
         nc.scalar.copy(scale_packed[:], scale[:].rearrange("p s i -> p i s"))
         for cols in halves:
             places = item_list[:, cols.start // 16 : cols.stop // 16]
@@ -146,21 +148,41 @@ def tile_attend_gmf_hub_vu_kernel(tc, uT, vT, y, us, ts, offs, uoffs, out_0, out
             quantize(w_d, E4M3, cols.start, cols.stop)
         quantize(x_r, E4M3)
 
-        scaled = keep.tile([P, PACK, L], F32, name="scaled")
-        for n, cols in enumerate(halves):
-            for pair in range(2):
-                acc = bank_tile(2 * n + pair)
-                for e in range(2):
-                    product(acc[:, e * HALF : (e + 1) * HALF], x_d, 2 * pair + e, w_d, E4M3, cols)
-                rows = slice(2 * pair, 2 * pair + 2)
-                nc.vector.tensor_tensor(
-                    scaled[:, rows, cols], acc[:].rearrange("p (e i) -> p e i", e=2), scale[:, rows, cols], ALU.mult
-                )
-        turn(w_d[0][:].bitcast(F32).rearrange("p (m s u) -> p s m u", s=PACK, u=2), w_i_values, (0, 1))
-
+        first, second = halves
+        pairs = (slice(0, 2), slice(2, 4))
         residual = keep.tile([P, PACK, L], F32, name="residual")
-        for cols in halves:
-            nc.vector.tensor_tensor(residual[:, :, cols], scaled[:, :, cols], y_rows[:, :, cols], ALU.subtract)
+        scaled = keep.tile([P, PACK, HALF], F32, name="scaled")
+        for n, rows in enumerate(pairs):
+            acc = bank_tile(n)
+            for e in range(2):
+                product(acc[:, e * HALF : (e + 1) * HALF], x_d, rows.start + e, w_d, E4M3, first)
+            nc.vector.tensor_tensor(
+                scaled[:, rows, :], acc[:].rearrange("p (e i) -> p e i", e=2), scale[:, rows, first], ALU.mult
+            )
+        for rows in pairs:
+            nc.vector.tensor_tensor(residual[:, rows, first], scaled[:, rows, :], y_rows[:, rows, first], ALU.subtract)
+
+        back = [bank_tile(4), bank_tile(5)]
+        for j in (2, 3):
+            acc = bank_tile(j)
+            product(acc[:], w_d, j, x_d, E4M3, slice(0, L))
+            item_scaled = keep.tile([P, L], F32, name="item_scaled%d" % j)
+            nc.scalar.activation(item_scaled[:], acc[:], COPY, scale=ts_cols[:, j : j + 1])
+            for s in range(PACK):
+                c = (s % 2) * HALF + (j - 2) * P
+                nc.tensor.transpose(back[s // 2][:, c : c + P], item_scaled[:, s * P : (s + 1) * P], identity[:])
+        for s in range(PACK):
+            c = (s % 2) * HALF
+            nc.vector.scalar_tensor_tensor(
+                residual[:, s, second],
+                back[s // 2][:, c : c + HALF],
+                us_cols[:, s : s + 1],
+                y_rows[:, s, second],
+                ALU.mult,
+                ALU.subtract,
+            )
+        turn(w_d[0][:].bitcast(F32).rearrange("p (m s u) -> p s m u", s=PACK, u=2), w_i_values, (3, 4))
+
         clipped = keep.tile([P, L, PACK], F32, name="clipped", align_bytes=64)
         for cols in halves:
             nc.vector.tensor_scalar(
@@ -185,14 +207,14 @@ def tile_attend_gmf_hub_vu_kernel(tc, uT, vT, y, us, ts, offs, uoffs, out_0, out
             nc.sync.dma_start(out[k * P : (k + 1) * P, :], window[:])
 
         def items(k):
-            finish("item", 4 + k, x_r, h_r, k, item_windows, item_list, out_0, halves if k == 0 else (slice(0, L),))
+            finish("item", (0, 1, 2, 5)[k], x_r, h_r, k, item_windows, item_list, out_0, halves if k == 0 else (slice(0, L),))
 
         def users(k):
-            finish("user", k, w_i, h_i, k, user_windows, user_list, out_1, (slice(0, L),))
+            finish("user", (6, 7, 3, 4)[k], w_i, h_i, k, user_windows, user_list, out_1, (slice(0, L),))
 
         items(0)
         items(1)
-        turn(h_r[0][:].bitcast(F32).rearrange("p (m s u) -> p s m u", s=PACK, u=2), h_i_values, (4, 5))
+        turn(h_r[0][:].bitcast(F32).rearrange("p (m s u) -> p s m u", s=PACK, u=2), h_i_values, (0, 1))
         items(2)
         h_i = operand("h_i", h_i_values, "item_sums1")
         quantize(h_i, E5M2)

@@ -34,7 +34,7 @@ def tile_attend_gmf_hub_vu_kernel(tc, uT, vT, y, us, ts, offs, uoffs, out_0, out
 
         user_list = keep.tile([P, L // 16], U16, name="user_list")
         item_list = keep.tile([P, L // 16], U16, name="item_list")
-        u_planes = [keep.tile([P, T], F32, name="u_plane%d" % t) for t in range(PACK)]
+        u_planes = [keep.tile([P, T], F32, name="u_plane%d" % t, align_bytes=64) for t in range(PACK)]
         v_planes = [keep.tile([P, T], F32, name="v_plane%d" % t, align_bytes=64) for t in range(PACK)]
         ts_table = keep.tile([P, T], F32, name="ts_table")
         us_cols = keep.tile([P, PACK], F32, name="us_cols")
@@ -43,15 +43,15 @@ def tile_attend_gmf_hub_vu_kernel(tc, uT, vT, y, us, ts, offs, uoffs, out_0, out
         user_windows = [keep.tile([P, T], F32, name="user_window%d" % k) for k in range(WINDOWS)]
         identity = keep.tile([P, P], F32, name="identity")
 
-        def packed_values(name):
-            return keep.tile([P, L * PACK], BF16, name=name + "_values", align_bytes=64)
+        def packed_values(name, columns=L):
+            return keep.tile([P, columns * PACK], BF16, name=name + "_values", align_bytes=64)
 
-        def operand(name, values, codes_tag=None):
-            codes = keep.tile([P, L], U32, name=codes_tag or name + "_codes", align_bytes=64)
-            scales = keep.tile([P, L], U8, name=name + "_scales", align_bytes=64)
+        def operand(name, values, codes_tag=None, columns=L):
+            codes = keep.tile([P, columns], U32, name=codes_tag or name + "_codes", align_bytes=64)
+            scales = keep.tile([P, columns], U8, name=name + "_scales", align_bytes=64)
             return values, codes, scales
 
-        def quantize(op, fmt, lo=0, hi=L):
+        def quantize(op, fmt, lo, hi):
             values, codes, scales = op
             nc.vector.quantize_mx(
                 out=codes[:, lo:hi].bitcast(fmt), scales=scales[:, lo:hi], in_=values[:, PACK * lo : PACK * hi]
@@ -69,20 +69,35 @@ def tile_attend_gmf_hub_vu_kernel(tc, uT, vT, y, us, ts, offs, uoffs, out_0, out
                 stop=True,
             )
 
-        def turn(words, target, banks):
-            turned = target[:].rearrange("m (p u e s) -> m p u e s", u=2, e=2, s=PACK)
-            for u in range(2):
-                bank = bank_tile(banks[u])
-                for s in range(PACK):
-                    nc.tensor.transpose(bank[:, s * P : (s + 1) * P], words[:, s, :, u], identity[:])
-                pairs = bank[:].bitcast(BF16)
-                nc.scalar.copy(turned[:, :, u, :, :], pairs.rearrange("m (s p e) -> m p e s", s=PACK, e=2))
+        def turn_planes(planes, target, bank):
+            words = planes.bitcast(F32).rearrange("p (a m u) -> p a u m", a=2, u=2)
+            for a in range(2):
+                for u in range(2):
+                    c = (2 * a + u) * P
+                    nc.tensor.transpose(bank[:, c : c + P], words[:, a, u, :], identity[:])
+            nc.scalar.copy(
+                target.bitcast(F32).rearrange("m (a p u) -> m a p u", a=2, u=2),
+                bank[:].rearrange("m (a u p) -> m a p u", a=2, u=2),
+            )
 
-        x_d = operand("x_d", packed_values("x_d"), "v_plane2")
-        x_r = operand("x_r", packed_values("x_r"), "v_plane3")
+        def turn_pairs(values, u, bank):
+            words = values[:].bitcast(F32).rearrange("p (m s u) -> p s m u", s=PACK, u=2)
+            for s in range(PACK):
+                nc.tensor.transpose(bank[:, s * P : (s + 1) * P], words[:, s, :, u], identity[:])
+            return bank[:].bitcast(BF16)
+
+        halves = (slice(0, HALF), slice(HALF, L))
+        first, second = halves
+
+        def places(offsets, cols):
+            return offsets[:, cols.start // 16 : cols.stop // 16]
+
+        x_d_values = packed_values("x_d")
+        x_lo_values = packed_values("x_lo", HALF)
+        late_values = packed_values("late")
         w_d = operand("w_d", packed_values("w_d"))
         h_r = operand("h_r", packed_values("h_r"))
-        w_i_values = packed_values("w_i")
+        w_hi_values = packed_values("w_hi", HALF)
         h_i_values = packed_values("h_i")
 
         u_rows = uT.rearrange("(p t) c -> t p c", t=PACK)
@@ -92,26 +107,18 @@ def tile_attend_gmf_hub_vu_kernel(tc, uT, vT, y, us, ts, offs, uoffs, out_0, out
         nc.sync.dma_start(user_list[:], uoffs)
         nc.sync.dma_start(item_list[:], offs)
         nc.scalar.dma_start(us_cols[:], us.rearrange("b (p s) o -> p (b s o)", s=PACK))
-        nc.sync.dma_start(u_planes[1][:], u_rows[1])
         nc.sync.dma_start(ts_table[0:1, :], ts[0:1, :])
-        for t in range(2, PACK):
+        for t in range(1, PACK):
             nc.sync.dma_start(u_planes[t][:], u_rows[t])
         for t in range(PACK):
             nc.sync.dma_start(v_planes[t][:], v_rows[t])
         nc.sync.dma_start(y_rows[:], y.rearrange("b (p s) i -> p (b s) i", s=PACK))
 
         make_identity(nc, identity[:])
+        nc.vector.memset(h_r[1][:, second], 0)
+        nc.vector.memset(h_r[2][:, second], 0)
         for window in item_windows + user_windows:
             nc.gpsimd.memset(window[:], 0.0)
-
-        x_planes = keep.tile([P, PACK, L], F32, name="x_planes")
-        for t in range(PACK):
-            nc.vector.tensor_copy(x_planes[:, t, :], u_planes[t][:].indirect(user_list[:]))
-        nc.scalar.copy(
-            x_d[0][:].rearrange("p (s m t) -> p m t s", s=PACK, t=PACK),
-            x_planes[:].rearrange("p t (m s) -> p m t s", s=PACK),
-        )
-        turn(x_d[0][:].bitcast(F32).rearrange("p (s m u) -> p s m u", s=PACK, u=2), x_r[0], (6, 7))
 
         ts_row = keep.tile([P, L], F32, name="ts_row")
         nc.vector.tensor_copy(ts_row[:], ts_table[:].indirect(item_list[:]))
@@ -121,47 +128,74 @@ def tile_attend_gmf_hub_vu_kernel(tc, uT, vT, y, us, ts, offs, uoffs, out_0, out
         ts_cols = keep.tile([P, PACK], F32, name="ts_cols")
         nc.scalar.copy(ts_cols[:], ts_turned[:, 0:L:P])
         ts_spread = bank_tile(5)
-        for j in range(PACK):
-            nc.tensor.transpose(
-                ts_spread[:, j * P : (j + 1) * P], ts_cols[:, j : j + 1].to_broadcast([P, P]), identity[:]
-            )
-        scale = keep.tile([P, PACK, L], F32, name="scale")
+        ts_first = bank_tile(2)
+        for spread, blocks in ((ts_spread, PACK), (ts_first, 2)):
+            for j in range(blocks):
+                nc.tensor.transpose(
+                    spread[:, j * P : (j + 1) * P], ts_cols[:, j : j + 1].to_broadcast([P, P]), identity[:]
+                )
+        scale = keep.tile([P, PACK, HALF], F32, name="scale")
         for s in range(PACK):
-            nc.scalar.activation(
-                scale[:, s, :], ts_spread[:], COPY, scale=us_cols[:, s : s + 1]
+            nc.scalar.activation(scale[:, s, :], ts_first[:, first], COPY, scale=us_cols[:, s : s + 1])
+        x_planes = keep.tile([P, PACK * L], BF16, name="x_planes")
+        for t in range(PACK):
+            nc.vector.tensor_copy(x_planes[:, t * L : (t + 1) * L], u_planes[t][:].indirect(user_list[:]))
+        for n in range(2):
+            cols = slice(2 * n * L, 2 * (n + 1) * L)
+            turn_planes(x_planes[:, cols], (x_lo_values[:], late_values[:, 0 : 2 * L])[n], bank_tile(6 + n))
+        nc.scalar.copy(
+            x_d_values[:].rearrange("p (s m t) -> p m t s", s=PACK, t=PACK),
+            x_planes[:].rearrange("p (t m s) -> p m t s", t=PACK, s=PACK),
+        )
+
+        scale_packed = [keep.tile([P, HALF, PACK], F32, name="u_plane%d" % (2 + n), align_bytes=64) for n in range(2)]
+        for n, cols in enumerate(halves):
+            nc.vector.tensor_tensor(
+                scale_packed[n][:],
+                ts_spread[:, cols].unsqueeze(2).to_broadcast([P, HALF, PACK]),
+                us_cols[:].unsqueeze(1).to_broadcast([P, HALF, PACK]),
+                ALU.mult,
             )
 
         w_packed = w_d[0][:].rearrange("p (i t) -> p i t", t=PACK)
-        halves = (slice(0, HALF), slice(HALF, L))
-        for t in range(PACK - 1):
-            nc.vector.tensor_copy(w_packed[:, :, t], v_planes[t][:].indirect(item_list[:]))
-        quantize(x_d, E4M3)
-        warm = bank_tile(2)
-        for k in range(3):
-            product(warm[:], x_d, k, x_d, E4M3, slice(0, L))
-        scale_packed = keep.tile([P, L, PACK], F32, name="v_plane1", align_bytes=64)
-        nc.scalar.copy(scale_packed[:], scale[:].rearrange("p s i -> p i s"))
+        w_planes = keep.tile([P, 2 * L], BF16, name="w_planes")
+        for t in range(2):
+            nc.vector.tensor_copy(w_planes[:, t * L : (t + 1) * L], v_planes[t][:].indirect(item_list[:]))
+        nc.vector.tensor_copy(w_packed[:, :, 0:2], w_planes[:].rearrange("p (t i) -> p i t", t=2))
+        turn_planes(w_planes[:], late_values[:, 2 * L : 4 * L], bank_tile(3))
+        nc.vector.tensor_copy(w_packed[:, :, 2], v_planes[2][:].indirect(item_list[:]))
+        x_d = operand("x_d", x_d_values, "v_plane1")
+        quantize(x_d, E4M3, 0, L)
+        x_lo = operand("x_lo", x_lo_values, "v_plane0", columns=HALF)
+        quantize(x_lo, E4M3, 0, HALF)
         for cols in halves:
-            places = item_list[:, cols.start // 16 : cols.stop // 16]
-            nc.vector.tensor_copy(w_packed[:, cols, PACK - 1], v_planes[PACK - 1][:].indirect(places))
-        for cols in halves:
+            nc.vector.tensor_copy(w_packed[:, cols, 3], v_planes[3][:].indirect(places(item_list, cols)))
             quantize(w_d, E4M3, cols.start, cols.stop)
-        quantize(x_r, E4M3)
+        late = operand("late", late_values, "v_plane3")
+        quantize(late, E4M3, 0, L)
 
-        first, second = halves
-        pairs = (slice(0, 2), slice(2, 4))
+        quarters = [slice(q * P, (q + 1) * P) for q in range(PACK)]
         residual = keep.tile([P, PACK, L], F32, name="residual")
         scaled = keep.tile([P, PACK, HALF], F32, name="scaled")
-        for n, rows in enumerate(pairs):
-            acc = bank_tile(n)
-            for e in range(2):
-                product(acc[:, e * HALF : (e + 1) * HALF], x_d, rows.start + e, w_d, E4M3, first)
-            nc.vector.tensor_tensor(
-                scaled[:, rows, :], acc[:].rearrange("p (e i) -> p e i", e=2), scale[:, rows, first], ALU.mult
-            )
-        for rows in pairs:
-            nc.vector.tensor_tensor(residual[:, rows, first], scaled[:, rows, :], y_rows[:, rows, first], ALU.subtract)
+        clipped = keep.tile([P, L, PACK], F32, name="clipped")
+        h_packed = h_r[0][:].rearrange("p (i s) -> p i s", s=PACK)
 
+        def clip(cols):
+            nc.vector.tensor_scalar(
+                clipped[:, cols, :], residual[:, :, cols].rearrange("p s i -> p i s"), -1.0, 1.0, ALU.max, ALU.min
+            )
+
+        def weigh(cols):
+            factors = scale_packed[cols.start // HALF][:, cols.start % HALF : cols.start % HALF + P, :]
+            nc.vector.tensor_tensor(h_packed[:, cols, :], clipped[:, cols, :], factors, ALU.mult)
+
+        for q in range(2):
+            acc = bank_tile(q)
+            for s in range(PACK):
+                product(acc[:, s * P : (s + 1) * P], x_d, s, w_d, E4M3, quarters[q])
+            nc.vector.tensor_tensor(
+                scaled[:, :, quarters[q]], acc[:].rearrange("p (s i) -> p s i", s=PACK), scale[:, :, quarters[q]], ALU.mult
+            )
         back = [bank_tile(4), bank_tile(5)]
         for j in (2, 3):
             acc = bank_tile(j)
@@ -169,57 +203,76 @@ def tile_attend_gmf_hub_vu_kernel(tc, uT, vT, y, us, ts, offs, uoffs, out_0, out
             item_scaled = keep.tile([P, L], F32, name="item_scaled%d" % j)
             nc.scalar.activation(item_scaled[:], acc[:], COPY, scale=ts_cols[:, j : j + 1])
             for s in range(PACK):
-                c = (s % 2) * HALF + (j - 2) * P
-                nc.tensor.transpose(back[s // 2][:, c : c + P], item_scaled[:, s * P : (s + 1) * P], identity[:])
-        for s in range(PACK):
-            c = (s % 2) * HALF
-            nc.vector.scalar_tensor_tensor(
-                residual[:, s, second],
-                back[s // 2][:, c : c + HALF],
-                us_cols[:, s : s + 1],
-                y_rows[:, s, second],
-                ALU.mult,
-                ALU.subtract,
-            )
-        turn(w_d[0][:].bitcast(F32).rearrange("p (m s u) -> p s m u", s=PACK, u=2), w_i_values, (3, 4))
-
-        clipped = keep.tile([P, L, PACK], F32, name="clipped", align_bytes=64)
-        for cols in halves:
-            nc.vector.tensor_scalar(
-                clipped[:, cols, :], residual[:, :, cols].rearrange("p s i -> p i s"), -1.0, 1.0, ALU.max, ALU.min
-            )
-        h_packed = h_r[0][:].rearrange("p (i s) -> p i s", s=PACK)
-        for cols in halves:
-            nc.vector.tensor_tensor(h_packed[:, cols, :], clipped[:, cols, :], scale_packed[:, cols, :], ALU.mult)
-        for cols in halves:
+                nc.tensor.transpose(
+                    back[j - 2][:, s * P : (s + 1) * P], item_scaled[:, s * P : (s + 1) * P], identity[:]
+                )
+        for cols in quarters[:2]:
+            nc.vector.tensor_tensor(residual[:, :, cols], scaled[:, :, cols], y_rows[:, :, cols], ALU.subtract)
+        for step in (clip, weigh):
+            for cols in quarters[:2]:
+                step(cols)
+        for cols in quarters[:2]:
             quantize(h_r, E5M2, cols.start, cols.stop)
-        w_i = operand("w_i", w_i_values, "clipped")
-        quantize(w_i, E4M3)
 
-        def finish(side, bank, stationary, moving, k, windows, places, out, pieces):
+        out_rows = {
+            "item": out_0.rearrange("(p t) c -> t p c", t=PACK),
+            "user": out_1.rearrange("(p t) c -> t p c", t=PACK),
+        }
+        windows = {"item": item_windows, "user": user_windows}
+        lists = {"item": item_list, "user": user_list}
+
+        def sums_of(side, k, bank, stationary, block, moving, cols):
             acc = bank_tile(bank)
-            product(acc[:], stationary, k, moving, E5M2, slice(0, L))
-            sums = keep.tile([P, L], F32, name="%s_sums%d" % (side, k), align_bytes=64)
-            window = windows[k % WINDOWS]
-            for cols in pieces:
-                nc.scalar.copy(sums[:, cols], acc[:, cols])
-                nc.vector.tensor_copy(window[:].indirect(places[:, cols.start // 16 : cols.stop // 16]), sums[:, cols])
-            nc.sync.dma_start(out[k * P : (k + 1) * P, :], window[:])
+            product(acc[:], stationary, block, moving, E5M2, slice(0, L))
+            sums = keep.tile([P, cols.stop - cols.start], F32, name="%s_sums%d_%d" % (side, k, cols.stop), align_bytes=64)
+            nc.scalar.copy(sums[:], acc[:, cols])
+            return sums
 
-        def items(k):
-            finish("item", (0, 1, 2, 5)[k], x_r, h_r, k, item_windows, item_list, out_0, halves if k == 0 else (slice(0, L),))
+        def scatter(side, k, sums, cols):
+            window = windows[side][k % WINDOWS]
+            nc.vector.tensor_copy(window[:].indirect(places(lists[side], cols)), sums[:])
+            if cols.stop == L:
+                nc.sync.dma_start(out_rows[side][k], window[:])
 
-        def users(k):
-            finish("user", (6, 7, 3, 4)[k], w_i, h_i, k, user_windows, user_list, out_1, (slice(0, L),))
+        early = sums_of("item", 0, 6, x_lo, 0, h_r, first)
 
-        items(0)
-        items(1)
-        turn(h_r[0][:].bitcast(F32).rearrange("p (m s u) -> p s m u", s=PACK, u=2), h_i_values, (0, 1))
-        items(2)
-        h_i = operand("h_i", h_i_values, "item_sums1")
-        quantize(h_i, E5M2)
-        items(3)
-        users(0)
-        users(1)
-        users(2)
-        users(3)
+        for q in (2, 3):
+            for s in range(PACK):
+                nc.vector.scalar_tensor_tensor(
+                    residual[:, s, quarters[q]],
+                    back[q - 2][:, s * P : (s + 1) * P],
+                    us_cols[:, s : s + 1],
+                    y_rows[:, s, quarters[q]],
+                    ALU.mult,
+                    ALU.subtract,
+                )
+        for step in (clip, weigh):
+            for cols in quarters[2:]:
+                step(cols)
+        for cols in quarters[2:]:
+            quantize(h_r, E5M2, cols.start, cols.stop)
+        scatter("item", 0, early, first)
+
+        whole = slice(0, L)
+        scatter("item", 0, sums_of("item", 0, 7, x_lo, 0, h_r, second), second)
+        scatter("item", 1, sums_of("item", 1, 0, x_lo, 1, h_r, whole), whole)
+        item2 = sums_of("item", 2, 1, late, 0, h_r, whole)
+        item3 = sums_of("item", 3, 2, late, 1, h_r, whole)
+
+        turned = h_i_values[:].rearrange("m (p u e s) -> m p u e s", u=2, e=2, s=PACK)
+        for u in range(2):
+            pairs = turn_pairs(h_r[0], u, bank_tile((7, 0)[u]))
+            nc.scalar.copy(turned[:, :, u, :, :], pairs.rearrange("m (s p e) -> m p e s", s=PACK, e=2))
+        pairs = turn_pairs(w_d[0], 1, bank_tile(1))
+        nc.scalar.copy(
+            w_hi_values[:].rearrange("m (e p s) -> m e p s", e=2, s=PACK),
+            pairs.rearrange("m (s p e) -> m e p s", s=PACK, e=2),
+        )
+        scatter("item", 2, item2, whole)
+        h_i = operand("h_i", h_i_values, "item_sums1_512")
+        quantize(h_i, E5M2, 0, L)
+        w_hi = operand("w_hi", w_hi_values, "item_sums2_512", columns=HALF)
+        quantize(w_hi, E4M3, 0, HALF)
+        scatter("item", 3, item3, whole)
+        for k in range(PACK):
+            scatter("user", k, sums_of("user", k, 3 + k, (late, w_hi)[k // 2], (2, 3, 0, 1)[k], h_i, whole), whole)

@@ -38,7 +38,7 @@ def tile_attend_gmf_hub_vu_kernel(tc, uT, vT, y, us, ts, offs, uoffs, out_0, out
         v_planes = [keep.tile([P, T], F32, name="v_plane%d" % t, align_bytes=64) for t in range(PACK)]
         ts_table = keep.tile([P, T], F32, name="ts_table")
         us_cols = keep.tile([P, PACK], F32, name="us_cols")
-        y_rows = keep.tile([P, PACK, L], F32, name="y_rows")
+        y_rows = keep.tile([P, PACK, L], F32, name="y_rows", align_bytes=64)
         item_windows = [keep.tile([P, T], F32, name="item_window%d" % k) for k in range(WINDOWS)]
         user_windows = [keep.tile([P, T], F32, name="user_window%d" % k) for k in range(WINDOWS)]
         identity = keep.tile([P, P], F32, name="identity")
@@ -102,7 +102,8 @@ def tile_attend_gmf_hub_vu_kernel(tc, uT, vT, y, us, ts, offs, uoffs, out_0, out
 
         u_rows = uT.rearrange("(p t) c -> t p c", t=PACK)
         v_rows = vT.rearrange("(p t) c -> t p c", t=PACK)
-        nc.vector.memset(ts_table[:].bitcast(U32), 0)
+        nc.gpsimd.memset(ts_table[:, 0 : T // 2], 0.0)
+        nc.vector.memset(ts_table[:, T // 2 : T], 0.0)
         nc.sync.dma_start(u_planes[0][:], u_rows[0])
         nc.sync.dma_start(user_list[:], uoffs)
         nc.sync.dma_start(item_list[:], offs)
@@ -142,13 +143,13 @@ def tile_attend_gmf_hub_vu_kernel(tc, uT, vT, y, us, ts, offs, uoffs, out_0, out
             nc.vector.tensor_copy(x_planes[:, t * L : (t + 1) * L], u_planes[t][:].indirect(user_list[:]))
         for n in range(2):
             cols = slice(2 * n * L, 2 * (n + 1) * L)
+            nc.scalar.copy(
+                x_d_values[:].rearrange("p (s m t) -> p s m t", s=PACK, t=PACK)[:, :, :, 2 * n : 2 * n + 2],
+                x_planes[:, cols].rearrange("p (t m s) -> p s m t", t=2, s=PACK),
+            )
             turn_planes(x_planes[:, cols], (x_lo_values[:], late_values[:, 0 : 2 * L])[n], bank_tile(6 + n))
-        nc.scalar.copy(
-            x_d_values[:].rearrange("p (s m t) -> p m t s", s=PACK, t=PACK),
-            x_planes[:].rearrange("p (t m s) -> p m t s", t=PACK, s=PACK),
-        )
 
-        scale_packed = [keep.tile([P, HALF, PACK], F32, name="u_plane%d" % (2 + n), align_bytes=64) for n in range(2)]
+        scale_packed = [keep.tile([P, HALF, PACK], F32, name="u_plane%d" % (1 + n), align_bytes=64) for n in range(2)]
         for n, cols in enumerate(halves):
             nc.vector.tensor_tensor(
                 scale_packed[n][:],
@@ -164,9 +165,9 @@ def tile_attend_gmf_hub_vu_kernel(tc, uT, vT, y, us, ts, offs, uoffs, out_0, out
         nc.vector.tensor_copy(w_packed[:, :, 0:2], w_planes[:].rearrange("p (t i) -> p i t", t=2))
         turn_planes(w_planes[:], late_values[:, 2 * L : 4 * L], bank_tile(3))
         nc.vector.tensor_copy(w_packed[:, :, 2], v_planes[2][:].indirect(item_list[:]))
-        x_d = operand("x_d", x_d_values, "v_plane1")
+        x_d = operand("x_d", x_d_values, "v_plane0")
         quantize(x_d, E4M3, 0, L)
-        x_lo = operand("x_lo", x_lo_values, "v_plane0", columns=HALF)
+        x_lo = operand("x_lo", x_lo_values, "v_plane1", columns=HALF)
         quantize(x_lo, E4M3, 0, HALF)
         for cols in halves:
             nc.vector.tensor_copy(w_packed[:, cols, 3], v_planes[3][:].indirect(places(item_list, cols)))
@@ -177,17 +178,17 @@ def tile_attend_gmf_hub_vu_kernel(tc, uT, vT, y, us, ts, offs, uoffs, out_0, out
         quarters = [slice(q * P, (q + 1) * P) for q in range(PACK)]
         residual = keep.tile([P, PACK, L], F32, name="residual")
         scaled = keep.tile([P, PACK, HALF], F32, name="scaled")
-        clipped = keep.tile([P, L, PACK], F32, name="clipped")
+        clipped = [keep.tile([P, P, PACK], F32, name="clipped%d" % q, align_bytes=64) for q in range(PACK)]
         h_packed = h_r[0][:].rearrange("p (i s) -> p i s", s=PACK)
 
-        def clip(cols):
-            nc.vector.tensor_scalar(
-                clipped[:, cols, :], residual[:, :, cols].rearrange("p s i -> p i s"), -1.0, 1.0, ALU.max, ALU.min
+        def clip(cols, engine=nc.vector):
+            engine.tensor_scalar(
+                clipped[cols.start // P][:], residual[:, :, cols].rearrange("p s i -> p i s"), -1.0, 1.0, ALU.max, ALU.min
             )
 
-        def weigh(cols):
+        def weigh(cols, engine=nc.vector):
             factors = scale_packed[cols.start // HALF][:, cols.start % HALF : cols.start % HALF + P, :]
-            nc.vector.tensor_tensor(h_packed[:, cols, :], clipped[:, cols, :], factors, ALU.mult)
+            engine.tensor_tensor(h_packed[:, cols, :], clipped[cols.start // P][:], factors, ALU.mult)
 
         for q in range(2):
             acc = bank_tile(q)
@@ -203,9 +204,8 @@ def tile_attend_gmf_hub_vu_kernel(tc, uT, vT, y, us, ts, offs, uoffs, out_0, out
             item_scaled = keep.tile([P, L], F32, name="item_scaled%d" % j)
             nc.scalar.activation(item_scaled[:], acc[:], COPY, scale=ts_cols[:, j : j + 1])
             for s in range(PACK):
-                nc.tensor.transpose(
-                    back[j - 2][:, s * P : (s + 1) * P], item_scaled[:, s * P : (s + 1) * P], identity[:]
-                )
+                c = (s % 2) * HALF + (j - 2) * P
+                nc.tensor.transpose(back[s // 2][:, c : c + P], item_scaled[:, s * P : (s + 1) * P], identity[:])
         for cols in quarters[:2]:
             nc.vector.tensor_tensor(residual[:, :, cols], scaled[:, :, cols], y_rows[:, :, cols], ALU.subtract)
         for step in (clip, weigh):
@@ -221,10 +221,10 @@ def tile_attend_gmf_hub_vu_kernel(tc, uT, vT, y, us, ts, offs, uoffs, out_0, out
         windows = {"item": item_windows, "user": user_windows}
         lists = {"item": item_list, "user": user_list}
 
-        def sums_of(side, k, bank, stationary, block, moving, cols):
+        def sums_of(side, k, bank, stationary, block, moving, cols, tag=None):
             acc = bank_tile(bank)
             product(acc[:], stationary, block, moving, E5M2, slice(0, L))
-            sums = keep.tile([P, cols.stop - cols.start], F32, name="%s_sums%d_%d" % (side, k, cols.stop), align_bytes=64)
+            sums = keep.tile([P, cols.stop - cols.start], F32, name=tag or "%s_sums%d_%d" % (side, k, cols.stop), align_bytes=64)
             nc.scalar.copy(sums[:], acc[:, cols])
             return sums
 
@@ -234,45 +234,53 @@ def tile_attend_gmf_hub_vu_kernel(tc, uT, vT, y, us, ts, offs, uoffs, out_0, out
             if cols.stop == L:
                 nc.sync.dma_start(out_rows[side][k], window[:])
 
-        early = sums_of("item", 0, 6, x_lo, 0, h_r, first)
+        x_r = ((x_lo, 0), (x_lo, 1), (late, 0), (late, 1))
+        early = [bank_tile(b) for b in (6, 7, 0)]
+        for k in range(3):
+            product(early[k][:], *x_r[k], h_r, E5M2, slice(0, L))
 
-        for q in (2, 3):
-            for s in range(PACK):
-                nc.vector.scalar_tensor_tensor(
-                    residual[:, s, quarters[q]],
-                    back[q - 2][:, s * P : (s + 1) * P],
-                    us_cols[:, s : s + 1],
-                    y_rows[:, s, quarters[q]],
-                    ALU.mult,
-                    ALU.subtract,
-                )
-        for step in (clip, weigh):
-            for cols in quarters[2:]:
-                step(cols)
+        def scatter_early(k, tag):
+            sums = keep.tile([P, HALF], F32, name=tag, align_bytes=64)
+            nc.scalar.copy(sums[:], early[k][:, first])
+            scatter("item", k, sums, first)
+
+        for s in range(PACK):
+            c = (s % 2) * HALF
+            nc.vector.scalar_tensor_tensor(
+                residual[:, s, second],
+                back[s // 2][:, c : c + HALF],
+                us_cols[:, s : s + 1],
+                y_rows[:, s, second],
+                ALU.mult,
+                ALU.subtract,
+            )
+        for cols in quarters[2:]:
+            clip(cols)
+            weigh(cols, nc.gpsimd)
+        scatter_early(0, "y_rows")
+        scatter_early(1, "early_sums")
         for cols in quarters[2:]:
             quantize(h_r, E5M2, cols.start, cols.stop)
-        scatter("item", 0, early, first)
+        scatter_early(2, "clipped3")
 
         whole = slice(0, L)
-        scatter("item", 0, sums_of("item", 0, 7, x_lo, 0, h_r, second), second)
-        scatter("item", 1, sums_of("item", 1, 0, x_lo, 1, h_r, whole), whole)
-        item2 = sums_of("item", 2, 1, late, 0, h_r, whole)
-        item3 = sums_of("item", 3, 2, late, 1, h_r, whole)
+        for k in range(3):
+            scatter("item", k, sums_of("item", k, (1, 2, 3)[k], *x_r[k], h_r, second), second)
+        item3 = sums_of("item", 3, 6, *x_r[3], h_r, whole)
 
         turned = h_i_values[:].rearrange("m (p u e s) -> m p u e s", u=2, e=2, s=PACK)
         for u in range(2):
-            pairs = turn_pairs(h_r[0], u, bank_tile((7, 0)[u]))
+            pairs = turn_pairs(h_r[0], u, bank_tile((1, 2)[u]))
             nc.scalar.copy(turned[:, :, u, :, :], pairs.rearrange("m (s p e) -> m p e s", s=PACK, e=2))
-        pairs = turn_pairs(w_d[0], 1, bank_tile(1))
+        pairs = turn_pairs(w_d[0], 1, bank_tile(0))
         nc.scalar.copy(
             w_hi_values[:].rearrange("m (e p s) -> m e p s", e=2, s=PACK),
             pairs.rearrange("m (s p e) -> m e p s", s=PACK, e=2),
         )
-        scatter("item", 2, item2, whole)
-        h_i = operand("h_i", h_i_values, "item_sums1_512")
-        quantize(h_i, E5M2, 0, L)
-        w_hi = operand("w_hi", w_hi_values, "item_sums2_512", columns=HALF)
+        w_hi = operand("w_hi", w_hi_values, "item_sums1_512", columns=HALF)
         quantize(w_hi, E4M3, 0, HALF)
+        h_i = operand("h_i", h_i_values, "item_sums2_512")
+        quantize(h_i, E5M2, 0, L)
         scatter("item", 3, item3, whole)
         for k in range(PACK):
             scatter("user", k, sums_of("user", k, 3 + k, (late, w_hi)[k // 2], (2, 3, 0, 1)[k], h_i, whole), whole)

@@ -37,7 +37,7 @@ def tile_attend_gmf_hub_vu_kernel(tc, uT, vT, y, us, ts, offs, uoffs, out_0, out
         u_planes = [keep.tile([P, T], F32, name="u_plane%d" % t, align_bytes=64) for t in range(PACK)]
         v_planes = [keep.tile([P, T], F32, name="v_plane%d" % t, align_bytes=64) for t in range(PACK)]
         ts_table = keep.tile([P, T], F32, name="ts_table")
-        us_cols = keep.tile([P, PACK], F32, name="us_cols")
+        us_cols = keep.tile([P, PACK], F32, name="us_cols", align_bytes=64)
         y_rows = keep.tile([P, PACK, L], F32, name="y_rows", align_bytes=64)
         item_windows = [keep.tile([P, T], F32, name="item_window%d" % k) for k in range(WINDOWS)]
         user_windows = [keep.tile([P, T], F32, name="user_window%d" % k) for k in range(WINDOWS)]
@@ -46,9 +46,9 @@ def tile_attend_gmf_hub_vu_kernel(tc, uT, vT, y, us, ts, offs, uoffs, out_0, out
         def packed_values(name, columns=L):
             return keep.tile([P, columns * PACK], BF16, name=name + "_values", align_bytes=64)
 
-        def operand(name, values, codes_tag=None, columns=L):
+        def operand(name, values, codes_tag=None, columns=L, scales_tag=None):
             codes = keep.tile([P, columns], U32, name=codes_tag or name + "_codes", align_bytes=64)
-            scales = keep.tile([P, columns], U8, name=name + "_scales", align_bytes=64)
+            scales = keep.tile([P, columns], U8, name=scales_tag or name + "_scales", align_bytes=64)
             return values, codes, scales
 
         def quantize(op, fmt, lo, hi):
@@ -167,7 +167,7 @@ def tile_attend_gmf_hub_vu_kernel(tc, uT, vT, y, us, ts, offs, uoffs, out_0, out
         nc.vector.tensor_copy(w_packed[:, :, 2], v_planes[2][:].indirect(item_list[:]))
         x_d = operand("x_d", x_d_values, "v_plane0")
         quantize(x_d, E4M3, 0, L)
-        x_lo = operand("x_lo", x_lo_values, "v_plane1", columns=HALF)
+        x_lo = operand("x_lo", x_lo_values, "u_plane3", columns=HALF)
         quantize(x_lo, E4M3, 0, HALF)
         for cols in halves:
             nc.vector.tensor_copy(w_packed[:, cols, 3], v_planes[3][:].indirect(places(item_list, cols)))
@@ -181,8 +181,8 @@ def tile_attend_gmf_hub_vu_kernel(tc, uT, vT, y, us, ts, offs, uoffs, out_0, out
         clipped = [keep.tile([P, P, PACK], F32, name="clipped%d" % q, align_bytes=64) for q in range(PACK)]
         h_packed = h_r[0][:].rearrange("p (i s) -> p i s", s=PACK)
 
-        def clip(cols, engine=nc.vector):
-            engine.tensor_scalar(
+        def clip(cols):
+            nc.vector.tensor_scalar(
                 clipped[cols.start // P][:], residual[:, :, cols].rearrange("p s i -> p i s"), -1.0, 1.0, ALU.max, ALU.min
             )
 
@@ -211,8 +211,6 @@ def tile_attend_gmf_hub_vu_kernel(tc, uT, vT, y, us, ts, offs, uoffs, out_0, out
         for step in (clip, weigh):
             for cols in quarters[:2]:
                 step(cols)
-        for cols in quarters[:2]:
-            quantize(h_r, E5M2, cols.start, cols.stop)
 
         out_rows = {
             "item": out_0.rearrange("(p t) c -> t p c", t=PACK),
@@ -221,28 +219,29 @@ def tile_attend_gmf_hub_vu_kernel(tc, uT, vT, y, us, ts, offs, uoffs, out_0, out
         windows = {"item": item_windows, "user": user_windows}
         lists = {"item": item_list, "user": user_list}
 
-        def sums_of(side, k, bank, stationary, block, moving, cols, tag=None):
+        def sums_of(side, k, bank, stationary, block, moving, cols):
             acc = bank_tile(bank)
             product(acc[:], stationary, block, moving, E5M2, slice(0, L))
-            sums = keep.tile([P, cols.stop - cols.start], F32, name=tag or "%s_sums%d_%d" % (side, k, cols.stop), align_bytes=64)
+            sums = keep.tile([P, cols.stop - cols.start], F32, name="%s_sums%d_%d" % (side, k, cols.stop), align_bytes=64)
             nc.scalar.copy(sums[:], acc[:, cols])
-            return sums
+            return sums[:]
 
         def scatter(side, k, sums, cols):
             window = windows[side][k % WINDOWS]
-            nc.vector.tensor_copy(window[:].indirect(places(lists[side], cols)), sums[:])
+            nc.vector.tensor_copy(window[:].indirect(places(lists[side], cols)), sums)
             if cols.stop == L:
                 nc.sync.dma_start(out_rows[side][k], window[:])
 
         x_r = ((x_lo, 0), (x_lo, 1), (late, 0), (late, 1))
+        quantize(h_r, E5M2, 0, HALF)
         early = [bank_tile(b) for b in (6, 7, 0)]
         for k in range(3):
             product(early[k][:], *x_r[k], h_r, E5M2, slice(0, L))
-
-        def scatter_early(k, tag):
-            sums = keep.tile([P, HALF], F32, name=tag, align_bytes=64)
-            nc.scalar.copy(sums[:], early[k][:, first])
-            scatter("item", k, sums, first)
+        pairs = turn_pairs(w_d[0], 1, bank_tile(3))
+        nc.scalar.copy(
+            w_hi_values[:].rearrange("m (e p s) -> m e p s", e=2, s=PACK),
+            pairs.rearrange("m (s p e) -> m e p s", s=PACK, e=2),
+        )
 
         for s in range(PACK):
             c = (s % 2) * HALF
@@ -254,33 +253,31 @@ def tile_attend_gmf_hub_vu_kernel(tc, uT, vT, y, us, ts, offs, uoffs, out_0, out
                 ALU.mult,
                 ALU.subtract,
             )
+        w_hi = operand("w_hi", w_hi_values, columns=HALF, scales_tag="us_cols")
+        quantize(w_hi, E4M3, 0, HALF)
         for cols in quarters[2:]:
             clip(cols)
             weigh(cols, nc.gpsimd)
-        scatter_early(0, "y_rows")
-        scatter_early(1, "early_sums")
-        for cols in quarters[2:]:
-            quantize(h_r, E5M2, cols.start, cols.stop)
-        scatter_early(2, "clipped3")
+        early_sums = keep.tile([P, L], F32, name="y_rows", align_bytes=64)
+        for k in range(2):
+            nc.scalar.copy(early_sums[:, halves[k]], early[k][:, first])
+            scatter("item", k, early_sums[:, halves[k]], first)
+        quantize(h_r, E5M2, HALF, L)
+        held_sums = keep.tile([P, HALF], F32, name="clipped3", align_bytes=64)
+        nc.scalar.copy(held_sums[:], early[2][:, first])
+        scatter("item", 2, held_sums[:], first)
 
         whole = slice(0, L)
         for k in range(3):
-            scatter("item", k, sums_of("item", k, (1, 2, 3)[k], *x_r[k], h_r, second), second)
+            scatter("item", k, sums_of("item", k, 1 + k, *x_r[k], h_r, second), second)
         item3 = sums_of("item", 3, 6, *x_r[3], h_r, whole)
 
         turned = h_i_values[:].rearrange("m (p u e s) -> m p u e s", u=2, e=2, s=PACK)
         for u in range(2):
-            pairs = turn_pairs(h_r[0], u, bank_tile((1, 2)[u]))
+            pairs = turn_pairs(h_r[0], u, bank_tile((2, 3)[u]))
             nc.scalar.copy(turned[:, :, u, :, :], pairs.rearrange("m (s p e) -> m p e s", s=PACK, e=2))
-        pairs = turn_pairs(w_d[0], 1, bank_tile(0))
-        nc.scalar.copy(
-            w_hi_values[:].rearrange("m (e p s) -> m e p s", e=2, s=PACK),
-            pairs.rearrange("m (s p e) -> m e p s", s=PACK, e=2),
-        )
-        w_hi = operand("w_hi", w_hi_values, "item_sums1_512", columns=HALF)
-        quantize(w_hi, E4M3, 0, HALF)
         h_i = operand("h_i", h_i_values, "item_sums2_512")
         quantize(h_i, E5M2, 0, L)
         scatter("item", 3, item3, whole)
         for k in range(PACK):
-            scatter("user", k, sums_of("user", k, 3 + k, (late, w_hi)[k // 2], (2, 3, 0, 1)[k], h_i, whole), whole)
+            scatter("user", k, sums_of("user", k, 4 + k, (late, w_hi)[k // 2], (2, 3, 0, 1)[k], h_i, whole), whole)

@@ -92,8 +92,9 @@ def tile_attend_gmf_hub_vu_kernel(tc, uT, vT, y, us, ts, offs, uoffs, out_0, out
         def places(offsets, cols):
             return offsets[:, cols.start // 16 : cols.stop // 16]
 
-        x_d_values = packed_values("x_d")
-        x_lo_values = packed_values("x_lo", HALF)
+        x_values = packed_values("x", L + HALF)
+        x_d_values = x_values[:, 0 : PACK * L]
+        x_lo_values = x_values[:, PACK * L : PACK * (L + HALF)]
         late_values = packed_values("late")
         w_d = operand("w_d", packed_values("w_d"))
         h_r = operand("h_r", packed_values("h_r"))
@@ -102,8 +103,8 @@ def tile_attend_gmf_hub_vu_kernel(tc, uT, vT, y, us, ts, offs, uoffs, out_0, out
 
         u_rows = uT.rearrange("(p t) c -> t p c", t=PACK)
         v_rows = vT.rearrange("(p t) c -> t p c", t=PACK)
-        nc.gpsimd.memset(ts_table[:, 0 : T // 2], 0.0)
-        nc.vector.memset(ts_table[:, T // 2 : T], 0.0)
+        nc.vector.memset(ts_table[:], 0.0)
+        nc.vector.memset(item_windows[0][:], 0.0)
         nc.sync.dma_start(u_planes[0][:], u_rows[0])
         nc.sync.dma_start(user_list[:], uoffs)
         nc.sync.dma_start(item_list[:], offs)
@@ -116,9 +117,11 @@ def tile_attend_gmf_hub_vu_kernel(tc, uT, vT, y, us, ts, offs, uoffs, out_0, out
         nc.sync.dma_start(y_rows[:], y.rearrange("b (p s) i -> p (b s) i", s=PACK))
 
         make_identity(nc, identity[:])
-        nc.vector.memset(h_r[1][:, second], 0)
-        nc.vector.memset(h_r[2][:, second], 0)
-        for window in item_windows + user_windows:
+        nc.gpsimd.memset(h_r[1][:, second], 0)
+        nc.gpsimd.memset(h_r[2][:, second], 0)
+        nc.gpsimd.memset(item_windows[1][:, 0 : T // 2], 0.0)
+        nc.gpsimd.memset(item_windows[1][:, T // 2 : T], 0.0)
+        for window in item_windows[2:] + user_windows:
             nc.gpsimd.memset(window[:], 0.0)
 
         ts_row = keep.tile([P, L], F32, name="ts_row")
@@ -144,12 +147,16 @@ def tile_attend_gmf_hub_vu_kernel(tc, uT, vT, y, us, ts, offs, uoffs, out_0, out
         for n in range(2):
             cols = slice(2 * n * L, 2 * (n + 1) * L)
             nc.scalar.copy(
-                x_d_values[:].rearrange("p (s m t) -> p s m t", s=PACK, t=PACK)[:, :, :, 2 * n : 2 * n + 2],
+                x_d_values.rearrange("p (s m t) -> p s m t", s=PACK, t=PACK)[:, :, :, 2 * n : 2 * n + 2],
                 x_planes[:, cols].rearrange("p (t m s) -> p s m t", t=2, s=PACK),
             )
-            turn_planes(x_planes[:, cols], (x_lo_values[:], late_values[:, 0 : 2 * L])[n], bank_tile(6 + n))
+            turn_planes(x_planes[:, cols], (x_lo_values, late_values[:, 0 : 2 * L])[n], bank_tile(6 + n))
 
-        scale_packed = [keep.tile([P, HALF, PACK], F32, name="u_plane%d" % (1 + n), align_bytes=64) for n in range(2)]
+        w_packed = w_d[0][:].rearrange("p (i t) -> p i t", t=PACK)
+        w_planes = keep.tile([P, 2 * L], BF16, name="w_planes")
+        for t in range(2):
+            nc.vector.tensor_copy(w_planes[:, t * L : (t + 1) * L], v_planes[t][:].indirect(item_list[:]))
+        scale_packed = [keep.tile([P, HALF, PACK], F32, name=("u_plane3", "v_plane0")[n], align_bytes=64) for n in range(2)]
         for n, cols in enumerate(halves):
             nc.vector.tensor_tensor(
                 scale_packed[n][:],
@@ -158,17 +165,12 @@ def tile_attend_gmf_hub_vu_kernel(tc, uT, vT, y, us, ts, offs, uoffs, out_0, out
                 ALU.mult,
             )
 
-        w_packed = w_d[0][:].rearrange("p (i t) -> p i t", t=PACK)
-        w_planes = keep.tile([P, 2 * L], BF16, name="w_planes")
-        for t in range(2):
-            nc.vector.tensor_copy(w_planes[:, t * L : (t + 1) * L], v_planes[t][:].indirect(item_list[:]))
-        nc.vector.tensor_copy(w_packed[:, :, 0:2], w_planes[:].rearrange("p (t i) -> p i t", t=2))
+        nc.scalar.copy(w_packed[:, :, 0:2], w_planes[:].rearrange("p (t i) -> p i t", t=2))
         turn_planes(w_planes[:], late_values[:, 2 * L : 4 * L], bank_tile(3))
         nc.vector.tensor_copy(w_packed[:, :, 2], v_planes[2][:].indirect(item_list[:]))
-        x_d = operand("x_d", x_d_values, "v_plane0")
+        x_d = operand("x", x_values, "v_plane1", columns=L + HALF)
+        quantize(x_d, E4M3, L, L + HALF)
         quantize(x_d, E4M3, 0, L)
-        x_lo = operand("x_lo", x_lo_values, "u_plane3", columns=HALF)
-        quantize(x_lo, E4M3, 0, HALF)
         for cols in halves:
             nc.vector.tensor_copy(w_packed[:, cols, 3], v_planes[3][:].indirect(places(item_list, cols)))
             quantize(w_d, E4M3, cols.start, cols.stop)
@@ -208,9 +210,10 @@ def tile_attend_gmf_hub_vu_kernel(tc, uT, vT, y, us, ts, offs, uoffs, out_0, out
                 nc.tensor.transpose(back[s // 2][:, c : c + P], item_scaled[:, s * P : (s + 1) * P], identity[:])
         for cols in quarters[:2]:
             nc.vector.tensor_tensor(residual[:, :, cols], scaled[:, :, cols], y_rows[:, :, cols], ALU.subtract)
-        for step in (clip, weigh):
-            for cols in quarters[:2]:
-                step(cols)
+        for cols in quarters[:2]:
+            clip(cols)
+        weigh(quarters[0])
+        weigh(quarters[1], nc.gpsimd)
 
         out_rows = {
             "item": out_0.rearrange("(p t) c -> t p c", t=PACK),
@@ -232,11 +235,7 @@ def tile_attend_gmf_hub_vu_kernel(tc, uT, vT, y, us, ts, offs, uoffs, out_0, out
             if cols.stop == L:
                 nc.sync.dma_start(out_rows[side][k], window[:])
 
-        x_r = ((x_lo, 0), (x_lo, 1), (late, 0), (late, 1))
-        quantize(h_r, E5M2, 0, HALF)
-        early = [bank_tile(b) for b in (6, 7, 0)]
-        for k in range(3):
-            product(early[k][:], *x_r[k], h_r, E5M2, slice(0, L))
+        x_r = ((x_d, 4), (x_d, 5), (late, 0), (late, 1))
         pairs = turn_pairs(w_d[0], 1, bank_tile(3))
         nc.scalar.copy(
             w_hi_values[:].rearrange("m (e p s) -> m e p s", e=2, s=PACK),
@@ -253,12 +252,16 @@ def tile_attend_gmf_hub_vu_kernel(tc, uT, vT, y, us, ts, offs, uoffs, out_0, out
                 ALU.mult,
                 ALU.subtract,
             )
+        quantize(h_r, E5M2, 0, HALF)
+        early = [bank_tile(b) for b in (6, 7, 0)]
+        for k in range(3):
+            product(early[k][:], *x_r[k], h_r, E5M2, slice(0, L))
         w_hi = operand("w_hi", w_hi_values, columns=HALF, scales_tag="us_cols")
         quantize(w_hi, E4M3, 0, HALF)
         for cols in quarters[2:]:
             clip(cols)
             weigh(cols, nc.gpsimd)
-        early_sums = keep.tile([P, L], F32, name="y_rows", align_bytes=64)
+        early_sums = keep.tile([P, L], F32, name="early_sums", align_bytes=64)
         for k in range(2):
             nc.scalar.copy(early_sums[:, halves[k]], early[k][:, first])
             scatter("item", k, early_sums[:, halves[k]], first)

@@ -131,16 +131,15 @@ def tile_attend_gmf_hub_vu_kernel(tc, uT, vT, y, us, ts, offs, uoffs, out_0, out
             nc.tensor.transpose(ts_turned[:, j * P : (j + 1) * P], ts_row[:, j * P : (j + 1) * P], identity[:])
         ts_cols = keep.tile([P, PACK], F32, name="ts_cols")
         nc.scalar.copy(ts_cols[:], ts_turned[:, 0:L:P])
-        ts_spread = bank_tile(5)
-        ts_first = bank_tile(2)
-        for spread, blocks in ((ts_spread, PACK), (ts_first, 2)):
-            for j in range(blocks):
-                nc.tensor.transpose(
-                    spread[:, j * P : (j + 1) * P], ts_cols[:, j : j + 1].to_broadcast([P, P]), identity[:]
-                )
+        ts_spread = [bank_tile(2), bank_tile(5)]
+        for j in range(PACK):
+            c = (j % 2) * P
+            nc.tensor.transpose(
+                ts_spread[j // 2][:, c : c + P], ts_cols[:, j : j + 1].to_broadcast([P, P]), identity[:]
+            )
         scale = keep.tile([P, PACK, HALF], F32, name="scale")
         for s in range(PACK):
-            nc.scalar.activation(scale[:, s, :], ts_first[:, first], COPY, scale=us_cols[:, s : s + 1])
+            nc.scalar.activation(scale[:, s, :], ts_spread[0][:, first], COPY, scale=us_cols[:, s : s + 1])
         x_planes = keep.tile([P, PACK * L], BF16, name="x_planes")
         for t in range(PACK):
             nc.vector.tensor_copy(x_planes[:, t * L : (t + 1) * L], u_planes[t][:].indirect(user_list[:]))
@@ -152,19 +151,19 @@ def tile_attend_gmf_hub_vu_kernel(tc, uT, vT, y, us, ts, offs, uoffs, out_0, out
             )
             turn_planes(x_planes[:, cols], (x_lo_values, late_values[:, 0 : 2 * L])[n], bank_tile(6 + n))
 
+        scale_packed = [keep.tile([P, HALF, PACK], F32, name="u_plane%d" % (3 - n), align_bytes=64) for n in range(2)]
+        nc.scalar.copy(scale_packed[0][:], scale[:].rearrange("p s i -> p i s"))
+        nc.vector.tensor_tensor(
+            scale_packed[1][:],
+            ts_spread[1][:, first].unsqueeze(2).to_broadcast([P, HALF, PACK]),
+            us_cols[:].unsqueeze(1).to_broadcast([P, HALF, PACK]),
+            ALU.mult,
+        )
+
         w_packed = w_d[0][:].rearrange("p (i t) -> p i t", t=PACK)
         w_planes = keep.tile([P, 2 * L], BF16, name="w_planes")
         for t in range(2):
             nc.vector.tensor_copy(w_planes[:, t * L : (t + 1) * L], v_planes[t][:].indirect(item_list[:]))
-        scale_packed = [keep.tile([P, HALF, PACK], F32, name=("u_plane3", "v_plane0")[n], align_bytes=64) for n in range(2)]
-        for n, cols in enumerate(halves):
-            nc.vector.tensor_tensor(
-                scale_packed[n][:],
-                ts_spread[:, cols].unsqueeze(2).to_broadcast([P, HALF, PACK]),
-                us_cols[:].unsqueeze(1).to_broadcast([P, HALF, PACK]),
-                ALU.mult,
-            )
-
         nc.scalar.copy(w_packed[:, :, 0:2], w_planes[:].rearrange("p (t i) -> p i t", t=2))
         turn_planes(w_planes[:], late_values[:, 2 * L : 4 * L], bank_tile(3))
         nc.vector.tensor_copy(w_packed[:, :, 2], v_planes[2][:].indirect(item_list[:]))

@@ -94,8 +94,9 @@ def tile_attend_gmf_hub_vu_kernel(tc, uT, vT, y, us, ts, offs, uoffs, out_0, out
 
         x_values = packed_values("x", L + HALF)
         x_d_values = x_values[:, 0 : PACK * L]
-        x_lo_values = x_values[:, PACK * L : PACK * (L + HALF)]
-        late_values = packed_values("late")
+        x_hi_values = x_values[:, PACK * L : PACK * (L + HALF)]
+        x_lo_values = packed_values("x_lo", HALF)
+        w_lo_values = packed_values("w_lo", HALF)
         w_d = operand("w_d", packed_values("w_d"))
         h_r = operand("h_r", packed_values("h_r"))
         w_hi_values = packed_values("w_hi", HALF)
@@ -149,7 +150,7 @@ def tile_attend_gmf_hub_vu_kernel(tc, uT, vT, y, us, ts, offs, uoffs, out_0, out
                 x_d_values.rearrange("p (s m t) -> p s m t", s=PACK, t=PACK)[:, :, :, 2 * n : 2 * n + 2],
                 x_planes[:, cols].rearrange("p (t m s) -> p s m t", t=2, s=PACK),
             )
-            turn_planes(x_planes[:, cols], (x_lo_values, late_values[:, 0 : 2 * L])[n], bank_tile(6 + n))
+            turn_planes(x_planes[:, cols], (x_lo_values[:], x_hi_values)[n], bank_tile(6 + n))
 
         scale_packed = [keep.tile([P, HALF, PACK], F32, name="u_plane%d" % (3 - n), align_bytes=64) for n in range(2)]
         nc.scalar.copy(scale_packed[0][:], scale[:].rearrange("p s i -> p i s"))
@@ -165,16 +166,18 @@ def tile_attend_gmf_hub_vu_kernel(tc, uT, vT, y, us, ts, offs, uoffs, out_0, out
         for t in range(2):
             nc.vector.tensor_copy(w_planes[:, t * L : (t + 1) * L], v_planes[t][:].indirect(item_list[:]))
         nc.scalar.copy(w_packed[:, :, 0:2], w_planes[:].rearrange("p (t i) -> p i t", t=2))
-        turn_planes(w_planes[:], late_values[:, 2 * L : 4 * L], bank_tile(3))
+        turn_planes(w_planes[:], w_lo_values[:], bank_tile(3))
         nc.vector.tensor_copy(w_packed[:, :, 2], v_planes[2][:].indirect(item_list[:]))
         x_d = operand("x", x_values, "v_plane1", columns=L + HALF)
-        quantize(x_d, E4M3, L, L + HALF)
         quantize(x_d, E4M3, 0, L)
+        quantize(x_d, E4M3, L, L + HALF)
+        x_lo = operand("x_lo", x_lo_values, "v_plane0", columns=HALF)
+        quantize(x_lo, E4M3, 0, HALF)
         for cols in halves:
             nc.vector.tensor_copy(w_packed[:, cols, 3], v_planes[3][:].indirect(places(item_list, cols)))
             quantize(w_d, E4M3, cols.start, cols.stop)
-        late = operand("late", late_values, "v_plane3")
-        quantize(late, E4M3, 0, L)
+        w_lo = operand("w_lo", w_lo_values, "v_plane3", columns=HALF)
+        quantize(w_lo, E4M3, 0, HALF)
 
         quarters = [slice(q * P, (q + 1) * P) for q in range(PACK)]
         residual = keep.tile([P, PACK, L], F32, name="residual")
@@ -234,7 +237,7 @@ def tile_attend_gmf_hub_vu_kernel(tc, uT, vT, y, us, ts, offs, uoffs, out_0, out
             if cols.stop == L:
                 nc.sync.dma_start(out_rows[side][k], window[:])
 
-        x_r = ((x_d, 4), (x_d, 5), (late, 0), (late, 1))
+        x_r = ((x_lo, 0), (x_lo, 1), (x_d, 4), (x_d, 5))
         pairs = turn_pairs(w_d[0], 1, bank_tile(3))
         nc.scalar.copy(
             w_hi_values[:].rearrange("m (e p s) -> m e p s", e=2, s=PACK),
@@ -278,8 +281,8 @@ def tile_attend_gmf_hub_vu_kernel(tc, uT, vT, y, us, ts, offs, uoffs, out_0, out
         for u in range(2):
             pairs = turn_pairs(h_r[0], u, bank_tile((2, 3)[u]))
             nc.scalar.copy(turned[:, :, u, :, :], pairs.rearrange("m (s p e) -> m p e s", s=PACK, e=2))
-        h_i = operand("h_i", h_i_values, "item_sums2_512")
+        h_i = operand("h_i", h_i_values, "item_sums1_512")
         quantize(h_i, E5M2, 0, L)
         scatter("item", 3, item3, whole)
         for k in range(PACK):
-            scatter("user", k, sums_of("user", k, 4 + k, (late, w_hi)[k // 2], (2, 3, 0, 1)[k], h_i, whole), whole)
+            scatter("user", k, sums_of("user", k, 4 + k, (w_lo, w_hi)[k // 2], k % 2, h_i, whole), whole)

@@ -18,7 +18,7 @@ PACK = 4
 L = 512
 T = 2048
 HALF = L // 2
-WINDOWS = 3
+USER_WINDOWS = 2
 
 FLOPS = 3 * 2 * L * L * L
 
@@ -39,8 +39,8 @@ def tile_attend_gmf_hub_vu_kernel(tc, uT, vT, y, us, ts, offs, uoffs, out_0, out
         ts_table = keep.tile([P, T], F32, name="ts_table")
         us_cols = keep.tile([P, PACK], F32, name="us_cols", align_bytes=64)
         y_rows = keep.tile([P, PACK, L], F32, name="y_rows", align_bytes=64)
-        item_windows = [keep.tile([P, T], F32, name="item_window%d" % k) for k in range(WINDOWS)]
-        user_windows = [keep.tile([P, T], F32, name="user_window%d" % k) for k in range(WINDOWS)]
+        item_windows = [keep.tile([P, T], F32, name="item_window%d" % k) for k in range(PACK)]
+        user_windows = [keep.tile([P, T], F32, name="user_window%d" % k) for k in range(USER_WINDOWS)]
         identity = keep.tile([P, P], F32, name="identity")
 
         def packed_values(name, columns=L):
@@ -92,12 +92,10 @@ def tile_attend_gmf_hub_vu_kernel(tc, uT, vT, y, us, ts, offs, uoffs, out_0, out
         def places(offsets, cols):
             return offsets[:, cols.start // 16 : cols.stop // 16]
 
-        x_values = packed_values("x", L + HALF)
-        x_d_values = x_values[:, 0 : PACK * L]
-        x_hi_values = x_values[:, PACK * L : PACK * (L + HALF)]
-        x_lo_values = packed_values("x_lo", HALF)
+        x_d_values = packed_values("x_d")
+        x_r_values = packed_values("x_r")
         w_lo_values = packed_values("w_lo", HALF)
-        w_d = operand("w_d", packed_values("w_d"))
+        w_values = packed_values("w_d")
         h_r = operand("h_r", packed_values("h_r"))
         w_hi_values = packed_values("w_hi", HALF)
         h_i_values = packed_values("h_i")
@@ -138,22 +136,25 @@ def tile_attend_gmf_hub_vu_kernel(tc, uT, vT, y, us, ts, offs, uoffs, out_0, out
             nc.tensor.transpose(
                 ts_spread[j // 2][:, c : c + P], ts_cols[:, j : j + 1].to_broadcast([P, P]), identity[:]
             )
-        scale = keep.tile([P, PACK, HALF], F32, name="scale")
-        for s in range(PACK):
-            nc.scalar.activation(scale[:, s, :], ts_spread[0][:, first], COPY, scale=us_cols[:, s : s + 1])
+        quarters = [slice(q * P, (q + 1) * P) for q in range(PACK)]
+        scale = [keep.tile([P, PACK, P], F32, name="scale%d" % q, align_bytes=64) for q in range(2)]
+        for q in range(2):
+            for s in range(PACK):
+                nc.scalar.activation(scale[q][:, s, :], ts_spread[0][:, quarters[q]], COPY, scale=us_cols[:, s : s + 1])
         x_planes = keep.tile([P, PACK * L], BF16, name="x_planes")
         for t in range(PACK):
             nc.vector.tensor_copy(x_planes[:, t * L : (t + 1) * L], u_planes[t][:].indirect(user_list[:]))
         for n in range(2):
             cols = slice(2 * n * L, 2 * (n + 1) * L)
             nc.scalar.copy(
-                x_d_values.rearrange("p (s m t) -> p s m t", s=PACK, t=PACK)[:, :, :, 2 * n : 2 * n + 2],
+                x_d_values[:].rearrange("p (s m t) -> p s m t", s=PACK, t=PACK)[:, :, :, 2 * n : 2 * n + 2],
                 x_planes[:, cols].rearrange("p (t m s) -> p s m t", t=2, s=PACK),
             )
-            turn_planes(x_planes[:, cols], (x_lo_values[:], x_hi_values)[n], bank_tile(6 + n))
+            turn_planes(x_planes[:, cols], x_r_values[:, cols], bank_tile(6 + n))
 
         scale_packed = [keep.tile([P, HALF, PACK], F32, name="u_plane%d" % (3 - n), align_bytes=64) for n in range(2)]
-        nc.scalar.copy(scale_packed[0][:], scale[:].rearrange("p s i -> p i s"))
+        for q in range(2):
+            nc.scalar.copy(scale_packed[0][:, quarters[q], :], scale[q][:].rearrange("p s i -> p i s"))
         nc.vector.tensor_tensor(
             scale_packed[1][:],
             ts_spread[1][:, first].unsqueeze(2).to_broadcast([P, HALF, PACK]),
@@ -161,61 +162,67 @@ def tile_attend_gmf_hub_vu_kernel(tc, uT, vT, y, us, ts, offs, uoffs, out_0, out
             ALU.mult,
         )
 
-        w_packed = w_d[0][:].rearrange("p (i t) -> p i t", t=PACK)
+        w_packed = w_values[:].rearrange("p (i t) -> p i t", t=PACK)
         w_planes = keep.tile([P, 2 * L], BF16, name="w_planes")
         for t in range(2):
             nc.vector.tensor_copy(w_planes[:, t * L : (t + 1) * L], v_planes[t][:].indirect(item_list[:]))
         nc.scalar.copy(w_packed[:, :, 0:2], w_planes[:].rearrange("p (t i) -> p i t", t=2))
         turn_planes(w_planes[:], w_lo_values[:], bank_tile(3))
         nc.vector.tensor_copy(w_packed[:, :, 2], v_planes[2][:].indirect(item_list[:]))
-        x_d = operand("x", x_values, "v_plane1", columns=L + HALF)
+        x_d = operand("x_d", x_d_values, "v_plane0")
         quantize(x_d, E4M3, 0, L)
-        quantize(x_d, E4M3, L, L + HALF)
-        x_lo = operand("x_lo", x_lo_values, "v_plane0", columns=HALF)
-        quantize(x_lo, E4M3, 0, HALF)
-        for cols in halves:
-            nc.vector.tensor_copy(w_packed[:, cols, 3], v_planes[3][:].indirect(places(item_list, cols)))
-            quantize(w_d, E4M3, cols.start, cols.stop)
-        w_lo = operand("w_lo", w_lo_values, "v_plane3", columns=HALF)
+        x_r = operand("x_r", x_r_values, "v_plane1")
+        quantize(x_r, E4M3, 0, L)
+        w_lo = operand("w_lo", w_lo_values, "v_plane2", columns=HALF)
         quantize(w_lo, E4M3, 0, HALF)
 
-        quarters = [slice(q * P, (q + 1) * P) for q in range(PACK)]
-        residual = keep.tile([P, PACK, L], F32, name="residual")
-        scaled = keep.tile([P, PACK, HALF], F32, name="scaled")
+        def gather_last(cols):
+            nc.vector.tensor_copy(w_packed[:, cols, 3], v_planes[3][:].indirect(places(item_list, cols)))
+
+        gather_last(first)
+        w_first = operand("w_first", w_values[:, 0 : PACK * HALF], columns=HALF)
+        for q in (1, 0):
+            quantize(w_first, E4M3, q * P, (q + 1) * P)
+        gather_last(slice(HALF - 32, L))
+
+        scaled = [keep.tile([P, PACK, P], F32, name="scaled%d" % q, align_bytes=64) for q in range(2)]
+        residual = [keep.tile([P, PACK, P], F32, name="residual%d" % q, align_bytes=64) for q in range(PACK)]
         clipped = [keep.tile([P, P, PACK], F32, name="clipped%d" % q, align_bytes=64) for q in range(PACK)]
         h_packed = h_r[0][:].rearrange("p (i s) -> p i s", s=PACK)
 
-        def clip(cols):
-            nc.vector.tensor_scalar(
-                clipped[cols.start // P][:], residual[:, :, cols].rearrange("p s i -> p i s"), -1.0, 1.0, ALU.max, ALU.min
+        def clip(q, engine):
+            engine.tensor_scalar(
+                clipped[q][:], residual[q][:].rearrange("p s i -> p i s"), 1.0, -1.0, ALU.min, ALU.max
             )
 
-        def weigh(cols, engine=nc.vector):
-            factors = scale_packed[cols.start // HALF][:, cols.start % HALF : cols.start % HALF + P, :]
-            engine.tensor_tensor(h_packed[:, cols, :], clipped[cols.start // P][:], factors, ALU.mult)
+        def weigh(q, engine):
+            factors = scale_packed[q // 2][:, quarters[q % 2], :]
+            engine.tensor_tensor(h_packed[:, quarters[q], :], clipped[q][:], factors, ALU.mult)
 
-        for q in range(2):
+        for q in (1, 0):
             acc = bank_tile(q)
             for s in range(PACK):
-                product(acc[:, s * P : (s + 1) * P], x_d, s, w_d, E4M3, quarters[q])
-            nc.vector.tensor_tensor(
-                scaled[:, :, quarters[q]], acc[:].rearrange("p (s i) -> p s i", s=PACK), scale[:, :, quarters[q]], ALU.mult
-            )
-        back = [bank_tile(4), bank_tile(5)]
-        for j in (2, 3):
-            acc = bank_tile(j)
-            product(acc[:], w_d, j, x_d, E4M3, slice(0, L))
-            item_scaled = keep.tile([P, L], F32, name="item_scaled%d" % j)
-            nc.scalar.activation(item_scaled[:], acc[:], COPY, scale=ts_cols[:, j : j + 1])
+                product(acc[:, quarters[s]], x_d, s, w_first, E4M3, quarters[q])
+            nc.vector.tensor_tensor(scaled[q][:], acc[:].rearrange("p (s i) -> p s i", s=PACK), scale[q][:], ALU.mult)
+        w_second = operand("w_second", w_values[:, PACK * HALF : PACK * L], "scale1", columns=HALF)
+        quantize(w_second, E4M3, 0, HALF)
+        back = {}
+        for q in (2, 3):
+            acc = bank_tile(q)
+            product(acc[:], w_second, q - 2, x_d, E4M3, slice(0, L))
+            item_scaled = keep.tile([P, L], F32, name="item_scaled%d" % q)
+            nc.scalar.activation(item_scaled[:], acc[:], COPY, scale=ts_cols[:, q : q + 1])
+            back[q] = bank_tile(q + 2)
             for s in range(PACK):
-                c = (s % 2) * HALF + (j - 2) * P
-                nc.tensor.transpose(back[s // 2][:, c : c + P], item_scaled[:, s * P : (s + 1) * P], identity[:])
-        for cols in quarters[:2]:
-            nc.vector.tensor_tensor(residual[:, :, cols], scaled[:, :, cols], y_rows[:, :, cols], ALU.subtract)
-        for cols in quarters[:2]:
-            clip(cols)
-        weigh(quarters[0])
-        weigh(quarters[1], nc.gpsimd)
+                nc.tensor.transpose(back[q][:, quarters[s]], item_scaled[:, quarters[s]], identity[:])
+        for q in (1, 0):
+            nc.vector.tensor_tensor(residual[q][:], scaled[q][:], y_rows[:, :, quarters[q]], ALU.subtract)
+        for q in (1, 0):
+            clip(q, nc.vector)
+        for q in (1, 0):
+            weigh(q, nc.vector)
+        for q in (1, 0):
+            quantize(h_r, E5M2, q * P, (q + 1) * P)
 
         out_rows = {
             "item": out_0.rearrange("(p t) c -> t p c", t=PACK),
@@ -223,66 +230,63 @@ def tile_attend_gmf_hub_vu_kernel(tc, uT, vT, y, us, ts, offs, uoffs, out_0, out
         }
         windows = {"item": item_windows, "user": user_windows}
         lists = {"item": item_list, "user": user_list}
+        whole = slice(0, L)
 
-        def sums_of(side, k, bank, stationary, block, moving, cols):
+        def gradient(bank, stationary, block, moving):
             acc = bank_tile(bank)
-            product(acc[:], stationary, block, moving, E5M2, slice(0, L))
-            sums = keep.tile([P, cols.stop - cols.start], F32, name="%s_sums%d_%d" % (side, k, cols.stop), align_bytes=64)
+            product(acc[:], stationary, block, moving, E5M2, whole)
+            return acc
+
+        def sums_of(acc, cols, tag):
+            sums = keep.tile([P, cols.stop - cols.start], F32, name=tag, align_bytes=64)
             nc.scalar.copy(sums[:], acc[:, cols])
             return sums[:]
 
         def scatter(side, k, sums, cols):
-            window = windows[side][k % WINDOWS]
+            window = windows[side][k % len(windows[side])]
             nc.vector.tensor_copy(window[:].indirect(places(lists[side], cols)), sums)
             if cols.stop == L:
                 nc.sync.dma_start(out_rows[side][k], window[:])
 
-        x_r = ((x_lo, 0), (x_lo, 1), (x_d, 4), (x_d, 5))
-        pairs = turn_pairs(w_d[0], 1, bank_tile(3))
+        early = [gradient((6, 7, 1)[k], x_r, k, h_r) for k in range(3)]
+
+        for q in (2, 3):
+            for s in range(PACK):
+                nc.vector.scalar_tensor_tensor(
+                    residual[q][:, s, :],
+                    back[q][:, quarters[s]],
+                    us_cols[:, s : s + 1],
+                    y_rows[:, s, quarters[q]],
+                    ALU.mult,
+                    ALU.subtract,
+                )
+            clip(q, nc.gpsimd)
+            weigh(q, nc.gpsimd)
+        for k in range(2):
+            scatter("item", k, sums_of(early[k], first, "early_sums%d" % k), first)
+        pairs = turn_pairs(w_values, 1, bank_tile(6))
         nc.scalar.copy(
             w_hi_values[:].rearrange("m (e p s) -> m e p s", e=2, s=PACK),
             pairs.rearrange("m (s p e) -> m e p s", s=PACK, e=2),
         )
-
-        for s in range(PACK):
-            c = (s % 2) * HALF
-            nc.vector.scalar_tensor_tensor(
-                residual[:, s, second],
-                back[s // 2][:, c : c + HALF],
-                us_cols[:, s : s + 1],
-                y_rows[:, s, second],
-                ALU.mult,
-                ALU.subtract,
-            )
-        quantize(h_r, E5M2, 0, HALF)
-        early = [bank_tile(b) for b in (6, 7, 0)]
-        for k in range(3):
-            product(early[k][:], *x_r[k], h_r, E5M2, slice(0, L))
-        w_hi = operand("w_hi", w_hi_values, columns=HALF, scales_tag="us_cols")
+        w_hi = operand("w_hi", w_hi_values, columns=HALF)
         quantize(w_hi, E4M3, 0, HALF)
-        for cols in quarters[2:]:
-            clip(cols)
-            weigh(cols, nc.gpsimd)
-        early_sums = keep.tile([P, L], F32, name="early_sums", align_bytes=64)
-        for k in range(2):
-            nc.scalar.copy(early_sums[:, halves[k]], early[k][:, first])
-            scatter("item", k, early_sums[:, halves[k]], first)
         quantize(h_r, E5M2, HALF, L)
-        held_sums = keep.tile([P, HALF], F32, name="clipped3", align_bytes=64)
-        nc.scalar.copy(held_sums[:], early[2][:, first])
-        scatter("item", 2, held_sums[:], first)
+        scatter("item", 2, sums_of(early[2], first, "clipped3"), first)
 
-        whole = slice(0, L)
         for k in range(3):
-            scatter("item", k, sums_of("item", k, 1 + k, *x_r[k], h_r, second), second)
-        item3 = sums_of("item", 3, 6, *x_r[3], h_r, whole)
+            scatter("item", k, sums_of(gradient((0, 2, 3)[k], x_r, k, h_r), second, "late_sums%d" % k), second)
 
         turned = h_i_values[:].rearrange("m (p u e s) -> m p u e s", u=2, e=2, s=PACK)
         for u in range(2):
-            pairs = turn_pairs(h_r[0], u, bank_tile((2, 3)[u]))
+            pairs = turn_pairs(h_r[0], u, bank_tile((4, 5)[u]))
             nc.scalar.copy(turned[:, :, u, :, :], pairs.rearrange("m (s p e) -> m p e s", s=PACK, e=2))
-        h_i = operand("h_i", h_i_values, "item_sums1_512")
+        h_i = operand("h_i", h_i_values)
         quantize(h_i, E5M2, 0, L)
-        scatter("item", 3, item3, whole)
+        last_item = gradient(5, x_r, 3, h_r)
+        scatter("item", 3, sums_of(last_item, first, "last_sums"), first)
         for k in range(PACK):
-            scatter("user", k, sums_of("user", k, 4 + k, (w_lo, w_hi)[k // 2], k % 2, h_i, whole), whole)
+            acc = gradient((6, 7, 0, 1)[k], (w_lo, w_hi)[k // 2], k % 2, h_i)
+            scatter("user", k, sums_of(acc, whole, "user_sums%d" % k), whole)
+            if k == 1:
+                scatter("item", 3, sums_of(last_item, second, "user_sums0"), second)

@@ -283,10 +283,9 @@ def tile_attend_gmf_hub_vu_kernel(tc, uT, vT, y, us, ts, offs, uoffs, out_0, out
             nc.scalar.copy(turned[:, :, u, :, :], pairs.rearrange("m (s p e) -> m p e s", s=PACK, e=2))
         h_i = operand("h_i", h_i_values)
         quantize(h_i, E5M2, 0, L)
-        last_item = gradient(5, x_r, 3, h_r)
-        scatter("item", 3, sums_of(last_item, first, "last_sums"), first)
+        user_windows.append(keep.tile([P, T], F32, name="h_i_values", align_bytes=64))
+        nc.gpsimd.memset(user_windows[2][:], 0.0)
+        scatter("item", 3, sums_of(gradient(5, x_r, 3, h_r), whole, "last_sums"), whole)
         for k in range(PACK):
             acc = gradient((6, 7, 0, 1)[k], (w_lo, w_hi)[k // 2], k % 2, h_i)
             scatter("user", k, sums_of(acc, whole, "user_sums%d" % k), whole)
-            if k == 1:
-                scatter("item", 3, sums_of(last_item, second, "user_sums0"), second)

@@ -108,8 +108,9 @@ def tile_attend_gmf_hub_vu_kernel(tc, uT, vT, y, us, ts, offs, uoffs, out_0, out
         nc.sync.dma_start(user_list[:], uoffs)
         nc.sync.dma_start(item_list[:], offs)
         nc.scalar.dma_start(us_cols[:], us.rearrange("b (p s) o -> p (b s o)", s=PACK))
+        nc.sync.dma_start(u_planes[1][:], u_rows[1])
         nc.sync.dma_start(ts_table[0:1, :], ts[0:1, :])
-        for t in range(1, PACK):
+        for t in range(2, PACK):
             nc.sync.dma_start(u_planes[t][:], u_rows[t])
         for t in range(PACK):
             nc.sync.dma_start(v_planes[t][:], v_rows[t])
@@ -137,10 +138,6 @@ def tile_attend_gmf_hub_vu_kernel(tc, uT, vT, y, us, ts, offs, uoffs, out_0, out
                 ts_spread[j // 2][:, c : c + P], ts_cols[:, j : j + 1].to_broadcast([P, P]), identity[:]
             )
         quarters = [slice(q * P, (q + 1) * P) for q in range(PACK)]
-        scale = [keep.tile([P, PACK, P], F32, name="scale%d" % q, align_bytes=64) for q in range(2)]
-        for q in range(2):
-            for s in range(PACK):
-                nc.scalar.activation(scale[q][:, s, :], ts_spread[0][:, quarters[q]], COPY, scale=us_cols[:, s : s + 1])
         x_planes = keep.tile([P, PACK * L], BF16, name="x_planes")
         for t in range(PACK):
             nc.vector.tensor_copy(x_planes[:, t * L : (t + 1) * L], u_planes[t][:].indirect(user_list[:]))
@@ -152,15 +149,11 @@ def tile_attend_gmf_hub_vu_kernel(tc, uT, vT, y, us, ts, offs, uoffs, out_0, out
             )
             turn_planes(x_planes[:, cols], x_r_values[:, cols], bank_tile(6 + n))
 
-        scale_packed = [keep.tile([P, HALF, PACK], F32, name="u_plane%d" % (3 - n), align_bytes=64) for n in range(2)]
-        for q in range(2):
-            nc.scalar.copy(scale_packed[0][:, quarters[q], :], scale[q][:].rearrange("p s i -> p i s"))
-        nc.vector.tensor_tensor(
-            scale_packed[1][:],
-            ts_spread[1][:, first].unsqueeze(2).to_broadcast([P, HALF, PACK]),
-            us_cols[:].unsqueeze(1).to_broadcast([P, HALF, PACK]),
-            ALU.mult,
-        )
+        scale = keep.tile([P, PACK, HALF], F32, name="u_plane3", align_bytes=64)
+        for s in range(PACK):
+            nc.scalar.activation(scale[:, s, :], ts_spread[0][:, first], COPY, scale=us_cols[:, s : s + 1])
+        scale_packed = [keep.tile([P, HALF, PACK], F32, name="scale_packed%d" % n, align_bytes=64) for n in range(2)]
+        nc.scalar.copy(scale_packed[0][:], scale[:].rearrange("p s i -> p i s"))
 
         w_packed = w_values[:].rearrange("p (i t) -> p i t", t=PACK)
         w_planes = keep.tile([P, 2 * L], BF16, name="w_planes")
@@ -173,8 +166,11 @@ def tile_attend_gmf_hub_vu_kernel(tc, uT, vT, y, us, ts, offs, uoffs, out_0, out
         quantize(x_d, E4M3, 0, L)
         x_r = operand("x_r", x_r_values, "v_plane1")
         quantize(x_r, E4M3, 0, L)
-        w_lo = operand("w_lo", w_lo_values, "v_plane2", columns=HALF)
-        quantize(w_lo, E4M3, 0, HALF)
+
+        late_scale = keep.tile([P, PACK, HALF], F32, name="v_plane2", align_bytes=64)
+        for s in range(PACK):
+            nc.scalar.activation(late_scale[:, s, :], ts_spread[1][:, first], COPY, scale=us_cols[:, s : s + 1])
+        nc.scalar.copy(scale_packed[1][:], late_scale[:].rearrange("p s i -> p i s"))
 
         def gather_last(cols):
             nc.vector.tensor_copy(w_packed[:, cols, 3], v_planes[3][:].indirect(places(item_list, cols)))
@@ -183,7 +179,11 @@ def tile_attend_gmf_hub_vu_kernel(tc, uT, vT, y, us, ts, offs, uoffs, out_0, out
         w_first = operand("w_first", w_values[:, 0 : PACK * HALF], columns=HALF)
         for q in (1, 0):
             quantize(w_first, E4M3, q * P, (q + 1) * P)
-        gather_last(slice(HALF - 32, L))
+        gather_last(second)
+        w_second = operand("w_second", w_values[:, PACK * HALF : PACK * L], columns=HALF)
+        quantize(w_second, E4M3, 0, HALF)
+        w_lo = operand("w_lo", w_lo_values, "v_plane3", columns=HALF)
+        quantize(w_lo, E4M3, 0, HALF)
 
         scaled = [keep.tile([P, PACK, P], F32, name="scaled%d" % q, align_bytes=64) for q in range(2)]
         residual = [keep.tile([P, PACK, P], F32, name="residual%d" % q, align_bytes=64) for q in range(PACK)]
@@ -203,9 +203,7 @@ def tile_attend_gmf_hub_vu_kernel(tc, uT, vT, y, us, ts, offs, uoffs, out_0, out
             acc = bank_tile(q)
             for s in range(PACK):
                 product(acc[:, quarters[s]], x_d, s, w_first, E4M3, quarters[q])
-            nc.vector.tensor_tensor(scaled[q][:], acc[:].rearrange("p (s i) -> p s i", s=PACK), scale[q][:], ALU.mult)
-        w_second = operand("w_second", w_values[:, PACK * HALF : PACK * L], "scale1", columns=HALF)
-        quantize(w_second, E4M3, 0, HALF)
+            nc.vector.tensor_tensor(scaled[q][:], acc[:].rearrange("p (s i) -> p s i", s=PACK), scale[:, :, quarters[q]], ALU.mult)
         back = {}
         for q in (2, 3):
             acc = bank_tile(q)
@@ -245,7 +243,10 @@ def tile_attend_gmf_hub_vu_kernel(tc, uT, vT, y, us, ts, offs, uoffs, out_0, out
         def scatter(side, k, sums, cols):
             window = windows[side][k % len(windows[side])]
             nc.vector.tensor_copy(window[:].indirect(places(lists[side], cols)), sums)
-            if cols.stop == L:
+            if side == "user" and k == PACK - 1:
+                nc.sync.dma_start(out_rows[side][k][:, 0 : T // 2], window[:, 0 : T // 2])
+                nc.scalar.dma_start(out_rows[side][k][:, T // 2 : T], window[:, T // 2 : T])
+            elif cols.stop == L:
                 nc.sync.dma_start(out_rows[side][k], window[:])
 
         early = [gradient((6, 7, 1)[k], x_r, k, h_r) for k in range(3)]

@@ -200,10 +200,17 @@ def tile_attend_gmf_hub_vu_kernel(tc, uT, vT, y, us, ts, offs, uoffs, out_0, out
             engine.tensor_tensor(h_packed[:, quarters[q], :], clipped[q][:], factors, ALU.mult)
 
         for q in (1, 0):
-            acc = bank_tile(q)
-            for s in range(PACK):
-                product(acc[:, quarters[s]], x_d, s, w_first, E4M3, quarters[q])
-            nc.vector.tensor_tensor(scaled[q][:], acc[:].rearrange("p (s i) -> p s i", s=PACK), scale[:, :, quarters[q]], ALU.mult)
+            for n in range(2):
+                acc = bank_tile((6 + q, q)[n])
+                for e in range(2):
+                    product(acc[:, quarters[e]], x_d, 2 * n + e, w_first, E4M3, quarters[q])
+                rows = slice(2 * n, 2 * n + 2)
+                nc.vector.tensor_tensor(
+                    scaled[q][:, rows, :],
+                    acc[:, first].rearrange("p (s i) -> p s i", s=2),
+                    scale[:, rows, quarters[q]],
+                    ALU.mult,
+                )
         back = {}
         for q in (2, 3):
             acc = bank_tile(q)

@@ -18,7 +18,9 @@ PACK = 4
 L = 512
 T = 2048
 HALF = L // 2
-USER_WINDOWS = 2
+BAND = 16
+EARLY_PLANES = 3
+HEAD_USER_WINDOWS = 2
 
 FLOPS = 3 * 2 * L * L * L
 
@@ -32,23 +34,23 @@ def tile_attend_gmf_hub_vu_kernel(tc, uT, vT, y, us, ts, offs, uoffs, out_0, out
         def bank_tile(b):
             return psum.tile([P, L], F32, name="bank%d" % b)
 
-        user_list = keep.tile([P, L // 16], U16, name="user_list")
-        item_list = keep.tile([P, L // 16], U16, name="item_list")
+        user_list = keep.tile([P, L // BAND], U16, name="user_list")
+        item_list = keep.tile([P, L // BAND], U16, name="item_list")
         u_planes = [keep.tile([P, T], F32, name="u_plane%d" % t, align_bytes=64) for t in range(PACK)]
         v_planes = [keep.tile([P, T], F32, name="v_plane%d" % t, align_bytes=64) for t in range(PACK)]
         ts_table = keep.tile([P, T], F32, name="ts_table")
         us_cols = keep.tile([P, PACK], F32, name="us_cols", align_bytes=64)
         y_rows = keep.tile([P, PACK, L], F32, name="y_rows", align_bytes=64)
         item_windows = [keep.tile([P, T], F32, name="item_window%d" % k) for k in range(PACK)]
-        user_windows = [keep.tile([P, T], F32, name="user_window%d" % k) for k in range(USER_WINDOWS)]
+        user_windows = [keep.tile([P, T], F32, name="user_window%d" % k) for k in range(HEAD_USER_WINDOWS)]
         identity = keep.tile([P, P], F32, name="identity")
 
         def packed_values(name, columns=L):
             return keep.tile([P, columns * PACK], BF16, name=name + "_values", align_bytes=64)
 
-        def operand(name, values, codes_tag=None, columns=L, scales_tag=None):
-            codes = keep.tile([P, columns], U32, name=codes_tag or name + "_codes", align_bytes=64)
-            scales = keep.tile([P, columns], U8, name=scales_tag or name + "_scales", align_bytes=64)
+        def operand(name, values, codes_buffer=None, columns=L):
+            codes = keep.tile([P, columns], U32, name=codes_buffer or name + "_codes", align_bytes=64)
+            scales = keep.tile([P, columns], U8, name=name + "_scales", align_bytes=64)
             return values, codes, scales
 
         def quantize(op, fmt, lo, hi):
@@ -57,14 +59,14 @@ def tile_attend_gmf_hub_vu_kernel(tc, uT, vT, y, us, ts, offs, uoffs, out_0, out
                 out=codes[:, lo:hi].bitcast(fmt), scales=scales[:, lo:hi], in_=values[:, PACK * lo : PACK * hi]
             )
 
-        def product(acc, stationary, k, moving, moving_fmt, n_cols):
-            cols = slice(k * P, (k + 1) * P)
+        def product(acc, stationary, block, moving, moving_fmt, moving_cols):
+            cols = slice(block * P, (block + 1) * P)
             nc.tensor.matmul_mx(
                 out=acc,
                 lhsT=stationary[1][:, cols].bitcast(E4M3),
                 lhsT_scale=stationary[2][:, cols],
-                rhs=moving[1][:, n_cols].bitcast(moving_fmt),
-                rhs_scale=moving[2][:, n_cols],
+                rhs=moving[1][:, moving_cols].bitcast(moving_fmt),
+                rhs_scale=moving[2][:, moving_cols],
                 start=True,
                 stop=True,
             )
@@ -86,11 +88,11 @@ def tile_attend_gmf_hub_vu_kernel(tc, uT, vT, y, us, ts, offs, uoffs, out_0, out
                 nc.tensor.transpose(bank[:, s * P : (s + 1) * P], words[:, s, :, u], identity[:])
             return bank[:].bitcast(BF16)
 
-        halves = (slice(0, HALF), slice(HALF, L))
-        first, second = halves
+        first, second, whole = slice(0, HALF), slice(HALF, L), slice(0, L)
+        quarters = [slice(q * P, (q + 1) * P) for q in range(PACK)]
 
         def places(offsets, cols):
-            return offsets[:, cols.start // 16 : cols.stop // 16]
+            return offsets[:, cols.start // BAND : cols.stop // BAND]
 
         x_d_values = packed_values("x_d")
         x_r_values = packed_values("x_r")
@@ -127,17 +129,16 @@ def tile_attend_gmf_hub_vu_kernel(tc, uT, vT, y, us, ts, offs, uoffs, out_0, out
         ts_row = keep.tile([P, L], F32, name="ts_row")
         nc.vector.tensor_copy(ts_row[:], ts_table[:].indirect(item_list[:]))
         ts_turned = bank_tile(4)
-        for j in range(PACK):
-            nc.tensor.transpose(ts_turned[:, j * P : (j + 1) * P], ts_row[:, j * P : (j + 1) * P], identity[:])
+        for q in range(PACK):
+            nc.tensor.transpose(ts_turned[:, quarters[q]], ts_row[:, quarters[q]], identity[:])
         ts_cols = keep.tile([P, PACK], F32, name="ts_cols")
         nc.scalar.copy(ts_cols[:], ts_turned[:, 0:L:P])
         ts_spread = [bank_tile(2), bank_tile(5)]
-        for j in range(PACK):
-            c = (j % 2) * P
+        for q in range(PACK):
             nc.tensor.transpose(
-                ts_spread[j // 2][:, c : c + P], ts_cols[:, j : j + 1].to_broadcast([P, P]), identity[:]
+                ts_spread[q // 2][:, quarters[q % 2]], ts_cols[:, q : q + 1].to_broadcast([P, P]), identity[:]
             )
-        quarters = [slice(q * P, (q + 1) * P) for q in range(PACK)]
+
         x_planes = keep.tile([P, PACK * L], BF16, name="x_planes")
         for t in range(PACK):
             nc.vector.tensor_copy(x_planes[:, t * L : (t + 1) * L], u_planes[t][:].indirect(user_list[:]))
@@ -149,11 +150,15 @@ def tile_attend_gmf_hub_vu_kernel(tc, uT, vT, y, us, ts, offs, uoffs, out_0, out
             )
             turn_planes(x_planes[:, cols], x_r_values[:, cols], bank_tile(6 + n))
 
-        scale = keep.tile([P, PACK, HALF], F32, name="u_plane3", align_bytes=64)
-        for s in range(PACK):
-            nc.scalar.activation(scale[:, s, :], ts_spread[0][:, first], COPY, scale=us_cols[:, s : s + 1])
+        def scales_of(half, buffer, packed):
+            plain = keep.tile([P, PACK, HALF], F32, name=buffer, align_bytes=64)
+            for s in range(PACK):
+                nc.scalar.activation(plain[:, s, :], ts_spread[half][:, first], COPY, scale=us_cols[:, s : s + 1])
+            nc.scalar.copy(packed[:], plain[:].rearrange("p s i -> p i s"))
+            return plain
+
         scale_packed = [keep.tile([P, HALF, PACK], F32, name="scale_packed%d" % n, align_bytes=64) for n in range(2)]
-        nc.scalar.copy(scale_packed[0][:], scale[:].rearrange("p s i -> p i s"))
+        scale = scales_of(0, "u_plane3", scale_packed[0])
 
         w_packed = w_values[:].rearrange("p (i t) -> p i t", t=PACK)
         w_planes = keep.tile([P, 2 * L], BF16, name="w_planes")
@@ -167,19 +172,16 @@ def tile_attend_gmf_hub_vu_kernel(tc, uT, vT, y, us, ts, offs, uoffs, out_0, out
         x_r = operand("x_r", x_r_values, "v_plane1")
         quantize(x_r, E4M3, 0, L)
 
-        late_scale = keep.tile([P, PACK, HALF], F32, name="v_plane2", align_bytes=64)
-        for s in range(PACK):
-            nc.scalar.activation(late_scale[:, s, :], ts_spread[1][:, first], COPY, scale=us_cols[:, s : s + 1])
-        nc.scalar.copy(scale_packed[1][:], late_scale[:].rearrange("p s i -> p i s"))
+        scales_of(1, "v_plane2", scale_packed[1])
 
-        def gather_last(cols):
+        def gather_last_plane(cols):
             nc.vector.tensor_copy(w_packed[:, cols, 3], v_planes[3][:].indirect(places(item_list, cols)))
 
-        gather_last(first)
+        gather_last_plane(first)
         w_first = operand("w_first", w_values[:, 0 : PACK * HALF], columns=HALF)
-        for q in (1, 0):
+        for q in range(2):
             quantize(w_first, E4M3, q * P, (q + 1) * P)
-        gather_last(second)
+        gather_last_plane(second)
         w_second = operand("w_second", w_values[:, PACK * HALF : PACK * L], columns=HALF)
         quantize(w_second, E4M3, 0, HALF)
         w_lo = operand("w_lo", w_lo_values, "v_plane3", columns=HALF)
@@ -199,7 +201,7 @@ def tile_attend_gmf_hub_vu_kernel(tc, uT, vT, y, us, ts, offs, uoffs, out_0, out
             factors = scale_packed[q // 2][:, quarters[q % 2], :]
             engine.tensor_tensor(h_packed[:, quarters[q], :], clipped[q][:], factors, ALU.mult)
 
-        for q in (1, 0):
+        for q in range(2):
             for n in range(2):
                 acc = bank_tile((6 + q, q)[n])
                 for e in range(2):
@@ -211,22 +213,22 @@ def tile_attend_gmf_hub_vu_kernel(tc, uT, vT, y, us, ts, offs, uoffs, out_0, out
                     scale[:, rows, quarters[q]],
                     ALU.mult,
                 )
-        back = {}
+        turned_back = {}
         for q in (2, 3):
             acc = bank_tile(q)
-            product(acc[:], w_second, q - 2, x_d, E4M3, slice(0, L))
+            product(acc[:], w_second, q - 2, x_d, E4M3, whole)
             item_scaled = keep.tile([P, L], F32, name="item_scaled%d" % q)
             nc.scalar.activation(item_scaled[:], acc[:], COPY, scale=ts_cols[:, q : q + 1])
-            back[q] = bank_tile(q + 2)
+            turned_back[q] = bank_tile(q + 2)
             for s in range(PACK):
-                nc.tensor.transpose(back[q][:, quarters[s]], item_scaled[:, quarters[s]], identity[:])
-        for q in (1, 0):
+                nc.tensor.transpose(turned_back[q][:, quarters[s]], item_scaled[:, quarters[s]], identity[:])
+        for q in range(2):
             nc.vector.tensor_tensor(residual[q][:], scaled[q][:], y_rows[:, :, quarters[q]], ALU.subtract)
-        for q in (1, 0):
+        for q in range(2):
             clip(q, nc.vector)
-        for q in (1, 0):
+        for q in range(2):
             weigh(q, nc.vector)
-        for q in (1, 0):
+        for q in range(2):
             quantize(h_r, E5M2, q * P, (q + 1) * P)
 
         out_rows = {
@@ -235,34 +237,30 @@ def tile_attend_gmf_hub_vu_kernel(tc, uT, vT, y, us, ts, offs, uoffs, out_0, out
         }
         windows = {"item": item_windows, "user": user_windows}
         lists = {"item": item_list, "user": user_list}
-        whole = slice(0, L)
 
         def gradient(bank, stationary, block, moving):
             acc = bank_tile(bank)
             product(acc[:], stationary, block, moving, E5M2, whole)
             return acc
 
-        def sums_of(acc, cols, tag):
-            sums = keep.tile([P, cols.stop - cols.start], F32, name=tag, align_bytes=64)
+        def sums_of(acc, cols, buffer):
+            sums = keep.tile([P, cols.stop - cols.start], F32, name=buffer, align_bytes=64)
             nc.scalar.copy(sums[:], acc[:, cols])
             return sums[:]
 
-        def scatter(side, k, sums, cols):
-            window = windows[side][k % len(windows[side])]
+        def scatter(side, plane, sums, cols):
+            window = windows[side][plane % len(windows[side])]
             nc.vector.tensor_copy(window[:].indirect(places(lists[side], cols)), sums)
-            if side == "user" and k == PACK - 1:
-                nc.sync.dma_start(out_rows[side][k][:, 0 : T // 2], window[:, 0 : T // 2])
-                nc.scalar.dma_start(out_rows[side][k][:, T // 2 : T], window[:, T // 2 : T])
-            elif cols.stop == L:
-                nc.sync.dma_start(out_rows[side][k], window[:])
+            if cols.stop == L:
+                nc.sync.dma_start(out_rows[side][plane], window[:])
 
-        early = [gradient((6, 7, 1)[k], x_r, k, h_r) for k in range(3)]
+        early = [gradient((6, 7, 0)[k], x_r, k, h_r) for k in range(EARLY_PLANES)]
 
         for q in (2, 3):
             for s in range(PACK):
                 nc.vector.scalar_tensor_tensor(
                     residual[q][:, s, :],
-                    back[q][:, quarters[s]],
+                    turned_back[q][:, quarters[s]],
                     us_cols[:, s : s + 1],
                     y_rows[:, s, quarters[q]],
                     ALU.mult,
@@ -270,7 +268,7 @@ def tile_attend_gmf_hub_vu_kernel(tc, uT, vT, y, us, ts, offs, uoffs, out_0, out
                 )
             clip(q, nc.gpsimd)
             weigh(q, nc.gpsimd)
-        for k in range(2):
+        for k in range(EARLY_PLANES - 1):
             scatter("item", k, sums_of(early[k], first, "early_sums%d" % k), first)
         pairs = turn_pairs(w_values, 1, bank_tile(6))
         nc.scalar.copy(
@@ -280,20 +278,22 @@ def tile_attend_gmf_hub_vu_kernel(tc, uT, vT, y, us, ts, offs, uoffs, out_0, out
         w_hi = operand("w_hi", w_hi_values, columns=HALF)
         quantize(w_hi, E4M3, 0, HALF)
         quantize(h_r, E5M2, HALF, L)
-        scatter("item", 2, sums_of(early[2], first, "clipped3"), first)
+        held = EARLY_PLANES - 1
+        scatter("item", held, sums_of(early[held], first, "clipped3"), first)
 
-        for k in range(3):
-            scatter("item", k, sums_of(gradient((0, 2, 3)[k], x_r, k, h_r), second, "late_sums%d" % k), second)
+        for k in range(EARLY_PLANES):
+            scatter("item", k, sums_of(gradient(1 + k, x_r, k, h_r), second, "late_sums%d" % k), second)
 
         turned = h_i_values[:].rearrange("m (p u e s) -> m p u e s", u=2, e=2, s=PACK)
         for u in range(2):
-            pairs = turn_pairs(h_r[0], u, bank_tile((4, 5)[u]))
+            pairs = turn_pairs(h_r[0], u, bank_tile(4 + u))
             nc.scalar.copy(turned[:, :, u, :, :], pairs.rearrange("m (s p e) -> m p e s", s=PACK, e=2))
         h_i = operand("h_i", h_i_values)
         quantize(h_i, E5M2, 0, L)
         user_windows.append(keep.tile([P, T], F32, name="h_i_values", align_bytes=64))
-        nc.gpsimd.memset(user_windows[2][:], 0.0)
-        scatter("item", 3, sums_of(gradient(5, x_r, 3, h_r), whole, "last_sums"), whole)
+        nc.gpsimd.memset(user_windows[HEAD_USER_WINDOWS][:], 0.0)
+        last = PACK - 1
+        scatter("item", last, sums_of(gradient(5, x_r, last, h_r), whole, "last_sums"), whole)
         for k in range(PACK):
             acc = gradient((6, 7, 0, 1)[k], (w_lo, w_hi)[k // 2], k % 2, h_i)
             scatter("user", k, sums_of(acc, whole, "user_sums%d" % k), whole)

@@ -222,8 +222,10 @@ def tile_attend_gmf_hub_vu_kernel(tc, uT, vT, y, us, ts, offs, uoffs, out_0, out
             turned_back[q] = bank_tile(q + 2)
             for s in range(PACK):
                 nc.tensor.transpose(turned_back[q][:, quarters[s]], item_scaled[:, quarters[s]], identity[:])
-        for q in range(2):
-            nc.vector.tensor_tensor(residual[q][:], scaled[q][:], y_rows[:, :, quarters[q]], ALU.subtract)
+        for engine, q, rows in ((nc.gpsimd, 0, slice(0, 2)), (nc.vector, 0, slice(2, 4)), (nc.vector, 1, slice(0, 4))):
+            engine.tensor_tensor(
+                residual[q][:, rows, :], scaled[q][:, rows, :], y_rows[:, rows, quarters[q]], ALU.subtract
+            )
         for q in range(2):
             clip(q, nc.vector)
         for q in range(2):

@@ -19,8 +19,6 @@ L = 512
 T = 2048
 HALF = L // 2
 BAND = 16
-EARLY_PLANES = 3
-HEAD_USER_WINDOWS = 2
 
 FLOPS = 3 * 2 * L * L * L
 
@@ -34,78 +32,68 @@ def tile_attend_gmf_hub_vu_kernel(tc, uT, vT, y, us, ts, offs, uoffs, out_0, out
         def bank_tile(b):
             return psum.tile([P, L], F32, name="bank%d" % b)
 
+        def tile(name, columns, dtype):
+            return keep.tile([P, columns], dtype, name=name, align_bytes=64)
+
+        first, second, whole = slice(0, HALF), slice(HALF, L), slice(0, L)
+        halves = (first, second)
+        quarters = [slice(q * P, (q + 1) * P) for q in range(PACK)]
+
         user_list = keep.tile([P, L // BAND], U16, name="user_list")
         item_list = keep.tile([P, L // BAND], U16, name="item_list")
-        u_planes = [keep.tile([P, T], F32, name="u_plane%d" % t, align_bytes=64) for t in range(PACK)]
-        v_planes = [keep.tile([P, T], F32, name="v_plane%d" % t, align_bytes=64) for t in range(PACK)]
-        ts_table = keep.tile([P, T], F32, name="ts_table")
-        us_cols = keep.tile([P, PACK], F32, name="us_cols", align_bytes=64)
+        u_planes = [tile("u_plane%d" % t, T, F32) for t in range(PACK)]
+        v_planes = [tile("v_plane%d" % t, T, F32) for t in range(PACK)]
+        ts_table = tile("ts_table", T, F32)
+        us_cols = tile("us_cols", PACK, F32)
         y_rows = keep.tile([P, PACK, L], F32, name="y_rows", align_bytes=64)
-        item_windows = [keep.tile([P, T], F32, name="item_window%d" % k) for k in range(PACK)]
-        user_windows = [keep.tile([P, T], F32, name="user_window%d" % k) for k in range(HEAD_USER_WINDOWS)]
-        identity = keep.tile([P, P], F32, name="identity")
+        item_windows = [tile("item_window%d" % k, T, F32) for k in range(PACK)]
+        user_windows = [tile("user_window%d" % k, T, F32) for k in range(2)]
+        identity = tile("identity", P, F32)
 
-        def packed_values(name, columns=L):
-            return keep.tile([P, columns * PACK], BF16, name=name + "_values", align_bytes=64)
+        def places(offsets, cols):
+            return offsets[:, cols.start // BAND : cols.stop // BAND]
 
-        def operand(name, values, codes_buffer=None, columns=L):
-            codes = keep.tile([P, columns], U32, name=codes_buffer or name + "_codes", align_bytes=64)
-            scales = keep.tile([P, columns], U8, name=name + "_scales", align_bytes=64)
-            return values, codes, scales
+        def operand(name, values, columns, codes_buffer=None):
+            codes = tile(codes_buffer or name + "_codes", columns, U32)
+            return values, codes, tile(name + "_scales", columns, U8)
 
-        def quantize(op, fmt, lo, hi):
+        def quantize(op, fmt, cols):
             values, codes, scales = op
             nc.vector.quantize_mx(
-                out=codes[:, lo:hi].bitcast(fmt), scales=scales[:, lo:hi], in_=values[:, PACK * lo : PACK * hi]
+                out=codes[:, cols].bitcast(fmt),
+                scales=scales[:, cols],
+                in_=values[:, PACK * cols.start : PACK * cols.stop],
             )
 
         def product(acc, stationary, block, moving, moving_fmt, moving_cols):
-            cols = slice(block * P, (block + 1) * P)
             nc.tensor.matmul_mx(
                 out=acc,
-                lhsT=stationary[1][:, cols].bitcast(E4M3),
-                lhsT_scale=stationary[2][:, cols],
+                lhsT=stationary[1][:, quarters[block]].bitcast(E4M3),
+                lhsT_scale=stationary[2][:, quarters[block]],
                 rhs=moving[1][:, moving_cols].bitcast(moving_fmt),
                 rhs_scale=moving[2][:, moving_cols],
                 start=True,
                 stop=True,
             )
 
-        def turn_planes(planes, target, bank):
+        def turn_planes(planes, bank):
             words = planes.bitcast(F32).rearrange("p (a m u) -> p a u m", a=2, u=2)
             for a in range(2):
                 for u in range(2):
-                    c = (2 * a + u) * P
-                    nc.tensor.transpose(bank[:, c : c + P], words[:, a, u, :], identity[:])
+                    nc.tensor.transpose(bank[:, quarters[2 * a + u]], words[:, a, u, :], identity[:])
+            return bank[:]
+
+        def turn_features(planes, target, bank):
             nc.scalar.copy(
                 target.bitcast(F32).rearrange("m (a p u) -> m a p u", a=2, u=2),
-                bank[:].rearrange("m (a u p) -> m a p u", a=2, u=2),
+                turn_planes(planes, bank).rearrange("m (a u p) -> m a p u", a=2, u=2),
             )
-
-        def turn_pairs(values, u, bank):
-            words = values[:].bitcast(F32).rearrange("p (m s u) -> p s m u", s=PACK, u=2)
-            for s in range(PACK):
-                nc.tensor.transpose(bank[:, s * P : (s + 1) * P], words[:, s, :, u], identity[:])
-            return bank[:].bitcast(BF16)
-
-        first, second, whole = slice(0, HALF), slice(HALF, L), slice(0, L)
-        quarters = [slice(q * P, (q + 1) * P) for q in range(PACK)]
-
-        def places(offsets, cols):
-            return offsets[:, cols.start // BAND : cols.stop // BAND]
-
-        x_d_values = packed_values("x_d")
-        x_r_values = packed_values("x_r")
-        w_lo_values = packed_values("w_lo", HALF)
-        w_values = packed_values("w_d")
-        h_r = operand("h_r", packed_values("h_r"))
-        w_hi_values = packed_values("w_hi", HALF)
-        h_i_values = packed_values("h_i")
 
         u_rows = uT.rearrange("(p t) c -> t p c", t=PACK)
         v_rows = vT.rearrange("(p t) c -> t p c", t=PACK)
         nc.vector.memset(ts_table[:], 0.0)
-        nc.vector.memset(item_windows[0][:], 0.0)
+        for window in item_windows[:2]:
+            nc.vector.memset(window[:], 0.0)
         nc.sync.dma_start(u_planes[0][:], u_rows[0])
         nc.sync.dma_start(user_list[:], uoffs)
         nc.sync.dma_start(item_list[:], offs)
@@ -119,119 +107,172 @@ def tile_attend_gmf_hub_vu_kernel(tc, uT, vT, y, us, ts, offs, uoffs, out_0, out
         nc.sync.dma_start(y_rows[:], y.rearrange("b (p s) i -> p (b s) i", s=PACK))
 
         make_identity(nc, identity[:])
-        nc.gpsimd.memset(h_r[1][:, second], 0)
-        nc.gpsimd.memset(h_r[2][:, second], 0)
-        nc.gpsimd.memset(item_windows[1][:, 0 : T // 2], 0.0)
-        nc.gpsimd.memset(item_windows[1][:, T // 2 : T], 0.0)
-        for window in item_windows[2:] + user_windows:
+        nc.gpsimd.memset(item_windows[2][:, 0 : T // 2], 0.0)
+        nc.gpsimd.memset(item_windows[2][:, T // 2 : T], 0.0)
+        for window in item_windows[3:] + user_windows:
             nc.gpsimd.memset(window[:], 0.0)
 
-        ts_row = keep.tile([P, L], F32, name="ts_row")
+        ts_row = tile("ts_row", L, F32)
         nc.vector.tensor_copy(ts_row[:], ts_table[:].indirect(item_list[:]))
         ts_turned = bank_tile(4)
         for q in range(PACK):
             nc.tensor.transpose(ts_turned[:, quarters[q]], ts_row[:, quarters[q]], identity[:])
-        ts_cols = keep.tile([P, PACK], F32, name="ts_cols")
+        ts_cols = tile("ts_cols", PACK, F32)
         nc.scalar.copy(ts_cols[:], ts_turned[:, 0:L:P])
-        ts_spread = [bank_tile(2), bank_tile(5)]
+        ts_spread = bank_tile(5)
         for q in range(PACK):
-            nc.tensor.transpose(
-                ts_spread[q // 2][:, quarters[q % 2]], ts_cols[:, q : q + 1].to_broadcast([P, P]), identity[:]
-            )
+            nc.tensor.transpose(ts_spread[:, quarters[q]], ts_cols[:, q : q + 1].to_broadcast([P, P]), identity[:])
+        scale = keep.tile([P, L, PACK], F32, name="scale", align_bytes=64)
+        nc.vector.tensor_tensor(
+            scale[:],
+            ts_spread[:].unsqueeze(2).to_broadcast([P, L, PACK]),
+            us_cols[:].unsqueeze(1).to_broadcast([P, L, PACK]),
+            ALU.mult,
+        )
 
-        x_planes = keep.tile([P, PACK * L], BF16, name="x_planes")
+        scale_rows = keep.tile([P, PACK, P], F32, name="scale_rows", align_bytes=64)
+        nc.vector.tensor_tensor(
+            scale_rows[:],
+            ts_spread[:, quarters[0]].unsqueeze(1).to_broadcast([P, PACK, P]),
+            us_cols[:].unsqueeze(2).to_broadcast([P, PACK, P]),
+            ALU.mult,
+        )
+
+        x_planes = tile("x_planes", PACK * L, BF16)
+        x_r = []
         for t in range(PACK):
-            nc.vector.tensor_copy(x_planes[:, t * L : (t + 1) * L], u_planes[t][:].indirect(user_list[:]))
+            nc.scalar.activation(x_planes[:, t * L : (t + 1) * L], u_planes[t][:].indirect(user_list[:]), COPY)
+        x_d = operand("x_d", tile("x_d_values", PACK * L, BF16), L)
+        nc.vector.tensor_copy(
+            x_d[0][:].rearrange("p (s m t) -> p s m t", s=PACK, t=PACK),
+            x_planes[:].rearrange("p (t m s) -> p s m t", t=PACK, s=PACK),
+        )
+        quantize(x_d, E4M3, whole)
         for n in range(2):
-            cols = slice(2 * n * L, 2 * (n + 1) * L)
-            nc.scalar.copy(
-                x_d_values[:].rearrange("p (s m t) -> p s m t", s=PACK, t=PACK)[:, :, :, 2 * n : 2 * n + 2],
-                x_planes[:, cols].rearrange("p (t m s) -> p s m t", t=2, s=PACK),
-            )
-            turn_planes(x_planes[:, cols], x_r_values[:, cols], bank_tile(6 + n))
+            x_r.append(operand("x_r%d" % n, tile("x_r%d_values" % n, 2 * L, BF16), HALF))
+            turn_features(x_planes[:, 2 * n * L : 2 * (n + 1) * L], x_r[n][0][:], bank_tile(6 + n))
+            quantize(x_r[n], E4M3, first)
 
-        def scales_of(half, buffer, packed):
-            plain = keep.tile([P, PACK, HALF], F32, name=buffer, align_bytes=64)
-            for s in range(PACK):
-                nc.scalar.activation(plain[:, s, :], ts_spread[half][:, first], COPY, scale=us_cols[:, s : s + 1])
-            nc.scalar.copy(packed[:], plain[:].rearrange("p s i -> p i s"))
-            return plain
-
-        scale_packed = [keep.tile([P, HALF, PACK], F32, name="scale_packed%d" % n, align_bytes=64) for n in range(2)]
-        scale = scales_of(0, "u_plane3", scale_packed[0])
-
-        w_packed = w_values[:].rearrange("p (i t) -> p i t", t=PACK)
-        w_planes = keep.tile([P, 2 * L], BF16, name="w_planes")
+        w_d = operand("w_d", tile("w_d_values", PACK * L, BF16), L)
+        w_packed = w_d[0][:].rearrange("p (i t) -> p i t", t=PACK)
+        w_planes = tile("w_planes", PACK * L, BF16)
+        w_plain = w_planes[:].rearrange("p (t i) -> p i t", t=PACK)
         for t in range(2):
-            nc.vector.tensor_copy(w_planes[:, t * L : (t + 1) * L], v_planes[t][:].indirect(item_list[:]))
-        nc.scalar.copy(w_packed[:, :, 0:2], w_planes[:].rearrange("p (t i) -> p i t", t=2))
-        turn_planes(w_planes[:], w_lo_values[:], bank_tile(3))
-        nc.vector.tensor_copy(w_packed[:, :, 2], v_planes[2][:].indirect(item_list[:]))
-        x_d = operand("x_d", x_d_values, "v_plane0")
-        quantize(x_d, E4M3, 0, L)
-        x_r = operand("x_r", x_r_values, "v_plane1")
-        quantize(x_r, E4M3, 0, L)
+            nc.scalar.activation(w_planes[:, t * L : (t + 1) * L], v_planes[t][:].indirect(item_list[:]), COPY)
+        nc.vector.tensor_copy(w_packed[:, first, 0:2], w_plain[:, first, 0:2])
+        w_lo_values = tile("w_lo_values", 2 * L, BF16)
+        turn_features(w_planes[:, 0 : 2 * L], w_lo_values[:], bank_tile(3))
+        for t in range(2, PACK):
+            nc.vector.tensor_copy(w_packed[:, first, t], v_planes[t][:].indirect(places(item_list, first)))
+            nc.scalar.activation(
+                w_planes[:, t * L + HALF : (t + 1) * L], v_planes[t][:].indirect(places(item_list, second)), COPY
+            )
+            if t == 2:
+                w_lo = operand("w_lo", w_lo_values, HALF, "v_plane2")
+                quantize(w_lo, E4M3, first)
+        nc.scalar.copy(w_packed[:, second, :], w_plain[:, second, :])
+        for cols in quarters[:2]:
+            quantize(w_d, E4M3, cols)
 
-        scales_of(1, "v_plane2", scale_packed[1])
+        item_scaled = [tile("item_scaled%d" % q, L, F32) for q in range(PACK)]
+        residual = [tile("residual%d" % q, L, F32) for q in range(PACK)]
+        clipped = [tile("clipped%d" % q, L, F32) for q in range(PACK)]
+        h_r = operand("h_r", tile("h_r_values", PACK * L, BF16), L)
 
-        def gather_last_plane(cols):
-            nc.vector.tensor_copy(w_packed[:, cols, 3], v_planes[3][:].indirect(places(item_list, cols)))
+        for n in range(2):
+            acc = bank_tile(n)
+            for e in range(2):
+                product(acc[:, quarters[e]], x_d, 2 * n + e, w_d, E4M3, quarters[0])
+            nc.vector.tensor_tensor(
+                item_scaled[0][:, halves[n]],
+                acc[:, first],
+                scale_rows[:, 2 * n : 2 * n + 2, :].rearrange("p s i -> p (s i)"),
+                ALU.mult,
+            )
+        quantize(w_d, E4M3, second)
+        nc.vector.tensor_tensor(
+            residual[0][:].rearrange("p (s i) -> p s i", s=PACK),
+            item_scaled[0][:].rearrange("p (s i) -> p s i", s=PACK),
+            y_rows[:, :, quarters[0]],
+            ALU.subtract,
+        )
 
-        gather_last_plane(first)
-        w_first = operand("w_first", w_values[:, 0 : PACK * HALF], columns=HALF)
-        for q in range(2):
-            quantize(w_first, E4M3, q * P, (q + 1) * P)
-        gather_last_plane(second)
-        w_second = operand("w_second", w_values[:, PACK * HALF : PACK * L], columns=HALF)
-        quantize(w_second, E4M3, 0, HALF)
-        w_lo = operand("w_lo", w_lo_values, "v_plane3", columns=HALF)
-        quantize(w_lo, E4M3, 0, HALF)
+        turned = {}
 
-        scaled = [keep.tile([P, PACK, P], F32, name="scaled%d" % q, align_bytes=64) for q in range(2)]
-        residual = [keep.tile([P, PACK, P], F32, name="residual%d" % q, align_bytes=64) for q in range(PACK)]
-        clipped = [keep.tile([P, P, PACK], F32, name="clipped%d" % q, align_bytes=64) for q in range(PACK)]
-        h_packed = h_r[0][:].rearrange("p (i s) -> p i s", s=PACK)
+        def score(q, cols, bank):
+            acc = bank_tile(bank)
+            product(acc[:, cols], w_d, q, x_d, E4M3, cols)
+            return acc
+
+        def turn_back(q, cols, acc, bank):
+            nc.scalar.activation(item_scaled[q][:, cols], acc[:, cols], COPY, scale=ts_cols[:, q : q + 1])
+            back = bank_tile(bank)
+            for s in range(cols.start // P, cols.stop // P):
+                nc.tensor.transpose(back[:, quarters[s]], item_scaled[q][:, quarters[s]], identity[:])
+                turned[q, s] = back[:, quarters[s]]
+
+        scores = [score(1, halves[n], 2 + n) for n in range(2)]
+        for n in range(2):
+            turn_back(1, halves[n], scores[n], (4, 7)[n])
+
+        def subtract(q):
+            for s in range(PACK):
+                nc.vector.scalar_tensor_tensor(
+                    residual[q][:, quarters[s]],
+                    turned[q, s],
+                    us_cols[:, s : s + 1],
+                    y_rows[:, s, quarters[q]],
+                    ALU.mult,
+                    ALU.subtract,
+                )
 
         def clip(q, engine):
             engine.tensor_scalar(
-                clipped[q][:], residual[q][:].rearrange("p s i -> p i s"), 1.0, -1.0, ALU.min, ALU.max
+                clipped[q][:].rearrange("p (i s) -> p i s", s=PACK),
+                residual[q][:].rearrange("p (s i) -> p i s", s=PACK),
+                1.0,
+                -1.0,
+                ALU.min,
+                ALU.max,
             )
 
-        def weigh(q, engine):
-            factors = scale_packed[q // 2][:, quarters[q % 2], :]
-            engine.tensor_tensor(h_packed[:, quarters[q], :], clipped[q][:], factors, ALU.mult)
-
-        for q in range(2):
-            for n in range(2):
-                acc = bank_tile((6 + q, q)[n])
-                for e in range(2):
-                    product(acc[:, quarters[e]], x_d, 2 * n + e, w_first, E4M3, quarters[q])
-                rows = slice(2 * n, 2 * n + 2)
-                nc.vector.tensor_tensor(
-                    scaled[q][:, rows, :],
-                    acc[:, first].rearrange("p (s i) -> p s i", s=2),
-                    scale[:, rows, quarters[q]],
-                    ALU.mult,
-                )
-        turned_back = {}
-        for q in (2, 3):
-            acc = bank_tile(q)
-            product(acc[:], w_second, q - 2, x_d, E4M3, whole)
-            item_scaled = keep.tile([P, L], F32, name="item_scaled%d" % q)
-            nc.scalar.activation(item_scaled[:], acc[:], COPY, scale=ts_cols[:, q : q + 1])
-            turned_back[q] = bank_tile(q + 2)
-            for s in range(PACK):
-                nc.tensor.transpose(turned_back[q][:, quarters[s]], item_scaled[:, quarters[s]], identity[:])
-        for engine, q, rows in ((nc.gpsimd, 0, slice(0, 2)), (nc.vector, 0, slice(2, 4)), (nc.vector, 1, slice(0, 4))):
-            engine.tensor_tensor(
-                residual[q][:, rows, :], scaled[q][:, rows, :], y_rows[:, rows, quarters[q]], ALU.subtract
+        def weigh(q):
+            nc.vector.tensor_tensor(
+                h_r[0][:, q * L : (q + 1) * L],
+                clipped[q][:],
+                scale[:, quarters[q], :].rearrange("p i s -> p (i s)"),
+                ALU.mult,
             )
-        for q in range(2):
-            clip(q, nc.vector)
-        for q in range(2):
-            weigh(q, nc.vector)
-        for q in range(2):
-            quantize(h_r, E5M2, q * P, (q + 1) * P)
+
+        clip(0, nc.gpsimd)
+        scores = [score(2, whole, 3)]
+        subtract(1)
+        scores.append(score(3, whole, 4))
+        for n in range(2):
+            turn_back(2 + n, whole, scores[n], n)
+        clip(1, nc.gpsimd)
+        weigh(0)
+        subtract(2)
+        clip(2, nc.gpsimd)
+        weigh(1)
+        subtract(3)
+        quantize(h_r, E5M2, first)
+        weigh(2)
+        clip(3, nc.vector)
+        quantize(h_r, E5M2, quarters[2])
+        weigh(3)
+
+        pair_bank = bank_tile(4)
+        words = w_d[0][:].bitcast(F32).rearrange("p (m s u) -> p s m u", s=PACK, u=2)
+        for s in range(PACK):
+            nc.tensor.transpose(pair_bank[:, quarters[s]], words[:, s, :, 1], identity[:])
+        w_hi = operand("w_hi", tile("w_hi_values", 2 * L, BF16), HALF)
+        nc.scalar.copy(
+            w_hi[0][:].rearrange("m (e p s) -> m e p s", e=2, s=PACK),
+            pair_bank[:].bitcast(BF16).rearrange("m (s p e) -> m e p s", s=PACK, e=2),
+        )
+        quantize(w_hi, E4M3, first)
+        quantize(h_r, E5M2, quarters[3])
 
         out_rows = {
             "item": out_0.rearrange("(p t) c -> t p c", t=PACK),
@@ -239,63 +280,82 @@ def tile_attend_gmf_hub_vu_kernel(tc, uT, vT, y, us, ts, offs, uoffs, out_0, out
         }
         windows = {"item": item_windows, "user": user_windows}
         lists = {"item": item_list, "user": user_list}
+        sums = {"item": tile("u_plane0", PACK * L, F32), "user": tile("u_plane1", PACK * L, F32)}
 
-        def gradient(bank, stationary, block, moving):
+        def gradient(bank, side, plane, cols):
             acc = bank_tile(bank)
-            product(acc[:], stationary, block, moving, E5M2, whole)
+            stationary, moving = (x_r, h_r) if side == "item" else ((w_lo, w_hi), h_i)
+            product(acc[:, cols], stationary[plane // 2], plane % 2, moving, E5M2, cols)
             return acc
 
-        def sums_of(acc, cols, buffer):
-            sums = keep.tile([P, cols.stop - cols.start], F32, name=buffer, align_bytes=64)
-            nc.scalar.copy(sums[:], acc[:, cols])
-            return sums[:]
+        def empty(engine, acc, side, plane, cols):
+            target = sums[side][:, plane * L + cols.start : plane * L + cols.stop]
+            if engine == "scalar":
+                nc.scalar.copy(target, acc[:, cols])
+            else:
+                nc.vector.tensor_copy(target, acc[:, cols])
 
-        def scatter(side, plane, sums, cols):
-            window = windows[side][plane % len(windows[side])]
-            nc.vector.tensor_copy(window[:].indirect(places(lists[side], cols)), sums)
+        def scatter(engine, side, plane, cols):
+            window = windows[side][plane]
+            target = window[:].indirect(places(lists[side], cols))
+            source = sums[side][:, plane * L + cols.start : plane * L + cols.stop]
+            if engine == "scalar":
+                nc.scalar.activation(target, source, COPY)
+            else:
+                nc.vector.tensor_copy(target, source)
             if cols.stop == L:
                 nc.sync.dma_start(out_rows[side][plane], window[:])
 
-        early = [gradient((6, 7, 0)[k], x_r, k, h_r) for k in range(EARLY_PLANES)]
+        for k in range(2):
+            empty("scalar", gradient(2 + k, "item", k, first), "item", k, first)
+            scatter("scalar", "item", k, first)
 
-        for q in (2, 3):
-            for s in range(PACK):
-                nc.vector.scalar_tensor_tensor(
-                    residual[q][:, s, :],
-                    turned_back[q][:, quarters[s]],
-                    us_cols[:, s : s + 1],
-                    y_rows[:, s, quarters[q]],
-                    ALU.mult,
-                    ALU.subtract,
-                )
-            clip(q, nc.gpsimd)
-            weigh(q, nc.gpsimd)
-        for k in range(EARLY_PLANES - 1):
-            scatter("item", k, sums_of(early[k], first, "early_sums%d" % k), first)
-        pairs = turn_pairs(w_values, 1, bank_tile(6))
-        nc.scalar.copy(
-            w_hi_values[:].rearrange("m (e p s) -> m e p s", e=2, s=PACK),
-            pairs.rearrange("m (s p e) -> m e p s", s=PACK, e=2),
+        late = [gradient(5 + k, "item", k, second) for k in range(2)]
+        third = gradient(7, "item", 2, whole)
+        empty("vector", late[0], "item", 0, second)
+        empty("vector", third, "item", 2, first)
+        scatter("vector", "item", 0, second)
+        empty("vector", third, "item", 2, second)
+        for cols in halves:
+            scatter("vector", "item", 2, cols)
+        empty("scalar", late[1], "item", 1, second)
+        scatter("scalar", "item", 1, second)
+
+        h_planes = tile("x_r0_codes", PACK * L, BF16)
+        nc.gpsimd.tensor_scalar(
+            h_planes[:].rearrange("p (s i) -> p s i", s=PACK),
+            h_r[0][:].rearrange("p (i s) -> p s i", s=PACK),
+            1.0,
+            0.0,
+            ALU.mult,
+            ALU.add,
         )
-        w_hi = operand("w_hi", w_hi_values, columns=HALF)
-        quantize(w_hi, E4M3, 0, HALF)
-        quantize(h_r, E5M2, HALF, L)
-        held = EARLY_PLANES - 1
-        scatter("item", held, sums_of(early[held], first, "clipped3"), first)
+        h_i = operand("h_i", tile("h_i_values", PACK * L, BF16), L)
+        h_i_words = h_i[0][:].bitcast(F32).rearrange("m (p s u) -> m p s u", s=PACK, u=2)
+        for n in range(2):
+            nc.scalar.copy(
+                h_i_words[:, :, 2 * n : 2 * n + 2, :],
+                turn_planes(h_planes[:, 2 * n * L : 2 * (n + 1) * L], bank_tile(n)).rearrange(
+                    "m (a u p) -> m p a u", a=2, u=2
+                ),
+            )
+        for cols in halves:
+            quantize(h_i, E5M2, cols)
+        for buffer in ("h_r_values", "h_i_values"):
+            user_windows.append(tile(buffer, T, F32))
+            nc.gpsimd.memset(user_windows[-1][:], 0.0)
 
-        for k in range(EARLY_PLANES):
-            scatter("item", k, sums_of(gradient(1 + k, x_r, k, h_r), second, "late_sums%d" % k), second)
-
-        turned = h_i_values[:].rearrange("m (p u e s) -> m p u e s", u=2, e=2, s=PACK)
-        for u in range(2):
-            pairs = turn_pairs(h_r[0], u, bank_tile(4 + u))
-            nc.scalar.copy(turned[:, :, u, :, :], pairs.rearrange("m (s p e) -> m p e s", s=PACK, e=2))
-        h_i = operand("h_i", h_i_values)
-        quantize(h_i, E5M2, 0, L)
-        user_windows.append(keep.tile([P, T], F32, name="h_i_values", align_bytes=64))
-        nc.gpsimd.memset(user_windows[HEAD_USER_WINDOWS][:], 0.0)
-        last = PACK - 1
-        scatter("item", last, sums_of(gradient(5, x_r, last, h_r), whole, "last_sums"), whole)
+        empty("scalar", gradient(1, "item", 3, whole), "item", 3, whole)
+        for cols in halves:
+            scatter("scalar", "item", 3, cols)
         for k in range(PACK):
-            acc = gradient((6, 7, 0, 1)[k], (w_lo, w_hi)[k // 2], k % 2, h_i)
-            scatter("user", k, sums_of(acc, whole, "user_sums%d" % k), whole)
+            engine = ("vector", "scalar")[k % 2]
+            if k == 0:
+                for n in range(2):
+                    empty(engine, gradient(2 + n, "user", k, halves[n]), "user", k, halves[n])
+            else:
+                acc = gradient(3 + k, "user", k, whole)
+                for cols in halves:
+                    empty(engine, acc, "user", k, cols)
+            for cols in halves:
+                scatter(engine, "user", k, cols)

@@ -211,9 +211,10 @@ def tile_attend_gmf_hub_vu_kernel(tc, uT, vT, y, us, ts, offs, uoffs, out_0, out
                 nc.tensor.transpose(back[:, quarters[s]], item_scaled[q][:, quarters[s]], identity[:])
                 turned[q, s] = back[:, quarters[s]]
 
-        scores = [score(1, halves[n], 2 + n) for n in range(2)]
-        for n in range(2):
-            turn_back(1, halves[n], scores[n], (4, 7)[n])
+        for q, banks, back_banks in ((1, (2, 3), (4, 7)), (2, (0, 1), (2, 3)), (3, (5, 6), (0, 1))):
+            scores = [score(q, halves[n], banks[n]) for n in range(2)]
+            for n in range(2):
+                turn_back(q, halves[n], scores[n], back_banks[n])
 
         def subtract(q):
             for s in range(PACK):
@@ -245,11 +246,7 @@ def tile_attend_gmf_hub_vu_kernel(tc, uT, vT, y, us, ts, offs, uoffs, out_0, out
             )
 
         clip(0, nc.gpsimd)
-        scores = [score(2, whole, 3)]
         subtract(1)
-        scores.append(score(3, whole, 4))
-        for n in range(2):
-            turn_back(2 + n, whole, scores[n], n)
         clip(1, nc.gpsimd)
         weigh(0)
         subtract(2)
@@ -262,7 +259,7 @@ def tile_attend_gmf_hub_vu_kernel(tc, uT, vT, y, us, ts, offs, uoffs, out_0, out
         quantize(h_r, E5M2, quarters[2])
         weigh(3)
 
-        pair_bank = bank_tile(4)
+        pair_bank = bank_tile(6)
         words = w_d[0][:].bitcast(F32).rearrange("p (m s u) -> p s m u", s=PACK, u=2)
         for s in range(PACK):
             nc.tensor.transpose(pair_bank[:, quarters[s]], words[:, s, :, 1], identity[:])
@@ -271,8 +268,6 @@ def tile_attend_gmf_hub_vu_kernel(tc, uT, vT, y, us, ts, offs, uoffs, out_0, out
             w_hi[0][:].rearrange("m (e p s) -> m e p s", e=2, s=PACK),
             pair_bank[:].bitcast(BF16).rearrange("m (s p e) -> m e p s", s=PACK, e=2),
         )
-        quantize(w_hi, E4M3, first)
-        quantize(h_r, E5M2, quarters[3])
 
         out_rows = {
             "item": out_0.rearrange("(p t) c -> t p c", t=PACK),
@@ -280,7 +275,11 @@ def tile_attend_gmf_hub_vu_kernel(tc, uT, vT, y, us, ts, offs, uoffs, out_0, out
         }
         windows = {"item": item_windows, "user": user_windows}
         lists = {"item": item_list, "user": user_list}
-        sums = {"item": tile("u_plane0", PACK * L, F32), "user": tile("u_plane1", PACK * L, F32)}
+        sums = {}
+        for side, buffer in (("item", "u_plane0"), ("user", "u_plane1")):
+            row = tile(buffer, PACK * L, F32)
+            for k in range(2 * PACK):
+                sums[side, k // 2, k % 2] = row[:, k * HALF : (k + 1) * HALF]
 
         def gradient(bank, side, plane, cols):
             acc = bank_tile(bank)
@@ -288,51 +287,54 @@ def tile_attend_gmf_hub_vu_kernel(tc, uT, vT, y, us, ts, offs, uoffs, out_0, out
             product(acc[:, cols], stationary[plane // 2], plane % 2, moving, E5M2, cols)
             return acc
 
-        def empty(engine, acc, side, plane, cols):
-            target = sums[side][:, plane * L + cols.start : plane * L + cols.stop]
+        def empty(engine, acc, side, plane, n):
             if engine == "scalar":
-                nc.scalar.copy(target, acc[:, cols])
+                nc.scalar.copy(sums[side, plane, n], acc[:, halves[n]])
             else:
-                nc.vector.tensor_copy(target, acc[:, cols])
+                nc.vector.tensor_copy(sums[side, plane, n], acc[:, halves[n]])
 
-        def scatter(engine, side, plane, cols):
-            window = windows[side][plane]
-            target = window[:].indirect(places(lists[side], cols))
-            source = sums[side][:, plane * L + cols.start : plane * L + cols.stop]
+        def scatter(engine, side, plane, n):
+            target = windows[side][plane][:].indirect(places(lists[side], halves[n]))
             if engine == "scalar":
-                nc.scalar.activation(target, source, COPY)
+                nc.scalar.activation(target, sums[side, plane, n], COPY)
             else:
-                nc.vector.tensor_copy(target, source)
-            if cols.stop == L:
-                nc.sync.dma_start(out_rows[side][plane], window[:])
+                nc.vector.tensor_copy(target, sums[side, plane, n])
 
+        def store(side, plane):
+            nc.sync.dma_start(out_rows[side][plane], windows[side][plane][:])
+
+        early = [gradient((4, 7, 5, 2)[k], "item", k, first) for k in range(PACK)]
         for k in range(2):
-            empty("scalar", gradient(2 + k, "item", k, first), "item", k, first)
-            scatter("scalar", "item", k, first)
-
-        late = [gradient(5 + k, "item", k, second) for k in range(2)]
-        third = gradient(7, "item", 2, whole)
-        empty("vector", late[0], "item", 0, second)
-        empty("vector", third, "item", 2, first)
-        scatter("vector", "item", 0, second)
-        empty("vector", third, "item", 2, second)
-        for cols in halves:
-            scatter("vector", "item", 2, cols)
-        empty("scalar", late[1], "item", 1, second)
-        scatter("scalar", "item", 1, second)
+            empty("scalar", early[k], "item", k, 0)
+            scatter("scalar", "item", k, 0)
+        empty("vector", early[2], "item", 2, 0)
+        quantize(h_r, E5M2, quarters[3])
+        empty("vector", early[3], "item", 3, 0)
+        late = [gradient((3, 4, 7, 5)[k], "item", k, second) for k in range(PACK)]
+        empty("vector", late[0], "item", 0, 1)
+        quantize(w_hi, E4M3, first)
+        scatter("vector", "item", 0, 1)
+        store("item", 0)
+        empty("scalar", late[1], "item", 1, 1)
+        scatter("scalar", "item", 1, 1)
+        store("item", 1)
+        empty("vector", late[2], "item", 2, 1)
+        for n in (1, 0):
+            scatter("vector", "item", 2, n)
+        store("item", 2)
 
         h_planes = tile("x_r0_codes", PACK * L, BF16)
-        nc.gpsimd.tensor_scalar(
-            h_planes[:].rearrange("p (s i) -> p s i", s=PACK),
-            h_r[0][:].rearrange("p (i s) -> p s i", s=PACK),
-            1.0,
-            0.0,
-            ALU.mult,
-            ALU.add,
-        )
         h_i = operand("h_i", tile("h_i_values", PACK * L, BF16), L)
         h_i_words = h_i[0][:].bitcast(F32).rearrange("m (p s u) -> m p s u", s=PACK, u=2)
         for n in range(2):
+            nc.gpsimd.tensor_scalar(
+                h_planes[:].rearrange("p (s i) -> p s i", s=PACK)[:, 2 * n : 2 * n + 2, :],
+                h_r[0][:].rearrange("p (i s) -> p s i", s=PACK)[:, 2 * n : 2 * n + 2, :],
+                1.0,
+                0.0,
+                ALU.mult,
+                ALU.add,
+            )
             nc.scalar.copy(
                 h_i_words[:, :, 2 * n : 2 * n + 2, :],
                 turn_planes(h_planes[:, 2 * n * L : 2 * (n + 1) * L], bank_tile(n)).rearrange(
@@ -345,17 +347,19 @@ def tile_attend_gmf_hub_vu_kernel(tc, uT, vT, y, us, ts, offs, uoffs, out_0, out
             user_windows.append(tile(buffer, T, F32))
             nc.gpsimd.memset(user_windows[-1][:], 0.0)
 
-        empty("scalar", gradient(1, "item", 3, whole), "item", 3, whole)
-        for cols in halves:
-            scatter("scalar", "item", 3, cols)
+        sums["item", 3, 1] = tile("x_r0_codes", HALF, F32)[:]
+        empty("scalar", late[3], "item", 3, 1)
+        for n in (1, 0):
+            scatter("scalar", "item", 3, n)
+        store("item", 3)
         for k in range(PACK):
             engine = ("vector", "scalar")[k % 2]
             if k == 0:
-                for n in range(2):
-                    empty(engine, gradient(2 + n, "user", k, halves[n]), "user", k, halves[n])
+                accs = [gradient(2 + n, "user", k, halves[n]) for n in range(2)]
             else:
-                acc = gradient(3 + k, "user", k, whole)
-                for cols in halves:
-                    empty(engine, acc, "user", k, cols)
-            for cols in halves:
-                scatter(engine, "user", k, cols)
+                accs = [gradient((4, 6, 7)[k - 1], "user", k, whole)] * 2
+            for n in range(2):
+                empty(engine, accs[n], "user", k, n)
+            for n in range(2):
+                scatter(engine, "user", k, n)
+            store("user", k)

@@ -27,6 +27,7 @@ def tile_attend_gmf_hub_vu_kernel(tc, uT, vT, y, us, ts, offs, uoffs, out_0, out
     nc = tc.nc
     with ExitStack() as ctx:
         keep = ctx.enter_context(tc.tile_pool(name="keep", bufs=1))
+        laid = ctx.enter_context(tc.tile_pool(name="laid", bufs=1))
         psum = ctx.enter_context(tc.psum_pool(name="psum", bufs=1))
 
         def bank_tile(b):
@@ -47,7 +48,7 @@ def tile_attend_gmf_hub_vu_kernel(tc, uT, vT, y, us, ts, offs, uoffs, out_0, out
         us_cols = tile("us_cols", PACK, F32)
         y_rows = keep.tile([P, PACK, L], F32, name="y_rows", align_bytes=64)
         item_windows = [tile("item_window%d" % k, T, F32) for k in range(PACK)]
-        user_windows = [tile("user_window%d" % k, T, F32) for k in range(2)]
+        user_windows = [tile("user_window%d" % k, T, F32) for k in range(1)]
         identity = tile("identity", P, F32)
 
         def places(offsets, cols):
@@ -83,8 +84,8 @@ def tile_attend_gmf_hub_vu_kernel(tc, uT, vT, y, us, ts, offs, uoffs, out_0, out
                     nc.tensor.transpose(bank[:, quarters[2 * a + u]], words[:, a, u, :], identity[:])
             return bank[:]
 
-        def turn_features(planes, target, bank):
-            nc.scalar.copy(
+        def turn_features(copy, planes, target, bank):
+            copy(
                 target.bitcast(F32).rearrange("m (a p u) -> m a p u", a=2, u=2),
                 turn_planes(planes, bank).rearrange("m (a u p) -> m a p u", a=2, u=2),
             )
@@ -92,8 +93,7 @@ def tile_attend_gmf_hub_vu_kernel(tc, uT, vT, y, us, ts, offs, uoffs, out_0, out
         u_rows = uT.rearrange("(p t) c -> t p c", t=PACK)
         v_rows = vT.rearrange("(p t) c -> t p c", t=PACK)
         nc.vector.memset(ts_table[:], 0.0)
-        for window in item_windows[:2]:
-            nc.vector.memset(window[:], 0.0)
+        nc.vector.memset(item_windows[0][:], 0.0)
         nc.sync.dma_start(u_planes[0][:], u_rows[0])
         nc.sync.dma_start(user_list[:], uoffs)
         nc.sync.dma_start(item_list[:], offs)
@@ -107,9 +107,9 @@ def tile_attend_gmf_hub_vu_kernel(tc, uT, vT, y, us, ts, offs, uoffs, out_0, out
         nc.sync.dma_start(y_rows[:], y.rearrange("b (p s) i -> p (b s) i", s=PACK))
 
         make_identity(nc, identity[:])
-        nc.gpsimd.memset(item_windows[2][:, 0 : T // 2], 0.0)
-        nc.gpsimd.memset(item_windows[2][:, T // 2 : T], 0.0)
-        for window in item_windows[3:] + user_windows:
+        nc.gpsimd.memset(item_windows[1][:, 0 : T // 2], 0.0)
+        nc.gpsimd.memset(item_windows[1][:, T // 2 : T], 0.0)
+        for window in item_windows[2:] + user_windows:
             nc.gpsimd.memset(window[:], 0.0)
 
         ts_row = tile("ts_row", L, F32)
@@ -118,14 +118,16 @@ def tile_attend_gmf_hub_vu_kernel(tc, uT, vT, y, us, ts, offs, uoffs, out_0, out
         for q in range(PACK):
             nc.tensor.transpose(ts_turned[:, quarters[q]], ts_row[:, quarters[q]], identity[:])
         ts_cols = tile("ts_cols", PACK, F32)
-        nc.scalar.copy(ts_cols[:], ts_turned[:, 0:L:P])
+        nc.vector.tensor_copy(ts_cols[:], ts_turned[:, 0:L:P])
         ts_spread = bank_tile(5)
         for q in range(PACK):
             nc.tensor.transpose(ts_spread[:, quarters[q]], ts_cols[:, q : q + 1].to_broadcast([P, P]), identity[:])
+        ts_rows = laid.tile([P, L], F32, name="ts_rows", align_bytes=64, offset=3 * 1024)
+        nc.vector.tensor_copy(ts_rows[:], ts_spread[:])
         scale = keep.tile([P, L, PACK], F32, name="scale", align_bytes=64)
         nc.vector.tensor_tensor(
             scale[:],
-            ts_spread[:].unsqueeze(2).to_broadcast([P, L, PACK]),
+            ts_rows[:].unsqueeze(2).to_broadcast([P, L, PACK]),
             us_cols[:].unsqueeze(1).to_broadcast([P, L, PACK]),
             ALU.mult,
         )
@@ -133,7 +135,7 @@ def tile_attend_gmf_hub_vu_kernel(tc, uT, vT, y, us, ts, offs, uoffs, out_0, out
         scale_rows = keep.tile([P, PACK, P], F32, name="scale_rows", align_bytes=64)
         nc.vector.tensor_tensor(
             scale_rows[:],
-            ts_spread[:, quarters[0]].unsqueeze(1).to_broadcast([P, PACK, P]),
+            ts_rows[:, quarters[0]].unsqueeze(1).to_broadcast([P, PACK, P]),
             us_cols[:].unsqueeze(2).to_broadcast([P, PACK, P]),
             ALU.mult,
         )
@@ -142,7 +144,7 @@ def tile_attend_gmf_hub_vu_kernel(tc, uT, vT, y, us, ts, offs, uoffs, out_0, out
         x_r = []
         for t in range(PACK):
             nc.scalar.activation(x_planes[:, t * L : (t + 1) * L], u_planes[t][:].indirect(user_list[:]), COPY)
-        x_d = operand("x_d", tile("x_d_values", PACK * L, BF16), L)
+        x_d = operand("x_d", laid.tile([P, PACK * L], BF16, name="x_d_values", align_bytes=64, offset=0), L)
         nc.vector.tensor_copy(
             x_d[0][:].rearrange("p (s m t) -> p s m t", s=PACK, t=PACK),
             x_planes[:].rearrange("p (t m s) -> p s m t", t=PACK, s=PACK),
@@ -150,25 +152,24 @@ def tile_attend_gmf_hub_vu_kernel(tc, uT, vT, y, us, ts, offs, uoffs, out_0, out
         quantize(x_d, E4M3, whole)
         for n in range(2):
             x_r.append(operand("x_r%d" % n, tile("x_r%d_values" % n, 2 * L, BF16), HALF))
-            turn_features(x_planes[:, 2 * n * L : 2 * (n + 1) * L], x_r[n][0][:], bank_tile(6 + n))
+            turn_features(nc.vector.tensor_copy, x_planes[:, 2 * n * L : 2 * (n + 1) * L], x_r[n][0][:], bank_tile(4 + n))
             quantize(x_r[n], E4M3, first)
 
-        w_d = operand("w_d", tile("w_d_values", PACK * L, BF16), L)
+        w_d = operand("w_d", laid.tile([P, PACK * L], BF16, name="w_d_values", align_bytes=64, offset=4 * 1024), L)
         w_packed = w_d[0][:].rearrange("p (i t) -> p i t", t=PACK)
         w_planes = tile("w_planes", PACK * L, BF16)
         w_plain = w_planes[:].rearrange("p (t i) -> p i t", t=PACK)
         for t in range(2):
             nc.scalar.activation(w_planes[:, t * L : (t + 1) * L], v_planes[t][:].indirect(item_list[:]), COPY)
         nc.vector.tensor_copy(w_packed[:, first, 0:2], w_plain[:, first, 0:2])
-        w_lo_values = tile("w_lo_values", 2 * L, BF16)
-        turn_features(w_planes[:, 0 : 2 * L], w_lo_values[:], bank_tile(3))
         for t in range(2, PACK):
             nc.vector.tensor_copy(w_packed[:, first, t], v_planes[t][:].indirect(places(item_list, first)))
             nc.scalar.activation(
                 w_planes[:, t * L + HALF : (t + 1) * L], v_planes[t][:].indirect(places(item_list, second)), COPY
             )
             if t == 2:
-                w_lo = operand("w_lo", w_lo_values, HALF, "v_plane2")
+                w_lo = operand("w_lo", tile("w_lo_values", 2 * L, BF16), HALF)
+                turn_features(nc.vector.tensor_copy, w_planes[:, 0 : 2 * L], w_lo[0][:], bank_tile(4))
                 quantize(w_lo, E4M3, first)
         nc.scalar.copy(w_packed[:, second, :], w_plain[:, second, :])
         for cols in quarters[:2]:
@@ -263,9 +264,9 @@ def tile_attend_gmf_hub_vu_kernel(tc, uT, vT, y, us, ts, offs, uoffs, out_0, out
         words = w_d[0][:].bitcast(F32).rearrange("p (m s u) -> p s m u", s=PACK, u=2)
         for s in range(PACK):
             nc.tensor.transpose(pair_bank[:, quarters[s]], words[:, s, :, 1], identity[:])
-        w_hi = operand("w_hi", tile("w_hi_values", 2 * L, BF16), HALF)
+        w_hi_values = tile("w_hi_values", 2 * L, BF16)
         nc.scalar.copy(
-            w_hi[0][:].rearrange("m (e p s) -> m e p s", e=2, s=PACK),
+            w_hi_values[:].rearrange("m (e p s) -> m e p s", e=2, s=PACK),
             pair_bank[:].bitcast(BF16).rearrange("m (s p e) -> m e p s", s=PACK, e=2),
         )
 
@@ -307,12 +308,13 @@ def tile_attend_gmf_hub_vu_kernel(tc, uT, vT, y, us, ts, offs, uoffs, out_0, out
         for k in range(2):
             empty("scalar", early[k], "item", k, 0)
             scatter("scalar", "item", k, 0)
-        empty("vector", early[2], "item", 2, 0)
+        w_hi = operand("w_hi", w_hi_values, HALF, "clipped2")
+        quantize(w_hi, E4M3, first)
         quantize(h_r, E5M2, quarters[3])
         empty("vector", early[3], "item", 3, 0)
         late = [gradient((3, 4, 7, 5)[k], "item", k, second) for k in range(PACK)]
         empty("vector", late[0], "item", 0, 1)
-        quantize(w_hi, E4M3, first)
+        empty("vector", early[2], "item", 2, 0)
         scatter("vector", "item", 0, 1)
         store("item", 0)
         empty("scalar", late[1], "item", 1, 1)
@@ -324,7 +326,7 @@ def tile_attend_gmf_hub_vu_kernel(tc, uT, vT, y, us, ts, offs, uoffs, out_0, out
         store("item", 2)
 
         h_planes = tile("x_r0_codes", PACK * L, BF16)
-        h_i = operand("h_i", tile("h_i_values", PACK * L, BF16), L)
+        h_i = operand("h_i", laid.tile([P, PACK * L], BF16, name="h_i_values", align_bytes=64, offset=14 * 1024), L)
         h_i_words = h_i[0][:].bitcast(F32).rearrange("m (p s u) -> m p s u", s=PACK, u=2)
         for n in range(2):
             nc.gpsimd.tensor_scalar(
@@ -343,9 +345,13 @@ def tile_attend_gmf_hub_vu_kernel(tc, uT, vT, y, us, ts, offs, uoffs, out_0, out
             )
         for cols in halves:
             quantize(h_i, E5M2, cols)
-        for buffer in ("h_r_values", "h_i_values"):
-            user_windows.append(tile(buffer, T, F32))
-            nc.gpsimd.memset(user_windows[-1][:], 0.0)
+        user_windows.append(tile("h_r_values", T, F32))
+        for k in (2, 3):
+            user_windows.append(
+                laid.tile([P, T], F32, name="user_window%d" % k, align_bytes=64, offset=(k - 1) * 8 * 1024)
+            )
+        for window in user_windows[1:]:
+            nc.gpsimd.memset(window[:], 0.0)
 
         sums["item", 3, 1] = tile("x_r0_codes", HALF, F32)[:]
         empty("scalar", late[3], "item", 3, 1)

@@ -228,8 +228,8 @@ def tile_attend_gmf_hub_vu_kernel(tc, uT, vT, y, us, ts, offs, uoffs, out_0, out
                     ALU.subtract,
                 )
 
-        def clip(q, engine):
-            engine.tensor_scalar(
+        def clip(q):
+            nc.vector.tensor_scalar(
                 clipped[q][:].rearrange("p (i s) -> p i s", s=PACK),
                 residual[q][:].rearrange("p (s i) -> p i s", s=PACK),
                 1.0,
@@ -246,19 +246,18 @@ def tile_attend_gmf_hub_vu_kernel(tc, uT, vT, y, us, ts, offs, uoffs, out_0, out
                 ALU.mult,
             )
 
-        clip(0, nc.gpsimd)
         subtract(1)
-        clip(1, nc.gpsimd)
+        for q in range(2):
+            clip(q)
         weigh(0)
         subtract(2)
-        clip(2, nc.gpsimd)
         weigh(1)
         subtract(3)
         quantize(h_r, E5M2, first)
-        weigh(2)
-        clip(3, nc.vector)
-        quantize(h_r, E5M2, quarters[2])
-        weigh(3)
+        for q in (2, 3):
+            clip(q)
+        for q in (2, 3):
+            weigh(q)
 
         pair_bank = bank_tile(6)
         words = w_d[0][:].bitcast(F32).rearrange("p (m s u) -> p s m u", s=PACK, u=2)
@@ -308,21 +307,26 @@ def tile_attend_gmf_hub_vu_kernel(tc, uT, vT, y, us, ts, offs, uoffs, out_0, out
         for k in range(2):
             empty("scalar", early[k], "item", k, 0)
             scatter("scalar", "item", k, 0)
-        w_hi = operand("w_hi", w_hi_values, HALF, "clipped2")
+        for q in (2, 3):
+            quantize(h_r, E5M2, quarters[q])
+        w_hi = operand("w_hi", w_hi_values, HALF, "clipped3")
         quantize(w_hi, E4M3, first)
-        quantize(h_r, E5M2, quarters[3])
-        empty("vector", early[3], "item", 3, 0)
-        late = [gradient((3, 4, 7, 5)[k], "item", k, second) for k in range(PACK)]
-        empty("vector", late[0], "item", 0, 1)
-        empty("vector", early[2], "item", 2, 0)
+        late = {k: gradient((3, 4, 0, 7)[k], "item", k, second) for k in (0, 2, 1, 3)}
+        sums["item", 0, 1] = laid.tile([P, HALF], F32, name="closing_sums", align_bytes=64, offset=24 * 1024 + 512)[:]
+        for k in (0, 2):
+            empty("vector", late[k], "item", k, 1)
         scatter("vector", "item", 0, 1)
         store("item", 0)
         empty("scalar", late[1], "item", 1, 1)
         scatter("scalar", "item", 1, 1)
         store("item", 1)
-        empty("vector", late[2], "item", 2, 1)
-        for n in (1, 0):
-            scatter("vector", "item", 2, n)
+        scatter("vector", "item", 2, 1)
+        for k in (2, 3):
+            sums["item", k, 0] = laid.tile(
+                [P, HALF], F32, name="held_sums%d" % k, align_bytes=64, offset=(22 + k) * 1024
+            )[:]
+            empty("vector", early[k], "item", k, 0)
+        scatter("vector", "item", 2, 0)
         store("item", 2)
 
         h_planes = tile("x_r0_codes", PACK * L, BF16)
@@ -339,7 +343,7 @@ def tile_attend_gmf_hub_vu_kernel(tc, uT, vT, y, us, ts, offs, uoffs, out_0, out
             )
             nc.scalar.copy(
                 h_i_words[:, :, 2 * n : 2 * n + 2, :],
-                turn_planes(h_planes[:, 2 * n * L : 2 * (n + 1) * L], bank_tile(n)).rearrange(
+                turn_planes(h_planes[:, 2 * n * L : 2 * (n + 1) * L], bank_tile((1, 6)[n])).rearrange(
                     "m (a u p) -> m p a u", a=2, u=2
                 ),
             )
@@ -363,7 +367,7 @@ def tile_attend_gmf_hub_vu_kernel(tc, uT, vT, y, us, ts, offs, uoffs, out_0, out
             if k == 0:
                 accs = [gradient(2 + n, "user", k, halves[n]) for n in range(2)]
             else:
-                accs = [gradient((4, 6, 7)[k - 1], "user", k, whole)] * 2
+                accs = [gradient((4, 0, 1)[k - 1], "user", k, whole)] * 2
             for n in range(2):
                 empty(engine, accs[n], "user", k, n)
             for n in range(2):

@@ -151,9 +151,11 @@ def tile_attend_gmf_hub_vu_kernel(tc, uT, vT, y, us, ts, offs, uoffs, out_0, out
         )
         quantize(x_d, E4M3, whole)
         for n in range(2):
-            x_r.append(operand("x_r%d" % n, tile("x_r%d_values" % n, 2 * L, BF16), HALF))
-            turn_features(nc.vector.tensor_copy, x_planes[:, 2 * n * L : 2 * (n + 1) * L], x_r[n][0][:], bank_tile(4 + n))
-            quantize(x_r[n], E4M3, first)
+            values = tile("x_r%d_values" % n, 2 * L, BF16)
+            turn_features(nc.vector.tensor_copy, x_planes[:, 2 * n * L : 2 * (n + 1) * L], values[:], bank_tile(4 + n))
+            for a in range(2):
+                x_r.append(operand("x_r%d" % (2 * n + a), values[:, a * L : (a + 1) * L], P))
+                quantize(x_r[-1], E4M3, quarters[0])
 
         w_d = operand("w_d", laid.tile([P, PACK * L], BF16, name="w_d_values", align_bytes=64, offset=4 * 1024), L)
         w_packed = w_d[0][:].rearrange("p (i t) -> p i t", t=PACK)
@@ -283,8 +285,10 @@ def tile_attend_gmf_hub_vu_kernel(tc, uT, vT, y, us, ts, offs, uoffs, out_0, out
 
         def gradient(bank, side, plane, cols):
             acc = bank_tile(bank)
-            stationary, moving = (x_r, h_r) if side == "item" else ((w_lo, w_hi), h_i)
-            product(acc[:, cols], stationary[plane // 2], plane % 2, moving, E5M2, cols)
+            if side == "item":
+                product(acc[:, cols], x_r[plane], 0, h_r, E5M2, cols)
+            else:
+                product(acc[:, cols], (w_lo, w_hi)[plane // 2], plane % 2, h_i, E5M2, cols)
             return acc
 
         def empty(engine, acc, side, plane, n):
@@ -311,10 +315,12 @@ def tile_attend_gmf_hub_vu_kernel(tc, uT, vT, y, us, ts, offs, uoffs, out_0, out
             quantize(h_r, E5M2, quarters[q])
         w_hi = operand("w_hi", w_hi_values, HALF, "clipped3")
         quantize(w_hi, E4M3, first)
-        late = {k: gradient((3, 4, 0, 7)[k], "item", k, second) for k in (0, 2, 1, 3)}
+        closing = [gradient((3, 1)[q - 2], "item", 0, quarters[q])[:, quarters[q]] for q in (2, 3)]
+        late = {k: gradient((4, 0, 7)[k - 1], "item", k, second) for k in (2, 1, 3)}
         sums["item", 0, 1] = laid.tile([P, HALF], F32, name="closing_sums", align_bytes=64, offset=24 * 1024 + 512)[:]
-        for k in (0, 2):
-            empty("vector", late[k], "item", k, 1)
+        for n in range(2):
+            nc.vector.tensor_copy(sums["item", 0, 1][:, quarters[n]], closing[n])
+        empty("vector", late[2], "item", 2, 1)
         scatter("vector", "item", 0, 1)
         store("item", 0)
         empty("scalar", late[1], "item", 1, 1)

@@ -214,10 +214,11 @@ def tile_attend_gmf_hub_vu_kernel(tc, uT, vT, y, us, ts, offs, uoffs, out_0, out
                 nc.tensor.transpose(back[:, quarters[s]], item_scaled[q][:, quarters[s]], identity[:])
                 turned[q, s] = back[:, quarters[s]]
 
-        for q, banks, back_banks in ((1, (2, 3), (4, 7)), (2, (0, 1), (2, 3)), (3, (5, 6), (0, 1))):
+        for q, banks, back_banks in ((1, (2, 3), (4, 7)), (2, (0, 1), (2, 3))):
             scores = [score(q, halves[n], banks[n]) for n in range(2)]
             for n in range(2):
                 turn_back(q, halves[n], scores[n], back_banks[n])
+        scores = [score(3, halves[n], 5 + n) for n in range(2)]
 
         def subtract(q):
             for s in range(PACK):
@@ -249,27 +250,30 @@ def tile_attend_gmf_hub_vu_kernel(tc, uT, vT, y, us, ts, offs, uoffs, out_0, out
             )
 
         subtract(1)
-        for q in range(2):
-            clip(q)
-        weigh(0)
-        subtract(2)
-        weigh(1)
-        subtract(3)
-        quantize(h_r, E5M2, first)
-        for q in (2, 3):
-            clip(q)
-        for q in (2, 3):
-            weigh(q)
 
-        pair_bank = bank_tile(6)
+        pair_bank = bank_tile(7)
         words = w_d[0][:].bitcast(F32).rearrange("p (m s u) -> p s m u", s=PACK, u=2)
         for s in range(PACK):
             nc.tensor.transpose(pair_bank[:, quarters[s]], words[:, s, :, 1], identity[:])
+        for n in range(2):
+            turn_back(3, halves[n], scores[n], n)
         w_hi_values = tile("w_hi_values", 2 * L, BF16)
         nc.scalar.copy(
             w_hi_values[:].rearrange("m (e p s) -> m e p s", e=2, s=PACK),
             pair_bank[:].bitcast(BF16).rearrange("m (s p e) -> m e p s", s=PACK, e=2),
         )
+
+        for q in range(2):
+            clip(q)
+        for q in range(2):
+            weigh(q)
+        subtract(2)
+        quantize(h_r, E5M2, first)
+        subtract(3)
+        for q in (2, 3):
+            clip(q)
+        for q in (2, 3):
+            weigh(q)
 
         out_rows = {
             "item": out_0.rearrange("(p t) c -> t p c", t=PACK),
@@ -307,31 +311,26 @@ def tile_attend_gmf_hub_vu_kernel(tc, uT, vT, y, us, ts, offs, uoffs, out_0, out
         def store(side, plane):
             nc.sync.dma_start(out_rows[side][plane], windows[side][plane][:])
 
-        early = [gradient((4, 7, 5, 2)[k], "item", k, first) for k in range(PACK)]
+        early = [gradient((4, 6, 5, 2)[k], "item", k, first) for k in range(PACK)]
         for k in range(2):
             empty("scalar", early[k], "item", k, 0)
             scatter("scalar", "item", k, 0)
+        empty("scalar", early[2], "item", 2, 0)
         for q in (2, 3):
             quantize(h_r, E5M2, quarters[q])
         w_hi = operand("w_hi", w_hi_values, HALF, "clipped3")
         quantize(w_hi, E4M3, first)
         closing = [gradient((3, 1)[q - 2], "item", 0, quarters[q])[:, quarters[q]] for q in (2, 3)]
-        late = {k: gradient((4, 0, 7)[k - 1], "item", k, second) for k in (2, 1, 3)}
-        sums["item", 0, 1] = laid.tile([P, HALF], F32, name="closing_sums", align_bytes=64, offset=24 * 1024 + 512)[:]
+        late = {k: gradient((4, 0, 6)[k - 1], "item", k, second) for k in (2, 1, 3)}
         for n in range(2):
             nc.vector.tensor_copy(sums["item", 0, 1][:, quarters[n]], closing[n])
-        empty("vector", late[2], "item", 2, 1)
         scatter("vector", "item", 0, 1)
         store("item", 0)
-        empty("scalar", late[1], "item", 1, 1)
+        for k in (2, 1):
+            empty("scalar", late[k], "item", k, 1)
         scatter("scalar", "item", 1, 1)
         store("item", 1)
         scatter("vector", "item", 2, 1)
-        for k in (2, 3):
-            sums["item", k, 0] = laid.tile(
-                [P, HALF], F32, name="held_sums%d" % k, align_bytes=64, offset=(22 + k) * 1024
-            )[:]
-            empty("vector", early[k], "item", k, 0)
         scatter("vector", "item", 2, 0)
         store("item", 2)
 
@@ -349,7 +348,7 @@ def tile_attend_gmf_hub_vu_kernel(tc, uT, vT, y, us, ts, offs, uoffs, out_0, out
             )
             nc.scalar.copy(
                 h_i_words[:, :, 2 * n : 2 * n + 2, :],
-                turn_planes(h_planes[:, 2 * n * L : 2 * (n + 1) * L], bank_tile((1, 6)[n])).rearrange(
+                turn_planes(h_planes[:, 2 * n * L : 2 * (n + 1) * L], bank_tile((3, 7)[n])).rearrange(
                     "m (a u p) -> m p a u", a=2, u=2
                 ),
             )
@@ -365,6 +364,8 @@ def tile_attend_gmf_hub_vu_kernel(tc, uT, vT, y, us, ts, offs, uoffs, out_0, out
 
         sums["item", 3, 1] = tile("x_r0_codes", HALF, F32)[:]
         empty("scalar", late[3], "item", 3, 1)
+        sums["item", 3, 0] = tile("h_r_codes", HALF, F32)[:]
+        empty("scalar", early[3], "item", 3, 0)
         for n in (1, 0):
             scatter("scalar", "item", 3, n)
         store("item", 3)
@@ -373,7 +374,7 @@ def tile_attend_gmf_hub_vu_kernel(tc, uT, vT, y, us, ts, offs, uoffs, out_0, out
             if k == 0:
                 accs = [gradient(2 + n, "user", k, halves[n]) for n in range(2)]
             else:
-                accs = [gradient((4, 0, 1)[k - 1], "user", k, whole)] * 2
+                accs = [gradient((4, 1, 0)[k - 1], "user", k, whole)] * 2
             for n in range(2):
                 empty(engine, accs[n], "user", k, n)
             for n in range(2):

@@ -220,8 +220,8 @@ def tile_attend_gmf_hub_vu_kernel(tc, uT, vT, y, us, ts, offs, uoffs, out_0, out
                 turn_back(q, halves[n], scores[n], back_banks[n])
         scores = [score(3, halves[n], 5 + n) for n in range(2)]
 
-        def subtract(q):
-            for s in range(PACK):
+        def subtract(q, blocks=range(PACK)):
+            for s in blocks:
                 nc.vector.scalar_tensor_tensor(
                     residual[q][:, quarters[s]],
                     turned[q, s],
@@ -267,8 +267,9 @@ def tile_attend_gmf_hub_vu_kernel(tc, uT, vT, y, us, ts, offs, uoffs, out_0, out
             clip(q)
         for q in range(2):
             weigh(q)
-        subtract(2)
+        subtract(2, range(2))
         quantize(h_r, E5M2, first)
+        subtract(2, range(2, PACK))
         subtract(3)
         for q in (2, 3):
             clip(q)

@@ -92,23 +92,22 @@ def tile_attend_gmf_hub_vu_kernel(tc, uT, vT, y, us, ts, offs, uoffs, out_0, out
 
         u_rows = uT.rearrange("(p t) c -> t p c", t=PACK)
         v_rows = vT.rearrange("(p t) c -> t p c", t=PACK)
-        nc.vector.memset(ts_table[:], 0.0)
-        nc.vector.memset(item_windows[0][:], 0.0)
+        nc.gpsimd.memset(ts_table[:], 0.0)
+        for window in item_windows[:2]:
+            for cols in (slice(0, T // 2 - 1), slice(T // 2 - 1, T)):
+                nc.vector.memset(window[:, cols], 0.0)
         nc.sync.dma_start(u_planes[0][:], u_rows[0])
         nc.sync.dma_start(user_list[:], uoffs)
         nc.sync.dma_start(item_list[:], offs)
         nc.scalar.dma_start(us_cols[:], us.rearrange("b (p s) o -> p (b s o)", s=PACK))
-        nc.sync.dma_start(u_planes[1][:], u_rows[1])
         nc.sync.dma_start(ts_table[0:1, :], ts[0:1, :])
-        for t in range(2, PACK):
+        for t in range(1, PACK):
             nc.sync.dma_start(u_planes[t][:], u_rows[t])
         for t in range(PACK):
             nc.sync.dma_start(v_planes[t][:], v_rows[t])
         nc.sync.dma_start(y_rows[:], y.rearrange("b (p s) i -> p (b s) i", s=PACK))
 
         make_identity(nc, identity[:])
-        nc.gpsimd.memset(item_windows[1][:, 0 : T // 2], 0.0)
-        nc.gpsimd.memset(item_windows[1][:, T // 2 : T], 0.0)
         for window in item_windows[2:] + user_windows:
             nc.gpsimd.memset(window[:], 0.0)
 
@@ -132,13 +131,15 @@ def tile_attend_gmf_hub_vu_kernel(tc, uT, vT, y, us, ts, offs, uoffs, out_0, out
             ALU.mult,
         )
 
-        scale_rows = keep.tile([P, PACK, P], F32, name="scale_rows", align_bytes=64)
-        nc.vector.tensor_tensor(
-            scale_rows[:],
-            ts_rows[:, quarters[0]].unsqueeze(1).to_broadcast([P, PACK, P]),
-            us_cols[:].unsqueeze(2).to_broadcast([P, PACK, P]),
-            ALU.mult,
-        )
+        scale_rows = []
+        for n in range(2):
+            scale_rows.append(keep.tile([P, 2, P], F32, name="scale_rows%d" % n, align_bytes=64))
+            nc.vector.tensor_tensor(
+                scale_rows[n][:],
+                ts_rows[:, quarters[0]].unsqueeze(1).to_broadcast([P, 2, P]),
+                us_cols[:, 2 * n : 2 * n + 2].unsqueeze(2).to_broadcast([P, 2, P]),
+                ALU.mult,
+            )
 
         x_planes = tile("x_planes", PACK * L, BF16)
         x_r = []
@@ -163,18 +164,22 @@ def tile_attend_gmf_hub_vu_kernel(tc, uT, vT, y, us, ts, offs, uoffs, out_0, out
         w_plain = w_planes[:].rearrange("p (t i) -> p i t", t=PACK)
         for t in range(2):
             nc.scalar.activation(w_planes[:, t * L : (t + 1) * L], v_planes[t][:].indirect(item_list[:]), COPY)
-        nc.vector.tensor_copy(w_packed[:, first, 0:2], w_plain[:, first, 0:2])
+        for cols in (second, first):
+            nc.vector.tensor_copy(w_packed[:, cols, 0:2], w_plain[:, cols, 0:2])
+        w_lo = operand("w_lo", tile("w_lo_values", 2 * L, BF16), HALF)
+        turn_features(nc.vector.tensor_copy, w_planes[:, 0 : 2 * L], w_lo[0][:], bank_tile(4))
         for t in range(2, PACK):
             nc.vector.tensor_copy(w_packed[:, first, t], v_planes[t][:].indirect(places(item_list, first)))
             nc.scalar.activation(
                 w_planes[:, t * L + HALF : (t + 1) * L], v_planes[t][:].indirect(places(item_list, second)), COPY
             )
             if t == 2:
-                w_lo = operand("w_lo", tile("w_lo_values", 2 * L, BF16), HALF)
-                turn_features(nc.vector.tensor_copy, w_planes[:, 0 : 2 * L], w_lo[0][:], bank_tile(4))
                 quantize(w_lo, E4M3, first)
-        nc.scalar.copy(w_packed[:, second, :], w_plain[:, second, :])
-        for cols in quarters[:2]:
+            else:
+                for cols in quarters[2:]:
+                    nc.scalar.copy(w_packed[:, cols, 2:4], w_plain[:, cols, 2:4])
+            nc.scalar.copy(w_plain[:, first, t], w_packed[:, first, t])
+        for cols in quarters[:3]:
             quantize(w_d, E4M3, cols)
 
         item_scaled = [tile("item_scaled%d" % q, L, F32) for q in range(PACK)]
@@ -189,22 +194,24 @@ def tile_attend_gmf_hub_vu_kernel(tc, uT, vT, y, us, ts, offs, uoffs, out_0, out
             nc.vector.tensor_tensor(
                 item_scaled[0][:, halves[n]],
                 acc[:, first],
-                scale_rows[:, 2 * n : 2 * n + 2, :].rearrange("p s i -> p (s i)"),
+                scale_rows[n][:].rearrange("p s i -> p (s i)"),
                 ALU.mult,
             )
-        quantize(w_d, E4M3, second)
-        nc.vector.tensor_tensor(
-            residual[0][:].rearrange("p (s i) -> p s i", s=PACK),
-            item_scaled[0][:].rearrange("p (s i) -> p s i", s=PACK),
-            y_rows[:, :, quarters[0]],
-            ALU.subtract,
-        )
+        for n in range(2):
+            nc.vector.tensor_tensor(
+                residual[0][:, halves[n]].rearrange("p (s i) -> p s i", s=2),
+                item_scaled[0][:, halves[n]].rearrange("p (s i) -> p s i", s=2),
+                y_rows[:, 2 * n : 2 * n + 2, quarters[0]],
+                ALU.subtract,
+            )
+        w_last = operand("w_last", w_d[0][:, 3 * L : 4 * L], P, "scale_rows1")
+        quantize(w_last, E4M3, quarters[0])
 
         turned = {}
 
         def score(q, cols, bank):
             acc = bank_tile(bank)
-            product(acc[:, cols], w_d, q, x_d, E4M3, cols)
+            product(acc[:, cols], w_last if q == 3 else w_d, q % 3, x_d, E4M3, cols)
             return acc
 
         def turn_back(q, cols, acc, bank):
@@ -214,11 +221,13 @@ def tile_attend_gmf_hub_vu_kernel(tc, uT, vT, y, us, ts, offs, uoffs, out_0, out
                 nc.tensor.transpose(back[:, quarters[s]], item_scaled[q][:, quarters[s]], identity[:])
                 turned[q, s] = back[:, quarters[s]]
 
-        for q, banks, back_banks in ((1, (2, 3), (4, 7)), (2, (0, 1), (2, 3))):
-            scores = [score(q, halves[n], banks[n]) for n in range(2)]
-            for n in range(2):
-                turn_back(q, halves[n], scores[n], back_banks[n])
-        scores = [score(3, halves[n], 5 + n) for n in range(2)]
+        scores = [score(1, halves[n], 2 + n) for n in range(2)]
+        third = score(2, whole, 5)
+        for n in range(2):
+            turn_back(1, halves[n], scores[n], (4, 7)[n])
+        scores = score(3, whole, 3)
+        for n in range(2):
+            turn_back(2, halves[n], third, n)
 
         def subtract(q, blocks=range(PACK)):
             for s in blocks:
@@ -241,32 +250,26 @@ def tile_attend_gmf_hub_vu_kernel(tc, uT, vT, y, us, ts, offs, uoffs, out_0, out
                 ALU.max,
             )
 
-        def weigh(q):
+        def weigh(q, cols=whole):
             nc.vector.tensor_tensor(
-                h_r[0][:, q * L : (q + 1) * L],
-                clipped[q][:],
-                scale[:, quarters[q], :].rearrange("p i s -> p (i s)"),
+                h_r[0][:, q * L + cols.start : q * L + cols.stop],
+                clipped[q][:, cols],
+                scale[:, quarters[q], :].rearrange("p i s -> p (i s)")[:, cols],
                 ALU.mult,
             )
 
+        clip(0)
         subtract(1)
 
-        pair_bank = bank_tile(7)
-        words = w_d[0][:].bitcast(F32).rearrange("p (m s u) -> p s m u", s=PACK, u=2)
-        for s in range(PACK):
-            nc.tensor.transpose(pair_bank[:, quarters[s]], words[:, s, :, 1], identity[:])
         for n in range(2):
-            turn_back(3, halves[n], scores[n], n)
+            turn_back(3, halves[n], scores, (2, 6)[n])
         w_hi_values = tile("w_hi_values", 2 * L, BF16)
-        nc.scalar.copy(
-            w_hi_values[:].rearrange("m (e p s) -> m e p s", e=2, s=PACK),
-            pair_bank[:].bitcast(BF16).rearrange("m (s p e) -> m e p s", s=PACK, e=2),
-        )
+        turn_features(nc.scalar.copy, w_planes[:, 2 * L : 4 * L], w_hi_values[:], bank_tile(3))
 
-        for q in range(2):
-            clip(q)
-        for q in range(2):
-            weigh(q)
+        weigh(0, first)
+        clip(1)
+        weigh(0, second)
+        weigh(1)
         subtract(2, range(2))
         quantize(h_r, E5M2, first)
         subtract(2, range(2, PACK))
@@ -312,7 +315,7 @@ def tile_attend_gmf_hub_vu_kernel(tc, uT, vT, y, us, ts, offs, uoffs, out_0, out
         def store(side, plane):
             nc.sync.dma_start(out_rows[side][plane], windows[side][plane][:])
 
-        early = [gradient((4, 6, 5, 2)[k], "item", k, first) for k in range(PACK)]
+        early = [gradient((5, 7, 4, 0)[k], "item", k, first) for k in range(PACK)]
         for k in range(2):
             empty("scalar", early[k], "item", k, 0)
             scatter("scalar", "item", k, 0)
@@ -322,7 +325,7 @@ def tile_attend_gmf_hub_vu_kernel(tc, uT, vT, y, us, ts, offs, uoffs, out_0, out
         w_hi = operand("w_hi", w_hi_values, HALF, "clipped3")
         quantize(w_hi, E4M3, first)
         closing = [gradient((3, 1)[q - 2], "item", 0, quarters[q])[:, quarters[q]] for q in (2, 3)]
-        late = {k: gradient((4, 0, 6)[k - 1], "item", k, second) for k in (2, 1, 3)}
+        late = {k: gradient((6, 2, 5)[k - 1], "item", k, second) for k in (2, 1, 3)}
         for n in range(2):
             nc.vector.tensor_copy(sums["item", 0, 1][:, quarters[n]], closing[n])
         scatter("vector", "item", 0, 1)
@@ -349,7 +352,7 @@ def tile_attend_gmf_hub_vu_kernel(tc, uT, vT, y, us, ts, offs, uoffs, out_0, out
             )
             nc.scalar.copy(
                 h_i_words[:, :, 2 * n : 2 * n + 2, :],
-                turn_planes(h_planes[:, 2 * n * L : 2 * (n + 1) * L], bank_tile((3, 7)[n])).rearrange(
+                turn_planes(h_planes[:, 2 * n * L : 2 * (n + 1) * L], bank_tile((7, 3)[n])).rearrange(
                     "m (a u p) -> m p a u", a=2, u=2
                 ),
             )
@@ -373,9 +376,9 @@ def tile_attend_gmf_hub_vu_kernel(tc, uT, vT, y, us, ts, offs, uoffs, out_0, out
         for k in range(PACK):
             engine = ("vector", "scalar")[k % 2]
             if k == 0:
-                accs = [gradient(2 + n, "user", k, halves[n]) for n in range(2)]
+                accs = [gradient(1 + n, "user", k, halves[n]) for n in range(2)]
             else:
-                accs = [gradient((4, 1, 0)[k - 1], "user", k, whole)] * 2
+                accs = [gradient((4, 6, 0)[k - 1], "user", k, whole)] * 2
             for n in range(2):
                 empty(engine, accs[n], "user", k, n)
             for n in range(2):

@@ -242,8 +242,8 @@ def tile_attend_gmf_hub_vu_kernel(tc, uT, vT, y, us, ts, offs, uoffs, out_0, out
 
         def clip(q):
             nc.vector.tensor_scalar(
-                clipped[q][:].rearrange("p (i s) -> p i s", s=PACK),
-                residual[q][:].rearrange("p (s i) -> p i s", s=PACK),
+                clipped[q][:].rearrange("p (c j s) -> p c s j", j=2, s=PACK),
+                residual[q][:].rearrange("p (s c j) -> p c s j", j=2, s=PACK),
                 1.0,
                 -1.0,
                 ALU.min,

@@ -46,9 +46,9 @@ def tile_attend_gmf_hub_vu_kernel(tc, uT, vT, y, us, ts, offs, uoffs, out_0, out
         v_planes = [tile("v_plane%d" % t, T, F32) for t in range(PACK)]
         ts_table = tile("ts_table", T, F32)
         us_cols = tile("us_cols", PACK, F32)
-        y_rows = keep.tile([P, PACK, L], F32, name="y_rows", align_bytes=64)
+        y_rows = [keep.tile([P, PACK, HALF], F32, name="y_rows%d" % n, align_bytes=64) for n in range(2)]
         item_windows = [tile("item_window%d" % k, T, F32) for k in range(PACK)]
-        user_windows = [tile("user_window%d" % k, T, F32) for k in range(1)]
+        user_windows = [tile("user_window%d" % k, T, F32) for k in range(2)]
         identity = tile("identity", P, F32)
 
         def places(offsets, cols):
@@ -84,10 +84,16 @@ def tile_attend_gmf_hub_vu_kernel(tc, uT, vT, y, us, ts, offs, uoffs, out_0, out
                     nc.tensor.transpose(bank[:, quarters[2 * a + u]], words[:, a, u, :], identity[:])
             return bank[:]
 
-        def turn_features(copy, planes, target, bank):
+        def turn_plane(plane, bank):
+            words = plane.bitcast(F32).rearrange("p (m u) -> p u m", u=2)
+            for u in range(2):
+                nc.tensor.transpose(bank[:, quarters[u]], words[:, u, :], identity[:])
+            return bank
+
+        def pack_turned(copy, target, bank):
             copy(
-                target.bitcast(F32).rearrange("m (a p u) -> m a p u", a=2, u=2),
-                turn_planes(planes, bank).rearrange("m (a u p) -> m a p u", a=2, u=2),
+                target.bitcast(F32).rearrange("m (p u) -> m p u", u=2),
+                bank[:, first].rearrange("m (u p) -> m p u", u=2),
             )
 
         u_rows = uT.rearrange("(p t) c -> t p c", t=PACK)
@@ -105,7 +111,8 @@ def tile_attend_gmf_hub_vu_kernel(tc, uT, vT, y, us, ts, offs, uoffs, out_0, out
             nc.sync.dma_start(u_planes[t][:], u_rows[t])
         for t in range(PACK):
             nc.sync.dma_start(v_planes[t][:], v_rows[t])
-        nc.sync.dma_start(y_rows[:], y.rearrange("b (p s) i -> p (b s) i", s=PACK))
+        for n in range(2):
+            nc.sync.dma_start(y_rows[n][:], y.rearrange("b (p s) i -> p (b s) i", s=PACK)[:, :, halves[n]])
 
         make_identity(nc, identity[:])
         for window in item_windows[2:] + user_windows:
@@ -136,61 +143,67 @@ def tile_attend_gmf_hub_vu_kernel(tc, uT, vT, y, us, ts, offs, uoffs, out_0, out
             scale_rows.append(keep.tile([P, 2, P], F32, name="scale_rows%d" % n, align_bytes=64))
             nc.vector.tensor_tensor(
                 scale_rows[n][:],
-                ts_rows[:, quarters[0]].unsqueeze(1).to_broadcast([P, 2, P]),
+                ts_spread[:, quarters[0]].unsqueeze(1).to_broadcast([P, 2, P]),
                 us_cols[:, 2 * n : 2 * n + 2].unsqueeze(2).to_broadcast([P, 2, P]),
                 ALU.mult,
             )
 
         x_planes = tile("x_planes", PACK * L, BF16)
         x_r = []
-        for t in range(PACK):
-            nc.scalar.activation(x_planes[:, t * L : (t + 1) * L], u_planes[t][:].indirect(user_list[:]), COPY)
         x_d = operand("x_d", laid.tile([P, PACK * L], BF16, name="x_d_values", align_bytes=64, offset=0), L)
-        nc.vector.tensor_copy(
-            x_d[0][:].rearrange("p (s m t) -> p s m t", s=PACK, t=PACK),
-            x_planes[:].rearrange("p (t m s) -> p s m t", t=PACK, s=PACK),
-        )
-        quantize(x_d, E4M3, whole)
-        for n in range(2):
-            values = tile("x_r%d_values" % n, 2 * L, BF16)
-            turn_features(nc.vector.tensor_copy, x_planes[:, 2 * n * L : 2 * (n + 1) * L], values[:], bank_tile(4 + n))
-            for a in range(2):
-                x_r.append(operand("x_r%d" % (2 * n + a), values[:, a * L : (a + 1) * L], P))
-                quantize(x_r[-1], E4M3, quarters[0])
+        for t in range(PACK):
+            plane = x_planes[:, t * L : (t + 1) * L]
+            nc.scalar.activation(plane, u_planes[t][:].indirect(user_list[:]), COPY)
+            if t == PACK - 1:
+                nc.vector.tensor_copy(
+                    x_d[0][:].rearrange("p (s m t) -> p s m t", s=PACK, t=PACK),
+                    x_planes[:].rearrange("p (t m s) -> p s m t", t=PACK, s=PACK),
+                )
+            x_r.append(operand("x_r%d" % t, tile("x_r%d_values" % t, L, BF16), P))
+            pack_turned(nc.vector.tensor_copy, x_r[t][0][:], turn_plane(plane, bank_tile((4, 4, 5, 4)[t])))
+            if t == PACK - 1:
+                quantize(x_d, E4M3, whole)
+            quantize(x_r[t], E4M3, quarters[0])
 
-        w_d = operand("w_d", laid.tile([P, PACK * L], BF16, name="w_d_values", align_bytes=64, offset=4 * 1024), L)
-        w_packed = w_d[0][:].rearrange("p (i t) -> p i t", t=PACK)
-        w_planes = tile("w_planes", PACK * L, BF16)
-        w_plain = w_planes[:].rearrange("p (t i) -> p i t", t=PACK)
+        w_values = laid.tile([P, PACK * L], BF16, name="w_d_values", align_bytes=64, offset=4 * 1024)
+        w_packed = w_values[:].rearrange("p (i t) -> p i t", t=PACK)
+        w_planes = tile("w_planes", 2 * L, BF16)
+        w_i = [operand("w_i%d" % t, tile("w_i%d_values" % t, L, BF16), P) for t in range(2)]
+        banks = []
         for t in range(2):
             nc.scalar.activation(w_planes[:, t * L : (t + 1) * L], v_planes[t][:].indirect(item_list[:]), COPY)
-        for cols in (second, first):
-            nc.vector.tensor_copy(w_packed[:, cols, 0:2], w_plain[:, cols, 0:2])
-        w_lo = operand("w_lo", tile("w_lo_values", 2 * L, BF16), HALF)
-        turn_features(nc.vector.tensor_copy, w_planes[:, 0 : 2 * L], w_lo[0][:], bank_tile(4))
-        for t in range(2, PACK):
-            nc.vector.tensor_copy(w_packed[:, first, t], v_planes[t][:].indirect(places(item_list, first)))
-            nc.scalar.activation(
-                w_planes[:, t * L + HALF : (t + 1) * L], v_planes[t][:].indirect(places(item_list, second)), COPY
-            )
-            if t == 2:
-                quantize(w_lo, E4M3, first)
-            else:
-                for cols in quarters[2:]:
-                    nc.scalar.copy(w_packed[:, cols, 2:4], w_plain[:, cols, 2:4])
-            nc.scalar.copy(w_plain[:, first, t], w_packed[:, first, t])
-        for cols in quarters[:3]:
-            quantize(w_d, E4M3, cols)
+            banks.append(turn_plane(w_planes[:, t * L : (t + 1) * L], bank_tile(4 + t)))
+        pack_turned(nc.vector.tensor_copy, w_i[0][0][:], banks[0])
+        nc.vector.tensor_copy(w_packed[:, :, 0:2], w_planes[:].rearrange("p (t i) -> p i t", t=2))
+        nc.scalar.activation(w_packed[:, :, 2], v_planes[2][:].indirect(item_list[:]), COPY)
+        pack_turned(nc.vector.tensor_copy, w_i[1][0][:], banks[1])
+        for t in range(2):
+            quantize(w_i[t], E4M3, quarters[0])
+        third_plane = tile("w_planes", L, BF16)
+        nc.vector.tensor_copy(third_plane[:], w_packed[:, :, 2])
+        for cols in quarters:
+            nc.scalar.activation(w_packed[:, cols, 3], v_planes[3][:].indirect(places(item_list, cols)), COPY)
+
+        w_d = {}
+
+        def quantize_items(q, codes_buffer=None):
+            w_d[q] = operand("w_d%d" % q, w_values[:, q * L : (q + 1) * L], P, codes_buffer)
+            quantize(w_d[q], E4M3, quarters[0])
 
         item_scaled = [tile("item_scaled%d" % q, L, F32) for q in range(PACK)]
         residual = [tile("residual%d" % q, L, F32) for q in range(PACK)]
         clipped = [tile("clipped%d" % q, L, F32) for q in range(PACK)]
         h_r = operand("h_r", tile("h_r_values", PACK * L, BF16), L)
 
+        def targets(q, blocks):
+            return y_rows[q // 2][:, blocks, quarters[q % 2]]
+
+        for q in range(3):
+            quantize_items(q)
         for n in range(2):
             acc = bank_tile(n)
             for e in range(2):
-                product(acc[:, quarters[e]], x_d, 2 * n + e, w_d, E4M3, quarters[0])
+                product(acc[:, quarters[e]], x_d, 2 * n + e, w_d[0], E4M3, quarters[0])
             nc.vector.tensor_tensor(
                 item_scaled[0][:, halves[n]],
                 acc[:, first],
@@ -201,17 +214,17 @@ def tile_attend_gmf_hub_vu_kernel(tc, uT, vT, y, us, ts, offs, uoffs, out_0, out
             nc.vector.tensor_tensor(
                 residual[0][:, halves[n]].rearrange("p (s i) -> p s i", s=2),
                 item_scaled[0][:, halves[n]].rearrange("p (s i) -> p s i", s=2),
-                y_rows[:, 2 * n : 2 * n + 2, quarters[0]],
+                targets(0, slice(2 * n, 2 * n + 2)),
                 ALU.subtract,
             )
-        w_last = operand("w_last", w_d[0][:, 3 * L : 4 * L], P, "scale_rows1")
-        quantize(w_last, E4M3, quarters[0])
+            if n == 0:
+                quantize_items(3, "scale_rows1")
 
         turned = {}
 
         def score(q, cols, bank):
             acc = bank_tile(bank)
-            product(acc[:, cols], w_last if q == 3 else w_d, q % 3, x_d, E4M3, cols)
+            product(acc[:, cols], w_d[q], 0, x_d, E4M3, cols)
             return acc
 
         def turn_back(q, cols, acc, bank):
@@ -222,12 +235,19 @@ def tile_attend_gmf_hub_vu_kernel(tc, uT, vT, y, us, ts, offs, uoffs, out_0, out
                 turned[q, s] = back[:, quarters[s]]
 
         scores = [score(1, halves[n], 2 + n) for n in range(2)]
-        third = score(2, whole, 5)
+        scores.append(score(2, whole, 6))
         for n in range(2):
-            turn_back(1, halves[n], scores[n], (4, 7)[n])
-        scores = score(3, whole, 3)
+            turn_back(1, halves[n], scores[n], 4 + n)
+        scores.append(score(3, whole, 3))
         for n in range(2):
-            turn_back(2, halves[n], third, n)
+            turn_back(2, halves[n], scores[2], n)
+        for n in range(2):
+            turn_back(3, halves[n], scores[3], (7, 2)[n])
+        last_plane = tile("scale_rows1", L, BF16)
+        nc.scalar.copy(last_plane[:], w_packed[:, :, 3])
+        w_hi_values = tile("w_hi_values", 2 * L, BF16)
+        for n, plane in enumerate((third_plane, last_plane)):
+            pack_turned(nc.scalar.copy, w_hi_values[:, n * L : (n + 1) * L], turn_plane(plane[:], bank_tile((3, 6)[n])))
 
         def subtract(q, blocks=range(PACK)):
             for s in blocks:
@@ -235,7 +255,7 @@ def tile_attend_gmf_hub_vu_kernel(tc, uT, vT, y, us, ts, offs, uoffs, out_0, out
                     residual[q][:, quarters[s]],
                     turned[q, s],
                     us_cols[:, s : s + 1],
-                    y_rows[:, s, quarters[q]],
+                    targets(q, s),
                     ALU.mult,
                     ALU.subtract,
                 )
@@ -258,14 +278,9 @@ def tile_attend_gmf_hub_vu_kernel(tc, uT, vT, y, us, ts, offs, uoffs, out_0, out
                 ALU.mult,
             )
 
+        subtract(1, range(2))
         clip(0)
-        subtract(1)
-
-        for n in range(2):
-            turn_back(3, halves[n], scores, (2, 6)[n])
-        w_hi_values = tile("w_hi_values", 2 * L, BF16)
-        turn_features(nc.scalar.copy, w_planes[:, 2 * L : 4 * L], w_hi_values[:], bank_tile(3))
-
+        subtract(1, range(2, PACK))
         weigh(0, first)
         clip(1)
         weigh(0, second)
@@ -278,6 +293,10 @@ def tile_attend_gmf_hub_vu_kernel(tc, uT, vT, y, us, ts, offs, uoffs, out_0, out
             clip(q)
         for q in (2, 3):
             weigh(q)
+        for q in (2, 3):
+            quantize(h_r, E5M2, quarters[q])
+        w_hi = operand("w_hi", w_hi_values, HALF, "clipped3")
+        quantize(w_hi, E4M3, first)
 
         out_rows = {
             "item": out_0.rearrange("(p t) c -> t p c", t=PACK),
@@ -296,7 +315,7 @@ def tile_attend_gmf_hub_vu_kernel(tc, uT, vT, y, us, ts, offs, uoffs, out_0, out
             if side == "item":
                 product(acc[:, cols], x_r[plane], 0, h_r, E5M2, cols)
             else:
-                product(acc[:, cols], (w_lo, w_hi)[plane // 2], plane % 2, h_i, E5M2, cols)
+                product(acc[:, cols], (w_i[0], w_i[1], w_hi, w_hi)[plane], plane // 2 * (plane % 2), h_i, E5M2, cols)
             return acc
 
         def empty(engine, acc, side, plane, n):
@@ -315,27 +334,24 @@ def tile_attend_gmf_hub_vu_kernel(tc, uT, vT, y, us, ts, offs, uoffs, out_0, out
         def store(side, plane):
             nc.sync.dma_start(out_rows[side][plane], windows[side][plane][:])
 
-        early = [gradient((5, 7, 4, 0)[k], "item", k, first) for k in range(PACK)]
+        early = [gradient((4, 5, 6, 0)[k], "item", k, first) for k in range(PACK)]
         for k in range(2):
             empty("scalar", early[k], "item", k, 0)
             scatter("scalar", "item", k, 0)
-        empty("scalar", early[2], "item", 2, 0)
-        for q in (2, 3):
-            quantize(h_r, E5M2, quarters[q])
-        w_hi = operand("w_hi", w_hi_values, HALF, "clipped3")
-        quantize(w_hi, E4M3, first)
-        closing = [gradient((3, 1)[q - 2], "item", 0, quarters[q])[:, quarters[q]] for q in (2, 3)]
-        late = {k: gradient((6, 2, 5)[k - 1], "item", k, second) for k in (2, 1, 3)}
+        closing = [gradient((1, 7)[q - 2], "item", 0, quarters[q])[:, quarters[q]] for q in (2, 3)]
+        late = {k: gradient((2, 3, 4)[k - 1], "item", k, second) for k in (1, 2, 3)}
         for n in range(2):
             nc.vector.tensor_copy(sums["item", 0, 1][:, quarters[n]], closing[n])
+        sums["item", 2, 0] = tile("x_r0_scales", HALF, F32)[:]
+        empty("vector", early[2], "item", 2, 0)
         scatter("vector", "item", 0, 1)
         store("item", 0)
-        for k in (2, 1):
+        for k in (1, 2):
             empty("scalar", late[k], "item", k, 1)
         scatter("scalar", "item", 1, 1)
         store("item", 1)
-        scatter("vector", "item", 2, 1)
-        scatter("vector", "item", 2, 0)
+        for n in range(2):
+            scatter("vector", "item", 2, n)
         store("item", 2)
 
         h_planes = tile("x_r0_codes", PACK * L, BF16)
@@ -352,19 +368,17 @@ def tile_attend_gmf_hub_vu_kernel(tc, uT, vT, y, us, ts, offs, uoffs, out_0, out
             )
             nc.scalar.copy(
                 h_i_words[:, :, 2 * n : 2 * n + 2, :],
-                turn_planes(h_planes[:, 2 * n * L : 2 * (n + 1) * L], bank_tile((7, 3)[n])).rearrange(
+                turn_planes(h_planes[:, 2 * n * L : 2 * (n + 1) * L], bank_tile((5, 1)[n])).rearrange(
                     "m (a u p) -> m p a u", a=2, u=2
                 ),
             )
         for cols in halves:
             quantize(h_i, E5M2, cols)
-        user_windows.append(tile("h_r_values", T, F32))
         for k in (2, 3):
             user_windows.append(
                 laid.tile([P, T], F32, name="user_window%d" % k, align_bytes=64, offset=(k - 1) * 8 * 1024)
             )
-        for window in user_windows[1:]:
-            nc.gpsimd.memset(window[:], 0.0)
+            nc.gpsimd.memset(user_windows[k][:], 0.0)
 
         sums["item", 3, 1] = tile("x_r0_codes", HALF, F32)[:]
         empty("scalar", late[3], "item", 3, 1)
@@ -376,9 +390,9 @@ def tile_attend_gmf_hub_vu_kernel(tc, uT, vT, y, us, ts, offs, uoffs, out_0, out
         for k in range(PACK):
             engine = ("vector", "scalar")[k % 2]
             if k == 0:
-                accs = [gradient(1 + n, "user", k, halves[n]) for n in range(2)]
+                accs = [gradient(7 - n, "user", k, halves[n]) for n in range(2)]
             else:
-                accs = [gradient((4, 6, 0)[k - 1], "user", k, whole)] * 2
+                accs = [gradient((2, 3, 0)[k - 1], "user", k, whole)] * 2
             for n in range(2):
                 empty(engine, accs[n], "user", k, n)
             for n in range(2):

@@ -175,19 +175,23 @@ def tile_attend_gmf_hub_vu_kernel(tc, uT, vT, y, us, ts, offs, uoffs, out_0, out
             banks.append(turn_plane(w_planes[:, t * L : (t + 1) * L], bank_tile(4 + t)))
         pack_turned(nc.vector.tensor_copy, w_i[0][0][:], banks[0])
         nc.vector.tensor_copy(w_packed[:, :, 0:2], w_planes[:].rearrange("p (t i) -> p i t", t=2))
-        nc.scalar.activation(w_packed[:, :, 2], v_planes[2][:].indirect(item_list[:]), COPY)
+        for cols in halves:
+            nc.scalar.activation(w_packed[:, cols, 2], v_planes[2][:].indirect(places(item_list, cols)), COPY)
         pack_turned(nc.vector.tensor_copy, w_i[1][0][:], banks[1])
         for t in range(2):
             quantize(w_i[t], E4M3, quarters[0])
         third_plane = tile("w_planes", L, BF16)
-        nc.vector.tensor_copy(third_plane[:], w_packed[:, :, 2])
-        for cols in quarters:
+        for cols in halves:
+            nc.vector.tensor_copy(third_plane[:, cols], w_packed[:, cols, 2])
+        last_quarter = tile("w_i1_values", P, BF16)
+        nc.vector.tensor_copy(last_quarter[:], v_planes[3][:].indirect(places(item_list, quarters[2])))
+        for cols in (quarters[0], quarters[1], quarters[3]):
             nc.scalar.activation(w_packed[:, cols, 3], v_planes[3][:].indirect(places(item_list, cols)), COPY)
 
         w_d = {}
 
-        def quantize_items(q, codes_buffer=None):
-            w_d[q] = operand("w_d%d" % q, w_values[:, q * L : (q + 1) * L], P, codes_buffer)
+        def quantize_items(q):
+            w_d[q] = operand("w_d%d" % q, w_values[:, q * L : (q + 1) * L], P)
             quantize(w_d[q], E4M3, quarters[0])
 
         item_scaled = [tile("item_scaled%d" % q, L, F32) for q in range(PACK)]
@@ -198,7 +202,9 @@ def tile_attend_gmf_hub_vu_kernel(tc, uT, vT, y, us, ts, offs, uoffs, out_0, out
         def targets(q, blocks):
             return y_rows[q // 2][:, blocks, quarters[q % 2]]
 
-        for q in range(3):
+        quantize_items(0)
+        nc.vector.tensor_copy(w_packed[:, quarters[2], 3], last_quarter[:])
+        for q in range(1, PACK):
             quantize_items(q)
         for n in range(2):
             acc = bank_tile(n)
@@ -217,8 +223,6 @@ def tile_attend_gmf_hub_vu_kernel(tc, uT, vT, y, us, ts, offs, uoffs, out_0, out
                 targets(0, slice(2 * n, 2 * n + 2)),
                 ALU.subtract,
             )
-            if n == 0:
-                quantize_items(3, "scale_rows1")
 
         turned = {}
 
@@ -243,7 +247,7 @@ def tile_attend_gmf_hub_vu_kernel(tc, uT, vT, y, us, ts, offs, uoffs, out_0, out
             turn_back(2, halves[n], scores[2], n)
         for n in range(2):
             turn_back(3, halves[n], scores[3], (7, 2)[n])
-        last_plane = tile("scale_rows1", L, BF16)
+        last_plane = tile("w_d3_codes", L, BF16)
         nc.scalar.copy(last_plane[:], w_packed[:, :, 3])
         w_hi_values = tile("w_hi_values", 2 * L, BF16)
         for n, plane in enumerate((third_plane, last_plane)):
@@ -342,7 +346,9 @@ def tile_attend_gmf_hub_vu_kernel(tc, uT, vT, y, us, ts, offs, uoffs, out_0, out
         late = {k: gradient((2, 3, 4)[k - 1], "item", k, second) for k in (1, 2, 3)}
         for n in range(2):
             nc.vector.tensor_copy(sums["item", 0, 1][:, quarters[n]], closing[n])
-        sums["item", 2, 0] = tile("x_r0_scales", HALF, F32)[:]
+        third_sums = tile("x_r0_scales", L, F32)
+        for n in range(2):
+            sums["item", 2, n] = third_sums[:, halves[n]]
         empty("vector", early[2], "item", 2, 0)
         scatter("vector", "item", 0, 1)
         store("item", 0)
@@ -350,9 +356,11 @@ def tile_attend_gmf_hub_vu_kernel(tc, uT, vT, y, us, ts, offs, uoffs, out_0, out
             empty("scalar", late[k], "item", k, 1)
         scatter("scalar", "item", 1, 1)
         store("item", 1)
-        for n in range(2):
-            scatter("vector", "item", 2, n)
+        nc.vector.tensor_copy(item_windows[2][:].indirect(item_list[:]), third_sums[:])
         store("item", 2)
+        last_sums = tile("h_r_codes", L, F32)
+        nc.scalar.copy(last_sums[:, first], early[3][:, first])
+        nc.scalar.copy(last_sums[:, second], late[3][:, second])
 
         h_planes = tile("x_r0_codes", PACK * L, BF16)
         h_i = operand("h_i", laid.tile([P, PACK * L], BF16, name="h_i_values", align_bytes=64, offset=14 * 1024), L)
@@ -372,6 +380,8 @@ def tile_attend_gmf_hub_vu_kernel(tc, uT, vT, y, us, ts, offs, uoffs, out_0, out
                     "m (a u p) -> m p a u", a=2, u=2
                 ),
             )
+        ones = tile("x_r0_codes", 1, F32)
+        nc.gpsimd.memset(ones[:], 1.0)
         for cols in halves:
             quantize(h_i, E5M2, cols)
         for k in (2, 3):
@@ -380,12 +390,7 @@ def tile_attend_gmf_hub_vu_kernel(tc, uT, vT, y, us, ts, offs, uoffs, out_0, out
             )
             nc.gpsimd.memset(user_windows[k][:], 0.0)
 
-        sums["item", 3, 1] = tile("x_r0_codes", HALF, F32)[:]
-        empty("scalar", late[3], "item", 3, 1)
-        sums["item", 3, 0] = tile("h_r_codes", HALF, F32)[:]
-        empty("scalar", early[3], "item", 3, 0)
-        for n in (1, 0):
-            scatter("scalar", "item", 3, n)
+        nc.scalar.activation(item_windows[3][:].indirect(item_list[:]), last_sums[:], COPY, scale=ones[:])
         store("item", 3)
         for k in range(PACK):
             engine = ("vector", "scalar")[k % 2]

@@ -196,7 +196,7 @@ def tile_attend_gmf_hub_vu_kernel(tc, uT, vT, y, us, ts, offs, uoffs, out_0, out
 
         item_scaled = [tile("item_scaled%d" % q, L, F32) for q in range(PACK)]
         residual = [tile("residual%d" % q, L, F32) for q in range(PACK)]
-        clipped = [tile("clipped%d" % q, L, F32) for q in range(PACK)]
+        clipped = {}
         h_r = operand("h_r", tile("h_r_values", PACK * L, BF16), L)
 
         def targets(q, blocks):
@@ -265,6 +265,7 @@ def tile_attend_gmf_hub_vu_kernel(tc, uT, vT, y, us, ts, offs, uoffs, out_0, out
                 )
 
         def clip(q):
+            clipped[q] = tile("clipped%d" % (0, 1, 1, 3)[q], L, F32)
             nc.vector.tensor_scalar(
                 clipped[q][:].rearrange("p (c j s) -> p c s j", j=2, s=PACK),
                 residual[q][:].rearrange("p (s c j) -> p c s j", j=2, s=PACK),
@@ -274,8 +275,8 @@ def tile_attend_gmf_hub_vu_kernel(tc, uT, vT, y, us, ts, offs, uoffs, out_0, out
                 ALU.max,
             )
 
-        def weigh(q, cols=whole):
-            nc.vector.tensor_tensor(
+        def weigh(q, cols=whole, engine=nc.vector):
+            engine.tensor_tensor(
                 h_r[0][:, q * L + cols.start : q * L + cols.stop],
                 clipped[q][:, cols],
                 scale[:, quarters[q], :].rearrange("p i s -> p (i s)")[:, cols],
@@ -285,14 +286,14 @@ def tile_attend_gmf_hub_vu_kernel(tc, uT, vT, y, us, ts, offs, uoffs, out_0, out
         subtract(1, range(2))
         clip(0)
         subtract(1, range(2, PACK))
-        weigh(0, first)
+        weigh(0)
         clip(1)
-        weigh(0, second)
-        weigh(1)
-        subtract(2, range(2))
-        quantize(h_r, E5M2, first)
-        subtract(2, range(2, PACK))
-        subtract(3)
+        quantize(h_r, E5M2, quarters[0])
+        weigh(1, quarters[0])
+        weigh(1, slice(P, L), nc.gpsimd)
+        for q in (2, 3):
+            subtract(q)
+        quantize(h_r, E5M2, quarters[1])
         for q in (2, 3):
             clip(q)
         for q in (2, 3):
@@ -338,12 +339,14 @@ def tile_attend_gmf_hub_vu_kernel(tc, uT, vT, y, us, ts, offs, uoffs, out_0, out
         def store(side, plane):
             nc.sync.dma_start(out_rows[side][plane], windows[side][plane][:])
 
-        early = [gradient((4, 5, 6, 0)[k], "item", k, first) for k in range(PACK)]
-        for k in range(2):
-            empty("scalar", early[k], "item", k, 0)
-            scatter("scalar", "item", k, 0)
-        closing = [gradient((1, 7)[q - 2], "item", 0, quarters[q])[:, quarters[q]] for q in (2, 3)]
-        late = {k: gradient((2, 3, 4)[k - 1], "item", k, second) for k in (1, 2, 3)}
+        for q in range(2):
+            nc.scalar.copy(sums["item", 0, 0][:, quarters[q]], gradient(4 + q, "item", 0, quarters[q])[:, quarters[q]])
+        early = {k: gradient((1, 6, 0)[k - 1], "item", k, first) for k in (1, 2, 3)}
+        scatter("scalar", "item", 0, 0)
+        empty("scalar", early[1], "item", 1, 0)
+        scatter("scalar", "item", 1, 0)
+        closing = [gradient((4, 7)[q - 2], "item", 0, quarters[q])[:, quarters[q]] for q in (2, 3)]
+        late = {k: gradient((2, 3, 5)[k - 1], "item", k, second) for k in (1, 2, 3)}
         for n in range(2):
             nc.vector.tensor_copy(sums["item", 0, 1][:, quarters[n]], closing[n])
         third_sums = tile("x_r0_scales", L, F32)
@@ -376,7 +379,7 @@ def tile_attend_gmf_hub_vu_kernel(tc, uT, vT, y, us, ts, offs, uoffs, out_0, out
             )
             nc.scalar.copy(
                 h_i_words[:, :, 2 * n : 2 * n + 2, :],
-                turn_planes(h_planes[:, 2 * n * L : 2 * (n + 1) * L], bank_tile((5, 1)[n])).rearrange(
+                turn_planes(h_planes[:, 2 * n * L : 2 * (n + 1) * L], bank_tile((1, 4)[n])).rearrange(
                     "m (a u p) -> m p a u", a=2, u=2
                 ),
             )

@@ -300,8 +300,6 @@ def tile_attend_gmf_hub_vu_kernel(tc, uT, vT, y, us, ts, offs, uoffs, out_0, out
             weigh(q)
         for q in (2, 3):
             quantize(h_r, E5M2, quarters[q])
-        w_hi = operand("w_hi", w_hi_values, HALF, "clipped3")
-        quantize(w_hi, E4M3, first)
 
         out_rows = {
             "item": out_0.rearrange("(p t) c -> t p c", t=PACK),
@@ -315,12 +313,14 @@ def tile_attend_gmf_hub_vu_kernel(tc, uT, vT, y, us, ts, offs, uoffs, out_0, out
             for k in range(2 * PACK):
                 sums[side, k // 2, k % 2] = row[:, k * HALF : (k + 1) * HALF]
 
+        w_planes_i = list(w_i)
+
         def gradient(bank, side, plane, cols):
             acc = bank_tile(bank)
             if side == "item":
                 product(acc[:, cols], x_r[plane], 0, h_r, E5M2, cols)
             else:
-                product(acc[:, cols], (w_i[0], w_i[1], w_hi, w_hi)[plane], plane // 2 * (plane % 2), h_i, E5M2, cols)
+                product(acc[:, cols], w_planes_i[min(plane, 2)], plane // 2 * (plane % 2), h_i, E5M2, cols)
             return acc
 
         def empty(engine, acc, side, plane, n):
@@ -345,8 +345,10 @@ def tile_attend_gmf_hub_vu_kernel(tc, uT, vT, y, us, ts, offs, uoffs, out_0, out
         scatter("scalar", "item", 0, 0)
         empty("scalar", early[1], "item", 1, 0)
         scatter("scalar", "item", 1, 0)
+        last_sums = tile("clipped3", L, F32)
+        nc.vector.tensor_copy(last_sums[:, first], early[3][:, first])
         closing = [gradient((4, 7)[q - 2], "item", 0, quarters[q])[:, quarters[q]] for q in (2, 3)]
-        late = {k: gradient((2, 3, 5)[k - 1], "item", k, second) for k in (1, 2, 3)}
+        late = {k: gradient((2, 3, 5)[k - 1], "item", k, second) for k in (2, 1, 3)}
         for n in range(2):
             nc.vector.tensor_copy(sums["item", 0, 1][:, quarters[n]], closing[n])
         third_sums = tile("x_r0_scales", L, F32)
@@ -355,18 +357,16 @@ def tile_attend_gmf_hub_vu_kernel(tc, uT, vT, y, us, ts, offs, uoffs, out_0, out
         empty("vector", early[2], "item", 2, 0)
         scatter("vector", "item", 0, 1)
         store("item", 0)
-        for k in (1, 2):
+        for k in (2, 1):
             empty("scalar", late[k], "item", k, 1)
         scatter("scalar", "item", 1, 1)
         store("item", 1)
         nc.vector.tensor_copy(item_windows[2][:].indirect(item_list[:]), third_sums[:])
         store("item", 2)
-        last_sums = tile("h_r_codes", L, F32)
-        nc.scalar.copy(last_sums[:, first], early[3][:, first])
         nc.scalar.copy(last_sums[:, second], late[3][:, second])
 
         h_planes = tile("x_r0_codes", PACK * L, BF16)
-        h_i = operand("h_i", laid.tile([P, PACK * L], BF16, name="h_i_values", align_bytes=64, offset=14 * 1024), L)
+        h_i = operand("h_i", laid.tile([P, PACK * L], BF16, name="h_i_values", align_bytes=64, offset=8 * 1024), L)
         h_i_words = h_i[0][:].bitcast(F32).rearrange("m (p s u) -> m p s u", s=PACK, u=2)
         for n in range(2):
             nc.gpsimd.tensor_scalar(
@@ -387,10 +387,9 @@ def tile_attend_gmf_hub_vu_kernel(tc, uT, vT, y, us, ts, offs, uoffs, out_0, out
         nc.gpsimd.memset(ones[:], 1.0)
         for cols in halves:
             quantize(h_i, E5M2, cols)
+        user_windows.append(tile("h_r_values", T, F32))
+        user_windows.append(laid.tile([P, T], F32, name="user_window3", align_bytes=64, offset=8 * 1024))
         for k in (2, 3):
-            user_windows.append(
-                laid.tile([P, T], F32, name="user_window%d" % k, align_bytes=64, offset=(k - 1) * 8 * 1024)
-            )
             nc.gpsimd.memset(user_windows[k][:], 0.0)
 
         nc.scalar.activation(item_windows[3][:].indirect(item_list[:]), last_sums[:], COPY, scale=ones[:])
@@ -405,4 +404,7 @@ def tile_attend_gmf_hub_vu_kernel(tc, uT, vT, y, us, ts, offs, uoffs, out_0, out
                 empty(engine, accs[n], "user", k, n)
             for n in range(2):
                 scatter(engine, "user", k, n)
+                if k == 0 and n == 0:
+                    w_planes_i.append(operand("w_hi", w_hi_values, HALF, "w_i0_codes"))
+                    quantize(w_planes_i[2], E4M3, first)
             store("user", k)

from contextlib import ExitStack

import concourse.mybir as mybir
from concourse.masks import make_identity

F32 = mybir.dt.float32
BF16 = mybir.dt.bfloat16
U32 = mybir.dt.uint32
U16 = mybir.dt.uint16
U8 = mybir.dt.uint8
E4M3 = mybir.dt.float8_e4m3fn_x4
E5M2 = mybir.dt.float8_e5m2_x4
ALU = mybir.AluOpType
COPY = mybir.ActivationFunctionType.Copy

P = 128
PACK = 4
L = 512
T = 2048
HALF = L // 2
BAND = 16

FLOPS = 3 * 2 * L * L * L


def tile_attend_gmf_hub_vu_kernel(tc, uT, vT, y, us, ts, offs, uoffs, out_0, out_1):
    nc = tc.nc
    with ExitStack() as ctx:
        keep = ctx.enter_context(tc.tile_pool(name="keep", bufs=1))
        laid = ctx.enter_context(tc.tile_pool(name="laid", bufs=1))
        psum = ctx.enter_context(tc.psum_pool(name="psum", bufs=1))

        def bank_tile(b):
            return psum.tile([P, L], F32, name="bank%d" % b)

        def tile(name, columns, dtype):
            return keep.tile([P, columns], dtype, name=name, align_bytes=64)

        first, second, whole = slice(0, HALF), slice(HALF, L), slice(0, L)
        halves = (first, second)
        quarters = [slice(q * P, (q + 1) * P) for q in range(PACK)]

        user_list = keep.tile([P, L // BAND], U16, name="user_list")
        item_list = keep.tile([P, L // BAND], U16, name="item_list")
        u_planes = [tile("u_plane%d" % t, T, F32) for t in range(PACK)]
        v_planes = [tile("v_plane%d" % t, T, F32) for t in range(PACK)]
        ts_table = tile("ts_table", T, F32)
        us_cols = tile("us_cols", PACK, F32)
        y_rows = [keep.tile([P, PACK, HALF], F32, name="y_rows%d" % n, align_bytes=64) for n in range(2)]
        item_windows = [tile("item_window%d" % k, T, F32) for k in range(PACK)]
        user_windows = [tile("user_window%d" % k, T, F32) for k in range(2)]
        identity = tile("identity", P, F32)

        def places(offsets, cols):
            return offsets[:, cols.start // BAND : cols.stop // BAND]

        def operand(name, values, columns, codes_buffer=None):
            codes = tile(codes_buffer or name + "_codes", columns, U32)
            return values, codes, tile(name + "_scales", columns, U8)

        def quantize(op, fmt, cols):
            values, codes, scales = op
            nc.vector.quantize_mx(
                out=codes[:, cols].bitcast(fmt),
                scales=scales[:, cols],
                in_=values[:, PACK * cols.start : PACK * cols.stop],
            )

        def product(acc, stationary, block, moving, moving_fmt, moving_cols):
            nc.tensor.matmul_mx(
                out=acc,
                lhsT=stationary[1][:, quarters[block]].bitcast(E4M3),
                lhsT_scale=stationary[2][:, quarters[block]],
                rhs=moving[1][:, moving_cols].bitcast(moving_fmt),
                rhs_scale=moving[2][:, moving_cols],
                start=True,
                stop=True,
            )

        def turn_planes(planes, bank):
            words = planes.bitcast(F32).rearrange("p (a m u) -> p a u m", a=2, u=2)
            for a in range(2):
                for u in range(2):
                    nc.tensor.transpose(bank[:, quarters[2 * a + u]], words[:, a, u, :], identity[:])
            return bank[:]

        def turn_plane(plane, bank):
            words = plane.bitcast(F32).rearrange("p (m u) -> p u m", u=2)
            for u in range(2):
                nc.tensor.transpose(bank[:, quarters[u]], words[:, u, :], identity[:])
            return bank

        def pack_turned(copy, target, bank):
            copy(
                target.bitcast(F32).rearrange("m (p u) -> m p u", u=2),
                bank[:, first].rearrange("m (u p) -> m p u", u=2),
            )

        u_rows = uT.rearrange("(p t) c -> t p c", t=PACK)
        v_rows = vT.rearrange("(p t) c -> t p c", t=PACK)
        nc.gpsimd.memset(ts_table[:], 0.0)
        for window in item_windows[:2]:
            for cols in (slice(0, T // 2 - 1), slice(T // 2 - 1, T)):
                nc.vector.memset(window[:, cols], 0.0)
        nc.sync.dma_start(u_planes[0][:], u_rows[0])
        nc.sync.dma_start(user_list[:], uoffs)
        nc.sync.dma_start(item_list[:], offs)
        nc.scalar.dma_start(us_cols[:], us.rearrange("b (p s) o -> p (b s o)", s=PACK))
        nc.sync.dma_start(ts_table[0:1, :], ts[0:1, :])
        for t in range(1, PACK):
            nc.sync.dma_start(u_planes[t][:], u_rows[t])
        for t in range(PACK):
            nc.sync.dma_start(v_planes[t][:], v_rows[t])
        for n in range(2):
            nc.sync.dma_start(y_rows[n][:], y.rearrange("b (p s) i -> p (b s) i", s=PACK)[:, :, halves[n]])

        make_identity(nc, identity[:])
        for window in item_windows[2:] + user_windows:
            nc.gpsimd.memset(window[:], 0.0)

        ts_row = tile("ts_row", L, F32)
        nc.vector.tensor_copy(ts_row[:], ts_table[:].indirect(item_list[:]))
        ts_turned = bank_tile(4)
        for q in range(PACK):
            nc.tensor.transpose(ts_turned[:, quarters[q]], ts_row[:, quarters[q]], identity[:])
        ts_cols = tile("ts_cols", PACK, F32)
        nc.vector.tensor_copy(ts_cols[:], ts_turned[:, 0:L:P])
        ts_spread = bank_tile(5)
        for q in range(PACK):
            nc.tensor.transpose(ts_spread[:, quarters[q]], ts_cols[:, q : q + 1].to_broadcast([P, P]), identity[:])
        ts_rows = laid.tile([P, L], F32, name="ts_rows", align_bytes=64, offset=3 * 1024)
        nc.vector.tensor_copy(ts_rows[:], ts_spread[:])
        scale = keep.tile([P, L, PACK], F32, name="scale", align_bytes=64)
        nc.vector.tensor_tensor(
            scale[:],
            ts_rows[:].unsqueeze(2).to_broadcast([P, L, PACK]),
            us_cols[:].unsqueeze(1).to_broadcast([P, L, PACK]),
            ALU.mult,
        )

        scale_rows = []
        for n in range(2):
            scale_rows.append(keep.tile([P, 2, P], F32, name="scale_rows%d" % n, align_bytes=64))
            nc.vector.tensor_tensor(
                scale_rows[n][:],
                ts_spread[:, quarters[0]].unsqueeze(1).to_broadcast([P, 2, P]),
                us_cols[:, 2 * n : 2 * n + 2].unsqueeze(2).to_broadcast([P, 2, P]),
                ALU.mult,
            )

        x_planes = tile("x_planes", PACK * L, BF16)
        x_r = []
        x_d = operand("x_d", laid.tile([P, PACK * L], BF16, name="x_d_values", align_bytes=64, offset=0), L)
        for t in range(PACK):
            plane = x_planes[:, t * L : (t + 1) * L]
            nc.scalar.activation(plane, u_planes[t][:].indirect(user_list[:]), COPY)
            if t == PACK - 1:
                nc.vector.tensor_copy(
                    x_d[0][:].rearrange("p (s m t) -> p s m t", s=PACK, t=PACK),
                    x_planes[:].rearrange("p (t m s) -> p s m t", t=PACK, s=PACK),
                )
            x_r.append(operand("x_r%d" % t, tile("x_r%d_values" % t, L, BF16), P))
            pack_turned(nc.vector.tensor_copy, x_r[t][0][:], turn_plane(plane, bank_tile((4, 4, 5, 4)[t])))
            if t == PACK - 1:
                quantize(x_d, E4M3, whole)
            quantize(x_r[t], E4M3, quarters[0])

        w_values = laid.tile([P, PACK * L], BF16, name="w_d_values", align_bytes=64, offset=4 * 1024)
        w_packed = w_values[:].rearrange("p (i t) -> p i t", t=PACK)
        w_planes = tile("w_planes", 2 * L, BF16)
        w_i = [operand("w_i%d" % t, tile("w_i%d_values" % t, L, BF16), P) for t in range(2)]
        banks = []
        for t in range(2):
            nc.scalar.activation(w_planes[:, t * L : (t + 1) * L], v_planes[t][:].indirect(item_list[:]), COPY)
            banks.append(turn_plane(w_planes[:, t * L : (t + 1) * L], bank_tile(4 + t)))
        pack_turned(nc.vector.tensor_copy, w_i[0][0][:], banks[0])
        nc.vector.tensor_copy(w_packed[:, :, 0:2], w_planes[:].rearrange("p (t i) -> p i t", t=2))
        for cols in halves:
            nc.scalar.activation(w_packed[:, cols, 2], v_planes[2][:].indirect(places(item_list, cols)), COPY)
        pack_turned(nc.vector.tensor_copy, w_i[1][0][:], banks[1])
        for t in range(2):
            quantize(w_i[t], E4M3, quarters[0])
        third_plane = tile("w_planes", L, BF16)
        for cols in halves:
            nc.vector.tensor_copy(third_plane[:, cols], w_packed[:, cols, 2])
        last_quarter = tile("w_i1_values", P, BF16)
        nc.vector.tensor_copy(last_quarter[:], v_planes[3][:].indirect(places(item_list, quarters[2])))
        for cols in (quarters[0], quarters[1], quarters[3]):
            nc.scalar.activation(w_packed[:, cols, 3], v_planes[3][:].indirect(places(item_list, cols)), COPY)

        w_d = {}

        def quantize_items(q):
            w_d[q] = operand("w_d%d" % q, w_values[:, q * L : (q + 1) * L], P)
            quantize(w_d[q], E4M3, quarters[0])

        item_scaled = [tile("item_scaled%d" % q, L, F32) for q in range(PACK)]
        residual = [tile("residual%d" % q, L, F32) for q in range(PACK)]
        clipped = {}
        h_r = operand("h_r", tile("h_r_values", PACK * L, BF16), L)

        def targets(q, blocks):
            return y_rows[q // 2][:, blocks, quarters[q % 2]]

        quantize_items(0)
        nc.vector.tensor_copy(w_packed[:, quarters[2], 3], last_quarter[:])
        for q in range(1, PACK):
            quantize_items(q)
        for n in range(2):
            acc = bank_tile(n)
            for e in range(2):
                product(acc[:, quarters[e]], x_d, 2 * n + e, w_d[0], E4M3, quarters[0])
            nc.vector.tensor_tensor(
                item_scaled[0][:, halves[n]],
                acc[:, first],
                scale_rows[n][:].rearrange("p s i -> p (s i)"),
                ALU.mult,
            )
        for n in range(2):
            nc.vector.tensor_tensor(
                residual[0][:, halves[n]].rearrange("p (s i) -> p s i", s=2),
                item_scaled[0][:, halves[n]].rearrange("p (s i) -> p s i", s=2),
                targets(0, slice(2 * n, 2 * n + 2)),
                ALU.subtract,
            )

        turned = {}

        def score(q, cols, bank):
            acc = bank_tile(bank)
            product(acc[:, cols], w_d[q], 0, x_d, E4M3, cols)
            return acc

        def turn_back(q, cols, acc, bank):
            nc.scalar.activation(item_scaled[q][:, cols], acc[:, cols], COPY, scale=ts_cols[:, q : q + 1])
            back = bank_tile(bank)
            for s in range(cols.start // P, cols.stop // P):
                nc.tensor.transpose(back[:, quarters[s]], item_scaled[q][:, quarters[s]], identity[:])
                turned[q, s] = back[:, quarters[s]]

        scores = [score(1, halves[n], 2 + n) for n in range(2)]
        scores.append(score(2, whole, 6))
        for n in range(2):
            turn_back(1, halves[n], scores[n], 4 + n)
        scores.append(score(3, whole, 3))
        for n in range(2):
            turn_back(2, halves[n], scores[2], n)
        for n in range(2):
            turn_back(3, halves[n], scores[3], (7, 2)[n])
        last_plane = tile("w_d3_codes", L, BF16)
        nc.scalar.copy(last_plane[:], w_packed[:, :, 3])
        w_hi_values = tile("w_hi_values", 2 * L, BF16)
        for n, plane in enumerate((third_plane, last_plane)):
            pack_turned(nc.scalar.copy, w_hi_values[:, n * L : (n + 1) * L], turn_plane(plane[:], bank_tile((3, 6)[n])))

        def subtract(q, blocks=range(PACK)):
            for s in blocks:
                nc.vector.scalar_tensor_tensor(
                    residual[q][:, quarters[s]],
                    turned[q, s],
                    us_cols[:, s : s + 1],
                    targets(q, s),
                    ALU.mult,
                    ALU.subtract,
                )

        def clip(q):
            clipped[q] = tile("clipped%d" % (0, 1, 1, 3)[q], L, F32)
            nc.vector.tensor_scalar(
                clipped[q][:].rearrange("p (c j s) -> p c s j", j=2, s=PACK),
                residual[q][:].rearrange("p (s c j) -> p c s j", j=2, s=PACK),
                1.0,
                -1.0,
                ALU.min,
                ALU.max,
            )

        def weigh(q, cols=whole, engine=nc.vector):
            engine.tensor_tensor(
                h_r[0][:, q * L + cols.start : q * L + cols.stop],
                clipped[q][:, cols],
                scale[:, quarters[q], :].rearrange("p i s -> p (i s)")[:, cols],
                ALU.mult,
            )

        subtract(1, range(2))
        clip(0)
        subtract(1, range(2, PACK))
        weigh(0)
        clip(1)
        quantize(h_r, E5M2, quarters[0])
        weigh(1, quarters[0])
        weigh(1, slice(P, L), nc.gpsimd)
        for q in (2, 3):
            subtract(q)
        quantize(h_r, E5M2, quarters[1])
        for q in (2, 3):
            clip(q)
        for q in (2, 3):
            weigh(q)
        for q in (2, 3):
            quantize(h_r, E5M2, quarters[q])

        out_rows = {
            "item": out_0.rearrange("(p t) c -> t p c", t=PACK),
            "user": out_1.rearrange("(p t) c -> t p c", t=PACK),
        }
        windows = {"item": item_windows, "user": user_windows}
        lists = {"item": item_list, "user": user_list}
        sums = {}
        for side, buffer in (("item", "u_plane0"), ("user", "u_plane1")):
            row = tile(buffer, PACK * L, F32)
            for k in range(2 * PACK):
                sums[side, k // 2, k % 2] = row[:, k * HALF : (k + 1) * HALF]

        w_planes_i = list(w_i)

        def gradient(bank, side, plane, cols):
            acc = bank_tile(bank)
            if side == "item":
                product(acc[:, cols], x_r[plane], 0, h_r, E5M2, cols)
            else:
                product(acc[:, cols], w_planes_i[min(plane, 2)], plane // 2 * (plane % 2), h_i, E5M2, cols)
            return acc

        def empty(engine, acc, side, plane, n):
            if engine == "scalar":
                nc.scalar.copy(sums[side, plane, n], acc[:, halves[n]])
            else:
                nc.vector.tensor_copy(sums[side, plane, n], acc[:, halves[n]])

        def scatter(engine, side, plane, n):
            target = windows[side][plane][:].indirect(places(lists[side], halves[n]))
            if engine == "scalar":
                nc.scalar.activation(target, sums[side, plane, n], COPY)
            else:
                nc.vector.tensor_copy(target, sums[side, plane, n])

        def store(side, plane):
            nc.sync.dma_start(out_rows[side][plane], windows[side][plane][:])

        for q in range(2):
            nc.scalar.copy(sums["item", 0, 0][:, quarters[q]], gradient(4 + q, "item", 0, quarters[q])[:, quarters[q]])
        early = {k: gradient((1, 6, 0)[k - 1], "item", k, first) for k in (1, 2, 3)}
        scatter("scalar", "item", 0, 0)
        empty("scalar", early[1], "item", 1, 0)
        scatter("scalar", "item", 1, 0)
        last_sums = tile("clipped3", L, F32)
        nc.vector.tensor_copy(last_sums[:, first], early[3][:, first])
        closing = [gradient((4, 7)[q - 2], "item", 0, quarters[q])[:, quarters[q]] for q in (2, 3)]
        late = {k: gradient((2, 3, 5)[k - 1], "item", k, second) for k in (2, 1, 3)}
        for n in range(2):
            nc.vector.tensor_copy(sums["item", 0, 1][:, quarters[n]], closing[n])
        third_sums = tile("x_r0_scales", L, F32)
        for n in range(2):
            sums["item", 2, n] = third_sums[:, halves[n]]
        empty("vector", early[2], "item", 2, 0)
        scatter("vector", "item", 0, 1)
        store("item", 0)
        for k in (2, 1):
            empty("scalar", late[k], "item", k, 1)
        scatter("scalar", "item", 1, 1)
        store("item", 1)
        nc.vector.tensor_copy(item_windows[2][:].indirect(item_list[:]), third_sums[:])
        store("item", 2)
        nc.scalar.copy(last_sums[:, second], late[3][:, second])

        h_planes = tile("x_r0_codes", PACK * L, BF16)
        h_i = operand("h_i", laid.tile([P, PACK * L], BF16, name="h_i_values", align_bytes=64, offset=8 * 1024), L)
        h_i_words = h_i[0][:].bitcast(F32).rearrange("m (p s u) -> m p s u", s=PACK, u=2)
        for n in range(2):
            nc.gpsimd.tensor_scalar(
                h_planes[:].rearrange("p (s i) -> p s i", s=PACK)[:, 2 * n : 2 * n + 2, :],
                h_r[0][:].rearrange("p (i s) -> p s i", s=PACK)[:, 2 * n : 2 * n + 2, :],
                1.0,
                0.0,
                ALU.mult,
                ALU.add,
            )
            nc.scalar.copy(
                h_i_words[:, :, 2 * n : 2 * n + 2, :],
                turn_planes(h_planes[:, 2 * n * L : 2 * (n + 1) * L], bank_tile((1, 4)[n])).rearrange(
                    "m (a u p) -> m p a u", a=2, u=2
                ),
            )
        ones = tile("x_r0_codes", 1, F32)
        nc.gpsimd.memset(ones[:], 1.0)
        for cols in halves:
            quantize(h_i, E5M2, cols)
        user_windows.append(tile("h_r_values", T, F32))
        user_windows.append(laid.tile([P, T], F32, name="user_window3", align_bytes=64, offset=8 * 1024))
        for k in (2, 3):
            nc.gpsimd.memset(user_windows[k][:], 0.0)

        nc.scalar.activation(item_windows[3][:].indirect(item_list[:]), last_sums[:], COPY, scale=ones[:])
        store("item", 3)
        for k in range(PACK):
            engine = ("vector", "scalar")[k % 2]
            if k == 0:
                accs = [gradient(7 - n, "user", k, halves[n]) for n in range(2)]
            else:
                accs = [gradient((2, 3, 0)[k - 1], "user", k, whole)] * 2
            for n in range(2):
                empty(engine, accs[n], "user", k, n)
            for n in range(2):
                scatter(engine, "user", k, n)
                if k == 0 and n == 0:
                    w_planes_i.append(operand("w_hi", w_hi_values, HALF, "w_i0_codes"))
                    quantize(w_planes_i[2], E4M3, first)
            store("user", k)
